import numpy as np, ml_dtypes
CORES = [16,18,20,22]
N = 4
import mx_ref
BF = ml_dtypes.bfloat16
def gentries(a):
    return np.ascontiguousarray(a.reshape(8, 16, -1).transpose(0, 2, 1)).reshape(8, -1)
def gtable(e):
    e = np.asarray(e); return np.ascontiguousarray(e.reshape(8, -1, 16).transpose(0, 2, 1)).reshape(128, -1).astype(np.int32)
def gcols(t, e):
    v = np.concatenate([t.reshape(8, 16, -1, 4), np.zeros((8, 16, 1, 4), BF)], axis=2)
    return np.ascontiguousarray(np.stack([v[g][:, e[g]] for g in range(8)])).reshape(128, -1)
def tile(rs):
    return np.stack(rs, axis=2).reshape(128, -1).astype(BF)
def pick(q, e):
    c = np.concatenate([q[0].reshape(128, -1, 4), np.zeros((128, 1, 4), np.uint8)], axis=1); s = np.concatenate([q[1], np.ones((16, 1), np.uint8)], axis=1)
    return (np.ascontiguousarray(c[:, e].reshape(128, -1)), np.ascontiguousarray(s[:, e]))
def join(*qs):
    return (np.concatenate([q[0] for q in qs], axis=1), np.concatenate([q[1] for q in qs], axis=1))
def put(q, e, v):
    c, s = q[0].reshape(128, -1, 4).copy(), q[1].copy(); c[:, e] = v[0].reshape(128, -1, 4); s[:, e] = v[1]
    return (c.reshape(128, -1), s)
def pk(c, s):
    return (np.ascontiguousarray(c), mx_ref.live(s))
def emit(q):
    return q[0], q[1]
def packed(v, rng):
    q = [mx_ref.quantize(np.ascontiguousarray(v[r])) for r in range(N)]
    return np.stack([a for a, b in q]), np.stack([mx_ref.plane(b, rng) for a, b in q])
def values_of_codes():
    e, c = np.zeros((128, 128, 4), np.float32), np.zeros((128, 2, 4), np.uint8)
    e[np.arange(128), np.arange(128), 0] = 1
    c[:127, :, 0] = np.arange(256).reshape(2, 128).T[:127]
    return mx_ref.matmul(mx_ref.quantize(e.reshape(128, 512).astype(BF)), (c.reshape(128, 8), np.full((16, 2), 127, np.uint8))).T.reshape(-1).astype(np.float64)
CODE_VALUE, SCALE_VALUE = values_of_codes(), 2.0 ** (np.arange(256) - 127.0)
def decode(q):
    return (CODE_VALUE[q[0]].reshape(16, 8, -1, 4) * SCALE_VALUE[q[1]][:, None, :, None] + 0.0).reshape(128, -1).astype(np.float32)
def f(rng, *shape):
    return mx_ref.flush((rng.standard_normal(shape, dtype=np.float32) * np.exp2(rng.integers(-2, 3, shape[:-1] + (1,)))).astype(BF))
def wide(rng, *shape, cols=0):
    v = rng.standard_normal(shape, dtype=np.float32) * np.exp2(rng.integers(-12, 13, shape)).astype(np.float32)
    if cols: v *= np.repeat(np.exp2(rng.integers(-cols, cols + 1, shape[:-2] + (1, shape[-1] // 4))) * (rng.random(shape[:-2] + (1, shape[-1] // 4)) > 0.0625), 4, axis=-1).astype(np.float32)
    return mx_ref.flush(v.astype(BF))
C = 448
STEP = [1, 2, 3]
def numbers_of(rng):
    return {"x": np.array(f(rng, N, 128, 4 * C)), "u": np.array(f(rng, N, 128, 512)), "v": np.array(f(rng, N, 128, 512))}
def stored(h, t):
    return {"hl": np.stack([gtable(h[r]) for r in range(N)]), "tl": np.stack([gtable(t[r]) for r in range(N)])}
def lists(rng):
    e = np.tile(np.arange(C), (N, 8, 1))
    return stored(rng.permuted(e, axis=2), rng.permuted(e, axis=2))
def layers(rng, still=()):
    w = np.array(f(rng, N, 128, 2048)).reshape(N, 8, 16, 4, 8, 16, 4)
    for i in still:
        w[:, :, i] = 0
        w[:, :, :, :, :, i] = 0
    return w
def weights(rng, w):
    c, s = packed(np.ascontiguousarray(w).reshape(N, 128, 2048), rng)
    return {"wc": c, "ws": s}
def setup_inputs(rng):
    return {**numbers_of(rng), **lists(rng), **weights(rng, layers(rng))}
def setup_inputs_ties(rng):
    d = numbers_of(rng)
    o = rng.permutation(N)
    k = rng.integers(0, 4, (N, 2, 8, C))
    k[o[1]] += 1
    for g in rng.permutation(8)[:4]: k[o[2], :, g] = 1
    x = d["x"].reshape(N, 8, 16, C, 4)
    u = d["u"].reshape(N, 128, 128, 4)
    for i in range(2):
        x[:, :, i] = 0
        x[:, :, i, :, 0] = k[:, i].astype(np.float32).astype(BF)
        u[:, :, i::16] = 0
        for r in range(N):
            for h in range(i, 128, 16): u[r, h, h, 0] = 0.0 if r == o[0] else -1.0 if r == o[1] else 1.0
    a = np.exp2(rng.integers(-3, 4, (8, 1)).astype(np.float32))
    x[:, :, 8:] = 0
    x[:, :, 8, :, 0] = (-1.125 * a).astype(BF)
    x[:, :, 10, :, 0] = (-0.0703125 * a).astype(BF)
    w = layers(rng, [0, 1])
    w[:, :, :, :, :, 8:] = 0
    for g in range(8):
        w[:, g, 8, 0, g, 8, 0] = -28.0
        for b in range(4): w[:, g, 10, b, g, 9, 0] = -2.0 ** (b - 5)
    return {"x": x.reshape(N, 128, 4 * C), "u": u.reshape(N, 128, 512), "v": d["v"], **lists(rng), **weights(rng, w)}
def setup_inputs_near(rng):
    d = numbers_of(rng)
    x = d["x"].astype(np.float32).reshape(N, 8, 16, C, 4)
    x[:, :, 0] = 0
    x[:, :, 8:] = 0
    u = d["u"].reshape(N, 128, 128, 4)
    for i in range(2): u[:, :, i::16] = 0
    w = layers(rng, [0, 8, 9, 10, 11, 12, 13, 14, 15])
    o = rng.permutation(N) % 4
    for r in range(N):
        c = rng.choice([-1.0, 1.0], (8, 1))
        k = 1.0 if o[r] == 0 else 2.0 ** -30
        if o[r] < 2:
            x[r, :, 0, :, 0] = c
            x[r, :, 11, :, 0] = 2.0 ** -10
        x[r, :, 13, :, 0] = rng.integers(0, 2, (8, C)) * (2.0 ** -20 if o[r] < 2 else 2.0 ** -30)
        x[r, :, 15, :, 0] = 2.0 ** -20 if o[r] < 2 else 2.0 ** -29
        for g in range(8):
            w[r, g, 13, 0, g, 12, 0] = 2.0 ** -18 if o[r] < 2 else 2.0 ** -8
            if o[r] < 2: w[r, g, 14, 0, g, 12, 0] = 2.0 ** -6
            w[r, g, 15, 0, g, 15, 0] = 2.0 ** -5 if o[r] < 2 else 16.0
        for i in range(2):
            s = rng.integers(0, 16, (8, C))
            digits = ((s[:, :, None] >> np.arange(4)) & 1) * np.exp2(np.arange(4) - 23.0)
            if o[r] < 2: x[r, :, 8 + i] = digits
            elif o[r] == 2: x[r, :, 8 + i] = digits * rng.choice([-1.0, 1.0], (8, C, 1))
            else:
                x[r, :, 8 + 2 * i, :, 0] = np.where(s < 8, 1.25, 0.0) * 2.0 ** -30 * c
                x[r, :, 9 + 2 * i, :, 0] = np.where(s < 8, 0.0, 1.125) * 2.0 ** -30 * c
                for g in rng.permutation(8)[:4]:
                    e = rng.choice([-1.0, 1.0], C) * 2.0 ** -30
                    x[r, g, 8 + 2 * i, :, 0] = 1.25 * e
                    x[r, g, 9 + 2 * i, :, 0] = -1.125 * e
            for p in range(0, 128, 16):
                u[r, p, p + i, 0] = k if o[r] < 2 else 1.0
                u[r, p + 12, p + i, 0] = k
                if o[r] < 2: u[r, p + 11, p + i, 0] = k
                if o[r] < 3: u[r, p + 8 + i, p + i] = k
                else:
                    u[r, p + 8 + 2 * i, p + i, 0] = k
                    u[r, p + 9 + 2 * i, p + i, 0] = 1.125 * k
        at = [0, C - 1, int(rng.integers(C)), int(rng.integers(C))]
        for g, j in zip(rng.permutation(8)[:4], at): x[r, g, 0, j, 0] = 2.0 ** 29 * rng.choice([-1.0, 1.0])
    return {"x": x.reshape(N, 128, 4 * C).astype(BF), "u": u.reshape(N, 128, 512), "v": d["v"], **lists(rng), **weights(rng, w)}
def setup_inputs_odd(rng):
    d = numbers_of(rng)
    x = (1.0 + (2 * rng.integers(0, 64, (N, 16, 8, C, 4)) + 1) * 2.0 ** -7) * np.exp2(-rng.integers(0, 7, (N, 16, 8, C, 4)).astype(np.float64)) * rng.choice([-1.0, 1.0], (N, 16, 8, C, 4))
    x[:, :, 0, :, 0] = 1.96875 * 2.0 ** 8 * rng.choice([-1.0, 1.0], (N, 16, 1))
    u = d["u"].reshape(N, 128, 128, 4)
    for i in range(2):
        x[:, ::2, 1 + i, :, 0] = (8 + rng.integers(0, 2, (N, 8, C))) * 2.0 ** -8
        u[:, :, i::16] = 0
        for h in range(i, 128, 16): u[:, h + 1, h, 0] = 1.0
    return {"x": x.astype(np.float32).reshape(N, 128, 4 * C).astype(BF), "u": u.reshape(N, 128, 512), "v": d["v"], **lists(rng), **weights(rng, layers(rng, [0, 8]))}
def setup_inputs_ends(rng):
    d = numbers_of(rng)
    x = np.zeros((N, 8, 16, C, 4))
    u = d["u"].astype(np.float32).reshape(N, 128, 128, 4)
    v = d["v"].astype(np.float32)
    w = np.zeros((N, 128, 4, 128, 4), np.float32)
    hh, tt = np.zeros((N, 8, C), np.int64), np.zeros((N, 8, C), np.int64)
    o, e = rng.permutation(N) % 4, rng.permutation(N) % 4
    i, a = np.arange(128), np.arange(C)
    for r in range(N):
        low = -(0.8 + 0.08 * rng.random((8, 16, C, 4))) * 2.0 ** 30
        low[:, 15] = -2.0 ** 30
        tiny = -(1.0 + 0.125 * rng.integers(0, 8, (8, 16, C, 4))) * 2.0 ** -30
        if o[r] == 0: x[r] = low
        if o[r] == 1: x[r] = np.where((rng.random(C) < 0.5)[:, None], -low, low)
        if o[r] == 2: x[r] = tiny
        if o[r] == 3: x[r] = d["x"][r].astype(np.float32).reshape(8, 16, C, 4)[:, :, :1]
        x[r, 0] = tiny[0] * 2.0 ** 20 if o[r] < 2 else tiny[0] if o[r] == 2 else -2.0 ** -30
        for k in range(2):
            h = rng.permutation(8)
            c = np.where(h < 2, 0.0, h % 2 * 2.0 - 1.0)[None, :, None]
            if o[r] < 2: u[r, :, k::16] = c * (0.9 + 0.1 * rng.random((128, 8, 4))) * 2.0 ** 30
            if o[r] == 2: u[r, :, k::16] = c * (1.0 + 0.125 * rng.integers(0, 8, (128, 8, 4))) * 2.0 ** -30
            if o[r] == 3: u[r, :, k::16] *= np.abs(c).astype(np.float32)
        if o[r] < 2: v[r] = rng.choice([-1.0, 1.0], (128, 512)) * (0.9 + 0.1 * rng.random((128, 512))) * 2.0 ** 30
        else: v[r] = rng.choice([-1.0, 1.0], (128, 512)) * (1.0 + 0.125 * rng.integers(0, 8, (128, 512))) * 2.0 ** -30
        k = np.array([0.25, 0.5, 1.0])[rng.permutation(8) % 3] * rng.choice([-1.0, 1.0], 8)
        if o[r] == 2: k[:] = 0.0
        k[0] = 2.0 ** 8 if o[r] > 1 else 2.0 ** -8
        for b in range(4): w[r, i, b, i, b] = np.where((i >= 16) & (i % 16 == 15), 0.0, k[i // 16])
        hh[r] = C - 1 - a if e[r] == 1 else a
        if e[r] == 3: hh[r] = rng.permuted(np.tile(a, (8, 1)), axis=1)
        tt[r] = hh[r] if e[r] < 2 else np.roll(a, 1) if e[r] == 2 else hh[r] ^ 1
    return {"x": x.astype(np.float32).reshape(N, 128, 4 * C).astype(BF), "u": u.reshape(N, 128, 512).astype(BF), "v": v.astype(BF), **stored(hh, tt), **weights(rng, w.astype(BF))}
def setup_inputs_spread(rng):
    d = setup_inputs(rng)
    d["x"] = wide(rng, N, 128, 4 * C, cols=6)
    return d
def check_inputs(d):
    b = []
    for k in ("x", "u", "v"):
        a = np.abs(d[k].astype(np.float32))
        if not (np.isfinite(a).all() and ((a == 0) | (a >= 2.0 ** -30) & (a <= 2.0 ** 30)).all()): b.append("a value of " + k)
    for k in ("hl", "tl"):
        for r in range(N):
            if not (np.sort(gentries(d[k][r]), axis=1) == np.arange(C)).all(): b.append(k + ": every number once in a group")
    none, least, most = [emit(mx_ref.quantize(np.full((128, 16), k, np.float32).astype(BF)))[1][0, 0] for k in (0.0, 2.0 ** -8, 2.0 ** 8)]
    for r in range(N):
        if ((d["wc"][r] == 0x7F) | (d["wc"][r] == 0xFF)).any(): b.append("wc: a code that is no number")
        s = mx_ref.live(d["ws"][r])
        if ((s != none) & ((s < least) | (s > most))).any(): b.append("ws: a scale out of range")
    return b
def ordered(s, a):
    e = np.sort(np.argsort(a, axis=1).reshape(8, -1, 2), axis=2)
    k = np.take_along_axis(s, e.reshape(8, -1), axis=1).reshape(e.shape)
    return np.where((k[:, :, 1] > k[:, :, 0])[:, :, None], e[:, :, ::-1], e).reshape(8, -1)
def transition(s, h, t):
    m = np.zeros((8, C), np.int64)
    np.put_along_axis(m, ordered(s, h), ordered(s, t), axis=1)
    return m
def behind(a, e):
    return np.take_along_axis(a, e, axis=1)
def reference(x, u, v, hl, tl, wc, ws):
    qu = [mx_ref.quantize(u[r]) for r in range(N)]
    lay = [pk(wc[r], ws[r]) for r in range(N)]
    now = [x[r] for r in range(N)]
    head, tail = [gentries(hl[r]) for r in range(N)], [gentries(tl[r]) for r in range(N)]
    for step in STEP:
        way, made = [], []
        for r in range(N):
            s = mx_ref.matmul(qu[r], mx_ref.quantize(now[r])) + np.float32(0.0)
            m0, m1 = transition(s[0::16], head[r], tail[r]), transition(s[1::16], head[r], tail[r])
            way.append(behind(m1, m0))
            z = mx_ref.quantize(((gcols(now[r], m0).astype(np.float32) + gcols(now[r], way[r]).astype(np.float32)) * np.float32(0.5)).astype(BF))
            made.append(mx_ref.quantize(tile([mx_ref.matmul(pick(lay[r], np.arange(128 * b, 128 * b + 128)), z) * np.float32(0.03125) for b in range(4)])))
        for r in range(N):
            p = r ^ step
            far = gcols(decode(made[p]).astype(BF), behind(way[r], way[p]))
            now[r] = (now[r].astype(np.float32) + far.astype(np.float32)).astype(BF)
            head[r], tail[r] = tail[r], behind(head[r], way[p])
    y, tp = np.zeros((N, 128, C), np.float32), np.zeros((N, 8, C), np.float32)
    oc, osc = np.zeros((N, 128, 4 * C), np.uint8), np.zeros((N, 16, C), np.uint8)
    for r in range(N):
        q = mx_ref.quantize(now[r])
        y[r] = mx_ref.matmul(mx_ref.quantize(v[r]), q)
        tp[r] = tail[r]
        oc[r], osc[r] = emit(q)
    return {"y": y, "tp": tp, "oc": oc, "osc": osc}

@@ -1,0 +1,415 @@
+from concourse.mybir import dt, AluOpType, ActivationFunctionType
+
+C = 448
+STEP = [1, 2, 3]
+R0 = 224
+RUNS = [(0, R0), (R0, C)]
+TINY, UP = 2.0 ** -91, 1024.0
+LIN = 464
+TW = 928
+A_, B_, LO_, HI_, HS_, LT_ = 0, 1, 2, 3, 4, 5
+
+
+def _sb(n, d):
+    return ("sbuf", [128, n], d)
+
+
+def _bf(n):
+    return _sb(n, "bfloat16")
+
+
+def _codes(n):
+    return _sb(n, "float8_e4m3fn_x4")
+
+
+def _plane(n):
+    return _sb(n, "uint8")
+
+
+SCRATCH = {
+    "hin": _sb(28, "int32"), "tin": _sb(28, "int32"),
+    "ut": _bf(512), "vt": _bf(512), "ones": _bf(512), "et": _bf(2048),
+    "xs": _bf(4 * 1792), "xp": _bf(3 * 1792), "yf": _sb(3 * 1792, "float32"),
+    "zt": _bf(3 * 1792), "ht": _bf(3 * 1792), "dp": _bf(3 * 1792),
+    "qu": _codes(128), "su": _plane(128), "qv": _codes(128), "sv": _plane(128),
+    "wq": _codes(512), "wp": _plane(512), "qe": _codes(512), "se": _plane(512),
+    "qx": _codes(4 * 448), "sx": _plane(4 * 448), "qz": _codes(3 * 448), "sz": _plane(3 * 448),
+    "qh": _codes(3 * 448), "sh": _plane(3 * 448), "qa": _codes(3 * 448), "sa": _plane(3 * 448),
+    "sf": _sb(3 * 448, "float32"), "sg": _sb(3 * 448, "float32"), "slo": _sb(3 * 448, "float32"),
+    "iot": _bf(448), "ln": _bf(8 * LIN + 16), "tt": _bf(6 * TW), "lg": _bf(11 * 448),
+    "tinv": _bf(4 * 448), "tp2": _bf(2 * 448), "tsw": _bf(4 * 448),
+    "seli": _sb(128, "int32"), "sel": _sb(8, "uint16"), "pg": _sb(8, "float32"),
+    "li": _sb(512, "int32"), "lu": _sb(1024, "uint16"), "lf": _sb(2560, "float32"), "bt": _bf(192),
+    "mu": _sb(192, "uint16"), "ma": _sb(192, "uint16"),
+    "tpf": _sb(448, "float32"), "yo": _sb(448, "float32"),
+    "ps": ("psum", [128, 4096], "float32"),
+}
+SEMAPHORES = (["cv", "cs", "ct", "cp", "loc", "ltl", "lhl", "lxx", "luu", "lww", "lvv", "lane", "outs"]
+              + ["ml%d" % n for n in range(3)] + ["ar%d" % n for n in range(3)])
+
+
+def rank_program(g, core, T, topo):
+    rank = T.rank_of(core)
+    if rank is None:
+        return
+    OP, AF = AluOpType, ActivationFunctionType
+    V, S, PE, Y = g.vector, g.scalar, g.tensor, g.sync
+    Q = {"v": V, "s": S, "t": PE, "p": g, "y": Y}
+    cnt = {"v": 0, "s": 0, "t": 0, "p": 0}
+    seen = {q: {} for q in Q}
+    ncl = {"i": 0, "u": 0, "f": 0}
+    tabs = {"i": T.li, "u": T.lu, "f": T.lf}
+
+    def need(q, *toks):
+        best = {}
+        for t in toks:
+            for a in (t if isinstance(t, list) else [t]):
+                if a is not None:
+                    best[a[0]] = max(best.get(a[0], 0), a[1])
+        for k, v in best.items():
+            if seen[q].get(k, 0) < v:
+                Q[q].wait_ge(T.sem[k], v)
+                seen[q][k] = v
+
+    def done(q, inst):
+        cnt[q] += 1
+        inst.then_inc(T.sem["c" + q], 1)
+        return ("c" + q, cnt[q])
+
+    def take(k, n):
+        a = ncl[k]
+        ncl[k] = a + n
+        return a
+
+    def cols(k, n):
+        a = take(k, n)
+        return tabs[k][:, a:a + n]
+
+    def vts(out, in0, s1, op0, deps, s2=None, op1=None):
+        need("v", *deps)
+        if op1 is None:
+            return done("v", V.tensor_scalar(out, in0, s1, None, op0))
+        return done("v", V.tensor_scalar(out, in0, s1, s2, op0, op1))
+
+    def vtt(out, in0, in1, op, deps):
+        need("v", *deps)
+        return done("v", V.tensor_tensor(out, in0, in1, op))
+
+    def vcp(out, in_, deps):
+        need("v", *deps)
+        return done("v", V.tensor_copy(out, in_))
+
+    def scp(out, in_, deps, scale=None):
+        need("s", *deps)
+        if scale is None:
+            return done("s", S.activation(out, in_, AF.Copy))
+        return done("s", S.activation(out, in_, AF.Copy, scale=scale))
+
+    def quant(qb, sb, a, b, tile, deps):
+        need("v", *deps)
+        return done("v", V.quantize_mx(qb[:, a:b], sb[:, a:b], tile))
+
+    free = [[] for _ in range(8)]
+
+    def mm(k, n, l, ls, r, rs, deps):
+        need("t", free[k], *deps)
+        free[k] = []
+        return done("t", PE.matmul_mx(T.ps[:, 512 * k:512 * k + n], l, ls, r, rs, True, True))
+
+    def bank(k, n):
+        return T.ps[:, 512 * k:512 * k + n]
+
+    def lin(k):
+        return T.ln[:, LIN * k + 16:LIN * k + LIN]
+
+    Y.dma_start(T.tin[:], T.tl[:, :]).then_inc(T.sem.ltl, 16)
+    Y.dma_start(T.xs[:, 0:1792], T.x[:, :]).then_inc(T.sem.lxx, 16)
+    S.dma_start(T.hin[:], T.hl[:, :]).then_inc(T.sem.lhl, 16)
+    S.dma_start(T.ut[:], T.u[:, :]).then_inc(T.sem.luu, 16)
+    S.dma_start(T.wq[:, 0:512].bitcast(dt.uint8), T.wc[:, :]).then_inc(T.sem.lww, 16)
+    S.dma_start(T.wp[:], T.ws[:, :]).then_inc(T.sem.lww, 16)
+    S.dma_start(T.vt[:], T.v[:, :]).then_inc(T.sem.lvv, 16)
+    TL, HL, LX, LU, LW, LV = ("ltl", 16), ("lhl", 16), ("lxx", 16), ("luu", 16), ("lww", 32), ("lvv", 16)
+
+    def si(k):
+        return T.seli[:, 8 * k:8 * k + 8]
+    iP = done("p", g.iota(si(0), [[0, 8]], 0, 1))
+    iC = done("p", g.iota(si(1), [[0, 4], [16, 2]], 0, 0))
+    iL = done("p", g.iota(si(2), [[1, 2], [0, 4]], 0, 0))
+    tIOT = done("p", g.iota(T.iot[:], [[1, 448]], -224, 0, allow_small_or_imprecise_dtypes=True))
+    iw0 = cols("f", 64)
+    iW = done("p", g.iota(iw0, [[0, 2], [16, 32]], -224, 1, allow_small_or_imprecise_dtypes=True))
+    tONE = done("v", V.memset(T.ones[:], 1.0))
+    pads = None
+    for k in range(9):
+        pads = done("v", V.memset(T.ln[:, LIN * k:LIN * k + 16], 0.0))
+    for b in range(4):
+        need("p", tONE)
+        tE = done("p", g.affine_select(T.et[:, 512 * b:512 * b + 512], T.ones[:], [[1, 512]], OP.is_equal, 0.0, -b, -4))
+    a1 = vts(si(3), si(0), 15, OP.bitwise_and, [iP])
+    a2 = vts(si(4), si(0), 16, OP.bitwise_and, [iP])
+    a3 = vts(si(5), si(0), 4, OP.arith_shift_right, [iP])
+    a4 = vtt(si(6), si(1), si(3), OP.add, [iC, a1])
+    a5 = vtt(si(7), si(0), si(5), OP.add, [iP, a3])
+    a6 = vtt(si(8), si(4), si(2), OP.add, [iL, a2])
+    a7 = vts(si(9), si(7), 1, OP.bitwise_and, [a5])
+    a8 = vtt(si(10), si(6), si(9), OP.add, [a4, a7])
+    a9 = vts(si(11), si(9), 448, OP.mult, [a7])
+    a10 = vts(si(12), si(10), 1, OP.arith_shift_right, [a8])
+    a11 = vtt(si(13), si(8), si(11), OP.add, [a6, a9])
+    a12 = vts(si(14), si(12), 32, OP.mult, [a10])
+    a13 = vtt(T.pg[:], si(0), si(3), OP.subtract, [a1])
+    a14 = vtt(si(15), si(14), si(13), OP.add, [a12, a11])
+    IW = cols("f", 64)
+    tIW = vts(IW, iw0, T.pg[:, 0:1], OP.subtract, [iW, a13], TINY, OP.mult)
+    tSEL = vts(T.sel[:], si(15), TW - 1, OP.min, [a14])
+    SEL, SEL2 = T.sel[:, 2:6], T.sel[:, 0:8]
+
+    lastT = {}
+    lastSel = {}
+
+    def turn(k, slot, deps):
+        a, o = LIN * k, TW * slot
+        need("v", pads, lastSel.get(slot), *deps)
+        done("v", V.transpose(T.tt[:, o:o + 448], T.ln[:, a + 16:a + 464]))
+        t2 = done("v", V.transpose(T.tt[:, o + 448:o + TW], T.ln[:, a:a + 480]))
+        lastT[k] = t2
+        return t2
+
+    def picked(slot, table=SEL):
+        return T.tt[:, TW * slot:TW * slot + TW].indirect(table)
+
+    def wrap(out, slot, deps, table=SEL):
+        t = vts(out, picked(slot, table), 224.0, OP.add, [tSEL] + deps)
+        lastSel[slot] = t
+        return t
+
+    def firsts(l32, deps):
+        b, e, u = cols("i", 28), cols("i", 28), cols("u", 28)
+        t1 = vts(b, l32, 1, OP.bitwise_and, deps)
+        t2 = vtt(e, l32, b, OP.subtract, [t1])
+        return u, vcp(u, e, [t2])
+
+    tab = [{}, {}, {}]
+
+    def sibling(n, deps):
+        d = tab[n]
+        t = turn(HS_, HS_, deps)
+        a = take("u", 64)
+        d["hs"], d["th"] = T.lu[:, a:a + 28], cols("f", 64)
+        d["ths"] = vts(T.lu[:, a:a + 64], picked(HS_), 1.0 / TINY, OP.mult, [tSEL, t], 224.0, OP.add)
+        d["tth"] = vtt(d["th"], picked(HS_), IW, OP.subtract, [t, tIW])
+        lastSel[HS_] = d["tth"]
+
+    def outs(n, gl, gh):
+        d = tab[n]
+        a = take("f", 256)
+        p, q = T.lf[:, a:a + 64], T.lf[:, a + 64:a + 128]
+        t1 = turn(LO_, LO_, [gl])
+        if gh is None:
+            t1 = t2 = wrap(T.lf[:, a:a + 128], LO_, [t1], SEL2)
+        else:
+            t2 = turn(HI_, HI_, [gh])
+            t1 = wrap(p, LO_, [t1])
+            t2 = wrap(q, HI_, [t2])
+        d["LO"], d["HI"] = T.lf[:, a + 128:a + 192], T.lf[:, a + 192:a + 256]
+        d["tLO"] = vtt(d["LO"], p, q, OP.min, [t1, t2])
+        d["tHI"] = vtt(d["HI"], p, q, OP.max, [t1, t2])
+        d["lo"], d["hi"] = cols("u", 28), cols("u", 28)
+        d["tlo"] = vcp(d["lo"], T.lf[:, a + 128:a + 156], [d["tLO"]])
+        d["thi"] = vcp(d["hi"], T.lf[:, a + 192:a + 220], [d["tHI"]])
+
+    def tinv(k):
+        return T.tinv[:, 448 * k:448 * k + 448]
+
+    def siblings(k, u, deps):
+        o = 448 * k
+        t1 = scp(T.tsw[:, o:o + 448:2], T.tinv[:, o + 1:o + 448:2], deps)
+        t2 = scp(T.tsw[:, o + 1:o + 448:2], T.tinv[:, o:o + 448:2], deps)
+        return scp(lin(HS_), T.tsw[:, o:o + 448].indirect(u), [t1, t2, pads, lastT.get(HS_)], scale=TINY)
+
+    hlin = [T.lg[:, 448 * 9:448 * 10], T.lg[:, 448 * 10:448 * 11]]
+    hrow = [T.lg[1::16, 448 * 9:448 * 10], T.lg[1::16, 448 * 10:448 * 11], T.ln[1::16, LIN * LT_ + 16:LIN * LT_ + LIN]]
+    tu, hu = cols("u", 28), cols("u", 28)
+    ttu = vcp(tu, T.tin[:], [TL])
+    thu = vcp(hu, T.hin[:], [HL])
+    thl = [scp(hlin[0], T.iot[:].indirect(hu), [thu, tIOT]), scp(hlin[1], T.iot[:].indirect(tu), [ttu]), None]
+    he, the = firsts(T.hin[:], [HL])
+    ho = cols("u", 28)
+    tho = vts(ho, he, 1.0, OP.add, [the])
+    tTI = [vcp(tinv(0).indirect(tu), T.iot[:], [ttu, tIOT])]
+    tHI = vcp(tinv(3).indirect(hu), T.iot[:], [thu, tIOT])
+    gl = scp(lin(LO_), tinv(0).indirect(he), [tTI[0], the, pads])
+    gh = scp(lin(HI_), tinv(0).indirect(ho), [tTI[0], tho])
+    gs = siblings(3, hu, [tHI, thu])
+    tQU = quant(T.qu, T.su, 0, 128, T.ut[:], [LU])
+    tX = [[LX], [], [], []]
+    tQX = [[None, None] for _ in range(4)]
+    t0 = quant(T.qx, T.sx, 0, 448, T.xs[:, 0:1792], [LX])
+    tQX[0] = [t0, t0]
+    sft, sgt = [], []
+
+    def score(n, h):
+        c0, c1 = RUNS[h]
+        a = 448 * n
+        t = mm(4 * h, c1 - c0, T.qu[:, 0:128], T.su[:, 0:128], T.qx[:, a + c0:a + c1], T.sx[:, a + c0:a + c1],
+               [tQU, tQX[n][h]])
+        r1 = scp(T.sf[:, a + c0:a + c1], bank(4 * h, c1 - c0), [t], scale=UP)
+        r2 = scp(T.sg[:, a + c0:a + c1], bank(4 * h, c1 - c0), [t], scale=UP)
+        free[4 * h] += [r1, r2]
+        sft.append(r1)
+        sgt.append(r2)
+
+    score(0, 0)
+    score(0, 1)
+    outs(0, gl, gh)
+    sibling(0, [gs])
+
+    nloc = [0]
+    told = {}
+
+    def send(dst, out, in_, sem):
+        rid, pid, _ = topo.addr(dst)
+        g.remote_dma(out, in_, T.sem[sem], T.sem.loc, pid, rid, topo.mask(core, dst))
+        nloc[0] += len(topo.engines(core, dst))
+
+    for n in range(3):
+        d = tab[n]
+        mate = T.cores[rank ^ STEP[n]]
+        eng = len(topo.engines(core, mate))
+        x0, a0 = 1792 * n, 448 * n
+        sf, sg, slo = T.sf[:, a0:a0 + 448], T.sg[:, a0:a0 + 448], T.slo[:, a0:a0 + 448]
+        ts = scp(slo, sf.indirect(d["lo"]), [sft, d["tlo"]])
+        tXP = []
+        for b in range(4):
+            tXP.append(scp(T.xp[:, x0 + 448 * b:x0 + 448 * b + 448], T.xs[:, x0 + b:x0 + 1792:4], [tX[n]]))
+        if n == 0:
+            gs = siblings(0, tu, [ttu, tTI[0]])
+        ta = vtt(lin(A_), sf.indirect(d["hs"]), sg, OP.subtract, [sft, sgt, d["ths"], lastT.get(A_), pads])
+        tb = vtt(lin(B_), sf.indirect(d["hi"]), slo, OP.is_gt, [ts, d["thi"], lastT.get(B_)])
+        ta = turn(A_, A_, [ta])
+        tb = turn(B_, B_, [tb])
+        ba = T.bt[:, 64 * n:64 * n + 64]
+        t = vtt(ba, picked(A_), d["th"], OP.is_gt, [ta, d["tth"], tSEL])
+        lastSel[A_] = t
+        e, w, m = cols("f", 64), cols("f", 64), cols("f", 64)
+        t = vtt(e, picked(B_), ba, OP.not_equal, [tb, t])
+        lastSel[B_] = t
+        t = vtt(w, e, d["HI"], OP.mult, [t, d["tHI"]])
+        t = vtt(m, w, d["LO"], OP.max, [t, d["tLO"]])
+        tm = vcp(T.mu[:, 64 * n:64 * n + 64], m, [t])
+        m0, m1 = T.mu[:, 64 * n:64 * n + 28], T.mu[:, 64 * n + 32:64 * n + 60]
+        need("p", tm)
+        send(mate, T.ma[:, 64 * n:64 * n + 64], T.mu[:, 64 * n:64 * n + 64], "ml%d" % n)
+        G = [T.lg[:, 448 * (3 * n + k):448 * (3 * n + k) + 448] for k in range(3)]
+        tg1 = scp(G[0], T.iot[:].indirect(m1), [tm, tIOT])
+        tz = []
+        for b in range(4):
+            p = x0 + 448 * b
+            yp = T.yf[:, p:p + 448]
+            ty = vtt(yp, T.xp[:, p:p + 448].indirect(m1), T.xs[:, x0 + b:x0 + 1792:4], OP.add, [tm, tXP[b], tX[n]])
+            if b < 3:
+                tz.append(scp(T.zt[:, x0 + b:x0 + 1792:4], yp.indirect(m0), [ty], scale=0.5))
+            else:
+                u = 64 * n + R0 // 16
+                tza = vts(T.zt[:, x0 + b:x0 + 4 * R0:4], yp.indirect(T.mu[:, 64 * n:u]), 0.5, OP.mult, [ty])
+                tzb = scp(T.zt[:, x0 + 4 * R0 + b:x0 + 1792:4], yp.indirect(T.mu[:, u:64 * n + 28]), [ty], scale=0.5)
+        tq = [quant(T.qz, T.sz, a0, a0 + R0, T.zt[:, x0:x0 + 4 * R0], tz + [tza]),
+              quant(T.qz, T.sz, a0 + R0, a0 + 448, T.zt[:, x0 + 4 * R0:x0 + 1792], tz + [tzb])]
+        tg2 = scp(G[1], G[0].indirect(m0), [tg1])
+        need("y", tg2, thl[n])
+        Y.dma_start(T.lg[1::16, 448 * (3 * n + 1):448 * (3 * n + 2)], hrow[n]).then_inc(T.sem.lane, 16)
+        for h in range(2):
+            c0, c1 = RUNS[h]
+            tr = [mm(b + 4 * h, c1 - c0, T.wq[:, 128 * b:128 * b + 128], T.wp[:, 128 * b:128 * b + 128],
+                     T.qz[:, a0 + c0:a0 + c1], T.sz[:, a0 + c0:a0 + c1], [LW, tq[h]]) for b in range(4)]
+            th = []
+            for b in range(4):
+                o = T.ht[:, x0 + 4 * c0 + b:x0 + 4 * c1:4]
+                if h == 0 and b < 2:
+                    r = vts(o, bank(b + 4 * h, c1 - c0), 0.03125, OP.mult, [tr[b]])
+                else:
+                    r = scp(o, bank(b + 4 * h, c1 - c0), [tr[b]], scale=0.03125)
+                free[b + 4 * h].append(r)
+                th.append(r)
+            r = quant(T.qh, T.sh, a0 + c0, a0 + c1, T.ht[:, x0 + 4 * c0:x0 + 4 * c1], th)
+            need("p", r)
+            send(mate, T.qa[:, a0 + c0:a0 + c1].bitcast(dt.uint8), T.qh[:, a0 + c0:a0 + c1].bitcast(dt.uint8), "ar%d" % n)
+            if h == 0 and n == 0:
+                te = firsts(T.tin[:], [TL])
+            elif h == 0 and n == 1:
+                l32 = cols("i", 28)
+                te = firsts(l32, [vcp(l32, told["u"], [told["t"]])])
+        send(mate, T.sa[:, a0:a0 + 448], T.sh[:, a0:a0 + 448], "ar%d" % n)
+        if n == 0:
+            scp(T.tp2[:, 0:448], T.iot[:], [tIOT])
+            tTP = scp(T.tp2[:, 448:896], T.iot[:], [tIOT])
+            tQE = quant(T.qe, T.se, 0, 512, T.et[:], [tE])
+            tQV = quant(T.qv, T.sv, 0, 128, T.vt[:], [LV])
+        if n < 2:
+            sibling(n + 1, [gs])
+        need("s", ("ml%d" % n, eng), ("lane", 48 * n + 16))
+        am0, am1 = T.ma[:, 64 * n:64 * n + 28], T.ma[:, 64 * n + 32:64 * n + 60]
+        t = scp(G[2], G[1].indirect(am1), [tg2])
+        tlt = scp(lin(LT_ + n), G[2].indirect(am0), [t, pads])
+        t = turn(LT_ + n, LT_, [tlt])
+        u0 = take("u", 64)
+        tl = wrap(T.lu[:, u0:u0 + 64], LT_, [t])
+        tn = T.lu[:, u0 + 32:u0 + 60]
+        told = {"u": tn, "t": tl}
+        if n == 0:
+            thl[2] = tlt
+        if n < 2:
+            tTI.append(vcp(tinv(n + 1).indirect(tn), T.iot[:], [tl]))
+            need("y", tTI[n + 1], tTP)
+            r = 448 * (n + 1)
+            Y.dma_start(T.tp2[0::16, r - 448:r], T.tinv[0::16, r:r + 448]).then_inc(T.sem.lane, 16)
+            Y.dma_start(T.tp2[1::16, r - 448:r - 1], T.tinv[1::16, r + 1:r + 448]).then_inc(T.sem.lane, 16)
+        tdp = [[], [], [], []]
+        need("t", ("ar%d" % n, 3 * eng))
+        for b in range(4):
+            for h in range(2):
+                c0, c1 = RUNS[h]
+                t = mm(b + 4 * h, c1 - c0, T.qe[:, 128 * b:128 * b + 128], T.se[:, 128 * b:128 * b + 128],
+                       T.qa[:, a0 + c0:a0 + c1], T.sa[:, a0 + c0:a0 + c1], [tQE])
+                r = scp(T.dp[:, x0 + 448 * b + c0:x0 + 448 * b + c1], bank(b + 4 * h, c1 - c0), [t])
+                free[b + 4 * h].append(r)
+                tdp[b].append(r)
+        if n < 2:
+            if n == 0:
+                gs = siblings(1, tn, [tl, tTI[1]])
+            need("s", ("lane", 48 * (n + 1)))
+            gl = scp(lin(LO_), T.tp2[:, a0:a0 + 448].indirect(te[0]), [te[1], lastT[LO_], tTI[n + 1]])
+        else:
+            need("s", tlt)
+            ttp = done("s", S.activation(T.tpf[:], lin(LT_ + 2), AF.Identity, bias=224.0))
+            need("y", ttp)
+            Y.dma_start(T.tp[:, :], T.tpf[1::16, 0:448]).then_inc(T.sem.outs, 16)
+        x1, a1 = x0 + 1792, a0 + 448
+        sft, sgt = [], []
+
+        def meet(b, c0, c1):
+            return vtt(T.xs[:, x1 + 4 * c0 + b:x1 + 4 * c1:4],
+                       T.dp[:, x0 + 448 * b:x0 + 448 * b + 448].indirect(T.lu[:, u0 + c0 // 16:u0 + c1 // 16]),
+                       T.xs[:, x0 + 4 * c0 + b:x0 + 4 * c1:4], OP.add, [tl, tdp[b], tX[n]])
+        if n < 2:
+            tX[n + 1] = [meet(b, 0, 448) for b in range(4)]
+        for h in range(2):
+            c0, c1 = RUNS[h]
+            if n == 2:
+                tX[3] = [meet(b, c0, c1) for b in range(4)]
+            tQX[n + 1][h] = quant(T.qx, T.sx, a1 + c0, a1 + c1, T.xs[:, x1 + 4 * c0:x1 + 4 * c1], tX[n + 1])
+            if n < 2:
+                score(n + 1, h)
+                continue
+            need("y", tQX[3][h])
+            Y.dma_start(T.oc[:, 4 * c0:4 * c1], T.qx[:, a1 + c0:a1 + c1].bitcast(dt.uint8)).then_inc(T.sem.outs, 16)
+            k = mm(4 * h, c1 - c0, T.qv[:, 0:128], T.sv[:, 0:128], T.qx[:, a1 + c0:a1 + c1], T.sx[:, a1 + c0:a1 + c1],
+                   [tQV, tQX[3][h]])
+            need("s", scp(T.yo[:, c0:c1], bank(4 * h, c1 - c0), [k]))
+            S.dma_start(T.y[:, c0:c1], T.yo[:, c0:c1]).then_inc(T.sem.outs, 16)
+        if n < 2:
+            outs(n + 1, gl, None)
+    for k in range(4):
+        Y.dma_start(T.osc[4 * k:4 * k + 4, 0:448], T.sx[32 * k:32 * k + 4, 1344:1792]).then_inc(T.sem.outs, 16)
+    need("y", ("outs", 16 * 9), ("loc", nloc[0]), ("lww", 32), ("lvv", 16), [("c" + q, cnt[q]) for q in cnt])

@@ -2,12 +2,25 @@ from concourse.mybir import dt, AluOpType, ActivationFunctionType
 
 C = 448
 STEP = [1, 2, 3]
-R0 = 224
-RUNS = [(0, R0), (R0, C)]
+RUNS = [(0, 224), (224, C)]
+LANDS = [(0, 224), (224, C)]
+LAID = [(2, 0), (3, 0), (2, 1), (3, 1)]
+ZV = 224
+VE = False
+G1AT = 0
+HALVES = False
+COMB = False
+TW0 = 1
+Z2 = 0
+MW = 2
+VA = 0
+ONV = [(2,), (1,)]
+HALF = [(0, 224), (224, C)]
+TAIL = [(0, 160), (160, 320), (320, C)]
 TINY, UP = 2.0 ** -91, 1024.0
 LIN = 464
 TW = 928
-A_, B_, LO_, HI_, HS_, LT_ = 0, 1, 2, 3, 4, 5
+IN_, OUT_, LT_ = 0, 3, 6
 
 
 def _sb(n, d):
@@ -28,24 +41,22 @@ def _plane(n):
 
 SCRATCH = {
     "hin": _sb(28, "int32"), "tin": _sb(28, "int32"),
-    "ut": _bf(512), "vt": _bf(512), "ones": _bf(512), "et": _bf(2048),
+    "ut": _bf(512), "vt": _bf(512), "ones": _bf(516), "et": _bf(516),
     "xs": _bf(4 * 1792), "xp": _bf(3 * 1792), "yf": _sb(3 * 1792, "float32"),
-    "zt": _bf(3 * 1792), "ht": _bf(3 * 1792), "dp": _bf(3 * 1792),
-    "qu": _codes(128), "su": _plane(128), "qv": _codes(128), "sv": _plane(128),
+    "zt": _bf(3 * 1792), "ht": _bf(3 * 1792), "dp": _bf(3 * 1792), "dg": _bf(1792),
+    "qu0": _codes(128), "su0": _plane(128), "qu": _codes(128), "su": _plane(128), "qv": _codes(128), "sv": _plane(128),
     "wq": _codes(512), "wp": _plane(512), "qe": _codes(512), "se": _plane(512),
     "qx": _codes(4 * 448), "sx": _plane(4 * 448), "qz": _codes(3 * 448), "sz": _plane(3 * 448),
-    "qh": _codes(3 * 448), "sh": _plane(3 * 448), "qa": _codes(3 * 448), "sa": _plane(3 * 448),
-    "sf": _sb(3 * 448, "float32"), "sg": _sb(3 * 448, "float32"), "slo": _sb(3 * 448, "float32"),
-    "iot": _bf(448), "ln": _bf(8 * LIN + 16), "tt": _bf(6 * TW), "lg": _bf(11 * 448),
-    "tinv": _bf(4 * 448), "tp2": _bf(2 * 448), "tsw": _bf(4 * 448),
-    "seli": _sb(128, "int32"), "sel": _sb(8, "uint16"), "pg": _sb(8, "float32"),
-    "li": _sb(512, "int32"), "lu": _sb(1024, "uint16"), "lf": _sb(2560, "float32"), "bt": _bf(192),
+    "qh": _codes(3 * C), "sh": _plane(3 * C), "qa": _codes(3 * C), "sa": _plane(3 * C),
+    "sf": _sb(3 * 448, "float32"), "sl": _sb(3 * 896, "float32"), "ab": _bf(3 * 896), "abt": _bf(3 * 896),
+    "iot": _bf(448), "ln": _bf(9 * LIN + 16), "tt": _bf(9 * TW), "lg": _bf(12 * 448), "inv": _bf(4 * 448),
+    "li": _sb(512, "int32"), "lu": _sb(1024, "uint16"), "lf": _sb(2560, "float32"),
     "mu": _sb(192, "uint16"), "ma": _sb(192, "uint16"),
     "tpf": _sb(448, "float32"), "yo": _sb(448, "float32"),
     "ps": ("psum", [128, 4096], "float32"),
 }
-SEMAPHORES = (["cv", "cs", "ct", "cp", "loc", "ltl", "lhl", "lxx", "luu", "lww", "lvv", "lane", "outs"]
-              + ["ml%d" % n for n in range(3)] + ["ar%d" % n for n in range(3)])
+SEMAPHORES = (["cv", "cs", "ct", "cp", "loc", "ltl", "lhl", "lxx", "luu", "lww", "lvv", "outs", "sh3"]
+              + ["%s%d" % (k, n) for k in ["ml", "sh", "hr"] + ["a%d" % j for j in range(len(LANDS))] for n in range(3)])
 
 
 def rank_program(g, core, T, topo):
@@ -62,10 +73,13 @@ def rank_program(g, core, T, topo):
 
     def need(q, *toks):
         best = {}
-        for t in toks:
-            for a in (t if isinstance(t, list) else [t]):
-                if a is not None:
-                    best[a[0]] = max(best.get(a[0], 0), a[1])
+        todo = list(toks)
+        while todo:
+            a = todo.pop()
+            if isinstance(a, list):
+                todo += a
+            elif a is not None:
+                best[a[0]] = max(best.get(a[0], 0), a[1])
         for k, v in best.items():
             if seen[q].get(k, 0) < v:
                 Q[q].wait_ge(T.sem[k], v)
@@ -99,15 +113,27 @@ def rank_program(g, core, T, topo):
         need("v", *deps)
         return done("v", V.tensor_copy(out, in_))
 
+    def vturn(out, in_, deps):
+        need("v", *deps)
+        return done("v", V.transpose(out, in_))
+
     def scp(out, in_, deps, scale=None):
         need("s", *deps)
         if scale is None:
             return done("s", S.activation(out, in_, AF.Copy))
-        return done("s", S.activation(out, in_, AF.Copy, scale=scale))
+        return done("s", S.activation(out, in_, AF.Identity, scale=scale))
 
     def quant(qb, sb, a, b, tile, deps):
         need("v", *deps)
         return done("v", V.quantize_mx(qb[:, a:b], sb[:, a:b], tile))
+
+    def count(k, pattern, base, step):
+        n = 1
+        for s, c in pattern:
+            n *= c
+        a = take(k, n)
+        t = done("p", g.iota(tabs[k][:, a:a + n], pattern, base, step, allow_small_or_imprecise_dtypes=(k == "f")))
+        return a, t
 
     free = [[] for _ in range(8)]
 
@@ -119,154 +145,194 @@ def rank_program(g, core, T, topo):
     def bank(k, n):
         return T.ps[:, 512 * k:512 * k + n]
 
-    def lin(k):
-        return T.ln[:, LIN * k + 16:LIN * k + LIN]
+    def lin(k, a=0, b=C):
+        return T.ln[:, LIN * k + 16 + a:LIN * k + 16 + b]
 
-    Y.dma_start(T.tin[:], T.tl[:, :]).then_inc(T.sem.ltl, 16)
-    Y.dma_start(T.xs[:, 0:1792], T.x[:, :]).then_inc(T.sem.lxx, 16)
-    S.dma_start(T.hin[:], T.hl[:, :]).then_inc(T.sem.lhl, 16)
+    def inv(k):
+        return T.inv[:, 448 * k:448 * k + 448]
+
+    S.dma_start(T.tin[:], T.tl[:, :]).then_inc(T.sem.ltl, 16)
+    Y.dma_start(T.hin[:], T.hl[:, :]).then_inc(T.sem.lhl, 16)
     S.dma_start(T.ut[:], T.u[:, :]).then_inc(T.sem.luu, 16)
-    S.dma_start(T.wq[:, 0:512].bitcast(dt.uint8), T.wc[:, :]).then_inc(T.sem.lww, 16)
-    S.dma_start(T.wp[:], T.ws[:, :]).then_inc(T.sem.lww, 16)
-    S.dma_start(T.vt[:], T.v[:, :]).then_inc(T.sem.lvv, 16)
+    Y.dma_start(T.xs[:, 0:1792], T.x[:, :]).then_inc(T.sem.lxx, 16)
     TL, HL, LX, LU, LW, LV = ("ltl", 16), ("lhl", 16), ("lxx", 16), ("luu", 16), ("lww", 32), ("lvv", 16)
 
-    def si(k):
-        return T.seli[:, 8 * k:8 * k + 8]
-    iP = done("p", g.iota(si(0), [[0, 8]], 0, 1))
-    iC = done("p", g.iota(si(1), [[0, 4], [16, 2]], 0, 0))
-    iL = done("p", g.iota(si(2), [[1, 2], [0, 4]], 0, 0))
+    a, iP = count("i", [[0, 8]], 0, 1)
+    part = T.li[:, a:a + 8]
+    a, iU = count("i", [[32, 4], [0, 2]], 0, 0)
+    upos = T.li[:, a:a + 8]
+    d0, iD = count("f", [[8, 2], [0, 2], [256, 2]], 0, 0)
+    count("f", [[8, 2], [0, 2], [256, 2]], 1, 0)
+    a, iD = count("f", [[1, 2], [256, 2]], 0, 0)
+    p0, iB = count("f", [[448, 2], [1, 2], [256, 2]], 0, 0)
+    e0, iE = count("f", [[32, 14], [0, 2]], -224, 0)
+    w0, iW = count("f", [[0, 2], [256, 32]], -3584, 0)
     tIOT = done("p", g.iota(T.iot[:], [[1, 448]], -224, 0, allow_small_or_imprecise_dtypes=True))
-    iw0 = cols("f", 64)
-    iW = done("p", g.iota(iw0, [[0, 2], [16, 32]], -224, 1, allow_small_or_imprecise_dtypes=True))
     tONE = done("v", V.memset(T.ones[:], 1.0))
-    pads = None
-    for k in range(9):
-        pads = done("v", V.memset(T.ln[:, LIN * k:LIN * k + 16], 0.0))
-    for b in range(4):
-        need("p", tONE)
-        tE = done("p", g.affine_select(T.et[:, 512 * b:512 * b + 512], T.ones[:], [[1, 512]], OP.is_equal, 0.0, -b, -4))
-    a1 = vts(si(3), si(0), 15, OP.bitwise_and, [iP])
-    a2 = vts(si(4), si(0), 16, OP.bitwise_and, [iP])
-    a3 = vts(si(5), si(0), 4, OP.arith_shift_right, [iP])
-    a4 = vtt(si(6), si(1), si(3), OP.add, [iC, a1])
-    a5 = vtt(si(7), si(0), si(5), OP.add, [iP, a3])
-    a6 = vtt(si(8), si(4), si(2), OP.add, [iL, a2])
-    a7 = vts(si(9), si(7), 1, OP.bitwise_and, [a5])
-    a8 = vtt(si(10), si(6), si(9), OP.add, [a4, a7])
-    a9 = vts(si(11), si(9), 448, OP.mult, [a7])
-    a10 = vts(si(12), si(10), 1, OP.arith_shift_right, [a8])
-    a11 = vtt(si(13), si(8), si(11), OP.add, [a6, a9])
-    a12 = vts(si(14), si(12), 32, OP.mult, [a10])
-    a13 = vtt(T.pg[:], si(0), si(3), OP.subtract, [a1])
-    a14 = vtt(si(15), si(14), si(13), OP.add, [a12, a11])
-    IW = cols("f", 64)
-    tIW = vts(IW, iw0, T.pg[:, 0:1], OP.subtract, [iW, a13], TINY, OP.mult)
-    tSEL = vts(T.sel[:], si(15), TW - 1, OP.min, [a14])
-    SEL, SEL2 = T.sel[:, 2:6], T.sel[:, 0:8]
 
-    lastT = {}
-    lastSel = {}
+    def word(k, in0, s1, op0, deps, s2=None, op1=None, n=8):
+        o = cols(k, n)
+        return o, vts(o, in0, s1, op0, deps, s2, op1)
 
-    def turn(k, slot, deps):
-        a, o = LIN * k, TW * slot
-        need("v", pads, lastSel.get(slot), *deps)
-        done("v", V.transpose(T.tt[:, o:o + 448], T.ln[:, a + 16:a + 464]))
-        t2 = done("v", V.transpose(T.tt[:, o + 448:o + TW], T.ln[:, a:a + 480]))
-        lastT[k] = t2
-        return t2
+    def column(x, y, deps):
+        a = take("f", 8)
+        return T.lf[:, a:a + 1], vtt(T.lf[:, a:a + 8], x, y, OP.add, deps)
 
-    def picked(slot, table=SEL):
-        return T.tt[:, TW * slot:TW * slot + TW].indirect(table)
+    lane, c1 = word("i", part, 15, OP.bitwise_and, [iP])
+    grp, c2 = word("i", part, 4, OP.arith_shift_right, [iP])
+    odd2, c3 = word("i", part, 3, OP.arith_shift_right, [iP], 2, OP.bitwise_and)
+    p32, c4 = word("i", part, 31, OP.bitwise_and, [iP])
+    nine, c5 = word("i", lane, 9, OP.mult, [c1])
+    a = take("f", 8)
+    lane16, L16 = T.lf[:, a:a + 8], T.lf[:, a:a + 1]
+    c6 = vts(lane16, lane, 16, OP.mult, [c1])
+    mix = cols("i", 8)
+    c7 = vtt(mix, part, grp, OP.add, [c2])
+    pair, c8 = word("i", nine, 17, OP.bitwise_and, [c5])
+    flip, c9 = word("i", mix, 1, OP.bitwise_and, [c7])
+    a = take("f", 8)
+    P32 = T.lf[:, a:a + 1]
+    c12 = vcp(T.lf[:, a:a + 8], p32, [c4])
+    CP, c13 = column(lane16, odd2, [c6, c3])
+    f464, c11 = word("f", flip, 464, OP.mult, [c9])
+    ul = cols("i", 8)
+    c10 = vtt(ul, upos, pair, OP.add, [iU, c8])
+    BP, c14 = column(lane16, f464, [c6, c11])
+    UL = cols("u", 8)
+    tUL = vcp(UL, ul, [c10])
+    pads = [scp(T.ln[:, LIN * k:LIN * k + 16], T.ones[:, 0:16], [tONE]) for k in range(10)]
+    a = take("f", 16)
+    M0, M1 = T.lf[:, a:a + 1], T.lf[:, a + 8:a + 9]
+    vts(T.lf[:, a:a + 8], lane, 0, OP.is_equal, [c1])
+    tMASK = vts(T.lf[:, a + 8:a + 16], lane, 1, OP.is_equal, [c1])
+    a = take("u", 20)
+    tSEL = vts(T.lu[:, a:a + 20], T.lf[:, d0:d0 + 20], BP, OP.add, [iD, c14], TW - 1, OP.min)
+    ONE, TWO, THREE, FOUR, SELW = [T.lu[:, a + 4 * k:a + 4 * k + 4] for k in range(5)]
+    s0 = take("u", 28)
+    tSELF = vts(T.lu[:, s0:s0 + 28], T.lf[:, e0:e0 + 28], P32, OP.add, [iE, c12], 224.0, OP.add)
+    SELF = [T.lu[:, s0:s0 + (c1 - c0) // 16] for c0, c1 in HALF]
 
-    def wrap(out, slot, deps, table=SEL):
-        t = vts(out, picked(slot, table), 224.0, OP.add, [tSEL] + deps)
-        lastSel[slot] = t
-        return t
-
-    def firsts(l32, deps):
-        b, e, u = cols("i", 28), cols("i", 28), cols("u", 28)
-        t1 = vts(b, l32, 1, OP.bitwise_and, deps)
-        t2 = vtt(e, l32, b, OP.subtract, [t1])
-        return u, vcp(u, e, [t2])
-
-    tab = [{}, {}, {}]
-
-    def sibling(n, deps):
-        d = tab[n]
-        t = turn(HS_, HS_, deps)
-        a = take("u", 64)
-        d["hs"], d["th"] = T.lu[:, a:a + 28], cols("f", 64)
-        d["ths"] = vts(T.lu[:, a:a + 64], picked(HS_), 1.0 / TINY, OP.mult, [tSEL, t], 224.0, OP.add)
-        d["tth"] = vtt(d["th"], picked(HS_), IW, OP.subtract, [t, tIW])
-        lastSel[HS_] = d["tth"]
-
-    def outs(n, gl, gh):
-        d = tab[n]
-        a = take("f", 256)
-        p, q = T.lf[:, a:a + 64], T.lf[:, a + 64:a + 128]
-        t1 = turn(LO_, LO_, [gl])
-        if gh is None:
-            t1 = t2 = wrap(T.lf[:, a:a + 128], LO_, [t1], SEL2)
-        else:
-            t2 = turn(HI_, HI_, [gh])
-            t1 = wrap(p, LO_, [t1])
-            t2 = wrap(q, HI_, [t2])
-        d["LO"], d["HI"] = T.lf[:, a + 128:a + 192], T.lf[:, a + 192:a + 256]
-        d["tLO"] = vtt(d["LO"], p, q, OP.min, [t1, t2])
-        d["tHI"] = vtt(d["HI"], p, q, OP.max, [t1, t2])
-        d["lo"], d["hi"] = cols("u", 28), cols("u", 28)
-        d["tlo"] = vcp(d["lo"], T.lf[:, a + 128:a + 156], [d["tLO"]])
-        d["thi"] = vcp(d["hi"], T.lf[:, a + 192:a + 220], [d["tHI"]])
-
-    def tinv(k):
-        return T.tinv[:, 448 * k:448 * k + 448]
-
-    def siblings(k, u, deps):
-        o = 448 * k
-        t1 = scp(T.tsw[:, o:o + 448:2], T.tinv[:, o + 1:o + 448:2], deps)
-        t2 = scp(T.tsw[:, o + 1:o + 448:2], T.tinv[:, o:o + 448:2], deps)
-        return scp(lin(HS_), T.tsw[:, o:o + 448].indirect(u), [t1, t2, pads, lastT.get(HS_)], scale=TINY)
-
-    hlin = [T.lg[:, 448 * 9:448 * 10], T.lg[:, 448 * 10:448 * 11]]
-    hrow = [T.lg[1::16, 448 * 9:448 * 10], T.lg[1::16, 448 * 10:448 * 11], T.ln[1::16, LIN * LT_ + 16:LIN * LT_ + LIN]]
     tu, hu = cols("u", 28), cols("u", 28)
     ttu = vcp(tu, T.tin[:], [TL])
+
+    def evens(l32, deps):
+        e, u = cols("i", 28), cols("u", 28)
+        return u, vcp(u, e, [vts(e, l32, 510, OP.bitwise_and, deps)]), e
+
+    tinv = [None]
+
+    def invert(u, deps):
+        k = len(tinv)
+        t = vcp(inv(k).indirect(u), T.iot[:], deps + [tIOT])
+        need("y", t)
+        r = 448 * k
+        Y.dma_start(T.inv[8::16, r:r + 447], T.inv[2::16, r + 1:r + 448]).then_inc(T.sem["sh%d" % k], 16)
+        if COMB and k > 1:
+            need("y", tinv[k - 1])
+            Y.dma_start(T.inv[1::8, r:r + 448], T.inv[0::8, r - 448:r]).then_inc(T.sem["sh%d" % k], 16)
+        tinv.append(("sh%d" % k, 32 if COMB and k > 1 else 16))
+
+    invert(tu, [ttu])
+    Y.dma_start(T.wq[:, 0:512].bitcast(dt.uint8), T.wc[:, :]).then_inc(T.sem.lww, 16)
+    Y.dma_start(T.wp[:], T.ws[:, :]).then_inc(T.sem.lww, 16)
+    Y.dma_start(T.vt[:], T.v[:, :]).then_inc(T.sem.lvv, 16)
+    e0_, e1, e2, he, hx = cols("i", 28), cols("i", 28), cols("i", 28), cols("u", 28), cols("u", 28)
+    t0 = vts(e0_, T.hin[:], 510, OP.bitwise_and, [HL])
     thu = vcp(hu, T.hin[:], [HL])
-    thl = [scp(hlin[0], T.iot[:].indirect(hu), [thu, tIOT]), scp(hlin[1], T.iot[:].indirect(tu), [ttu]), None]
-    he, the = firsts(T.hin[:], [HL])
-    ho = cols("u", 28)
-    tho = vts(ho, he, 1.0, OP.add, [the])
-    tTI = [vcp(tinv(0).indirect(tu), T.iot[:], [ttu, tIOT])]
-    tHI = vcp(tinv(3).indirect(hu), T.iot[:], [thu, tIOT])
-    gl = scp(lin(LO_), tinv(0).indirect(he), [tTI[0], the, pads])
-    gh = scp(lin(HI_), tinv(0).indirect(ho), [tTI[0], tho])
-    gs = siblings(3, hu, [tHI, thu])
-    tQU = quant(T.qu, T.su, 0, 128, T.ut[:], [LU])
+    tq = quant(T.qu0, T.su0, 0, 128, T.ut[:], [LU])
+    t = vts(e1, e0_, 2, OP.mult, [t0], 1, OP.add)
+    pairs = [(he, vcp(he, e0_, [t0]))]
+    t = vtt(e2, e1, T.hin[:], OP.subtract, [t])
+    tQU = [vcp(T.qu[:, 0:128].bitcast(dt.uint32), T.qu0[:, 0:128].bitcast(dt.uint32).indirect(UL), [tq, tUL])]
+    thx = vcp(hx, e2, [t])
+    tHI = vcp(inv(0).indirect(hu), T.iot[:], [thu])
+
+    def hm(n):
+        return T.lg[:, 448 * (9 + n):448 * (10 + n)]
+
+    thl = [None, scp(hm(1), T.iot[:].indirect(tu), [ttu, tIOT, tMASK], scale=M1), None]
+    thl[0] = scp(hm(0), T.iot[:].indirect(hu), [thu], scale=M1)
+    tQU.append(scp(T.su[:, 0:128], T.su0[:, 0:128].indirect(UL), [tq, tUL]))
     tX = [[LX], [], [], []]
     tQX = [[None, None] for _ in range(4)]
-    t0 = quant(T.qx, T.sx, 0, 448, T.xs[:, 0:1792], [LX])
-    tQX[0] = [t0, t0]
-    sft, sgt = [], []
+    sft, slf = [[], [], []], [[], [], []]
 
-    def score(n, h):
-        c0, c1 = RUNS[h]
+    def score(n, h, onv=False):
+        c0, c1 = HALF[h]
         a = 448 * n
         t = mm(4 * h, c1 - c0, T.qu[:, 0:128], T.su[:, 0:128], T.qx[:, a + c0:a + c1], T.sx[:, a + c0:a + c1],
                [tQU, tQX[n][h]])
-        r1 = scp(T.sf[:, a + c0:a + c1], bank(4 * h, c1 - c0), [t], scale=UP)
-        r2 = scp(T.sg[:, a + c0:a + c1], bank(4 * h, c1 - c0), [t], scale=UP)
-        free[4 * h] += [r1, r2]
-        sft.append(r1)
-        sgt.append(r2)
+        if onv:
+            r = vts(T.sf[:, a + c0:a + c1], bank(4 * h, c1 - c0), UP, OP.mult, [t])
+        else:
+            r = scp(T.sf[:, a + c0:a + c1], bank(4 * h, c1 - c0), [t], scale=UP)
+        free[4 * h].append(r)
+        sft[n].append(r)
 
-    score(0, 0)
-    score(0, 1)
-    outs(0, gl, gh)
-    sibling(0, [gs])
+    def selves(n, h, onv=False):
+        c0, c1 = HALF[h]
+        slf[n].append((scp, vcp)[onv](T.sl[:, 896 * n + c0:896 * n + c1],
+                                      T.sf[:, 448 * n + c0:448 * n + c1].indirect(SELF[h]), [sft[n][h], tSELF]))
+
+    def ends(k, n, w):
+        return scp(lin(k), inv(w).indirect(pairs[n][0]), [tinv[w], pairs[n][1]], scale=TINY)
+
+    tOUT = ends(OUT_, 0, 1)
+    tIN = scp(lin(IN_), inv(0).indirect(hx), [tHI, thx], scale=TINY)
+    for h in range(2):
+        c0, c1 = HALF[h]
+        tQX[0][h] = quant(T.qx, T.sx, c0, c1, T.xs[:, 4 * c0:4 * c1], [LX])
+        score(0, h)
+    selves(0, 0)
+    selves(0, 1)
+    IW, tIW = word("f", T.lf[:, w0:w0 + 64], L16, OP.add, [iW, c6], TINY / 16, OP.mult, n=64)
+    SELB, tSELB = word("u", T.lf[:, p0:p0 + 8], CP, OP.add, [iB, c13], 895, OP.min)
+
+    tXP = [[], [], []]
+
+    def plane(n, b, deps):
+        need("p", *deps)
+        x0 = 1792 * n
+        tXP[n].append(done("p", g.affine_select(T.xp[:, x0 + 448 * b:x0 + 448 * b + 448], T.xs[:, x0 + b:x0 + 1792:4],
+                                                [[0, 448]], OP.is_ge, 0.0, 0, 0)))
+
+    need("p", tONE)
+    tE = done("p", g.affine_select(T.et[:], T.ones[:], [[1, 516]], OP.is_equal, 0.0, -3, -4))
+    for b in range(4):
+        plane(0, b, [LX])
+
+    def turn(k, half, deps):
+        a, o = LIN * k, TW * k
+        if half == 0:
+            return vturn(T.tt[:, o:o + 448], T.ln[:, a + 16:a + 464], deps)
+        return vturn(T.tt[:, o + 448:o + TW], T.ln[:, a:a + 480], deps + [pads])
+
+    def whole(out, in_, deps):
+        return vts(out, in_, 1.0 / TINY, OP.mult, deps, 224.0, OP.add)
+
+    tab = [{}, {}, {}]
+
+    def siblings(n, k, r0, t1, t2):
+        d = tab[n]
+        o = TW * k
+        d["th"] = a = take("f", 128)
+        s1, s2, q = cols("f", 28), cols("f", 28), cols("f", 64)
+        d["sib"] = cols("u", 28)
+        t = vtt(s1, T.tt[:, o + r0:o + 448:16], EM, OP.subtract, [t1, tEM])
+        r = vtt(q, T.tt[:, o:o + TW].indirect((ONE, THREE)[r0]), IW2, OP.subtract, [t2, tIW, tSEL])
+        t = vtt(s2, T.tt[:, o + r0 + 8:o + 448:16], s1, OP.add, [t])
+        d["tth"] = vtt(T.lf[:, a:a + 64], T.tt[:, o:o + TW].indirect((TWO, FOUR)[r0]), q, OP.add, [r])
+        d["tsib"] = whole(d["sib"], s2, [t])
+
+    def first_siblings():
+        d = tab[0]
+        d["th"] = a = take("f", 128)
+        d["sib"] = cols("u", 28)
+        t1, t2 = turn(IN_, 0, [tIN]), turn(IN_, 1, [tIN])
+        d["tsib"] = whole(d["sib"], T.tt[:, TW * IN_:TW * IN_ + 448:16], [t1])
+        d["tth"] = vtt(T.lf[:, a:a + 64], T.tt[:, TW * IN_:TW * IN_ + TW].indirect(ONE), IW, OP.subtract, [t2, tIW, tSEL])
 
     nloc = [0]
-    told = {}
 
     def send(dst, out, in_, sem):
         rid, pid, _ = topo.addr(dst)
@@ -277,139 +343,178 @@ def rank_program(g, core, T, topo):
         d = tab[n]
         mate = T.cores[rank ^ STEP[n]]
         eng = len(topo.engines(core, mate))
-        x0, a0 = 1792 * n, 448 * n
-        sf, sg, slo = T.sf[:, a0:a0 + 448], T.sg[:, a0:a0 + 448], T.slo[:, a0:a0 + 448]
-        ts = scp(slo, sf.indirect(d["lo"]), [sft, d["tlo"]])
-        tXP = []
-        for b in range(4):
-            tXP.append(scp(T.xp[:, x0 + 448 * b:x0 + 448 * b + 448], T.xs[:, x0 + b:x0 + 1792:4], [tX[n]]))
+        x0, a0, b0 = 1792 * n, 448 * n, 896 * n
+        sf = T.sf[:, a0:a0 + 448]
+        o = TW * (OUT_ + n)
+        out0, out1 = cols("u", 28), cols("u", 28)
+        t1 = turn(OUT_ + n, 0, [tOUT])
+        t2 = turn(OUT_ + n, 1, [tOUT])
+        to0 = whole(out0, T.tt[:, o:o + 448:16], [t1])
+        to1 = whole(out1, T.tt[:, o + 8:o + 448:16], [t1])
+        if VA and n > 0:
+            score(n, 1, True)
+            selves(n, 1, VA == 2)
+        gout = scp(T.sl[:, b0 + 448:b0 + 896], sf.indirect(out0), [to0, sft[n]])
         if n == 0:
-            gs = siblings(0, tu, [ttu, tTI[0]])
-        ta = vtt(lin(A_), sf.indirect(d["hs"]), sg, OP.subtract, [sft, sgt, d["ths"], lastT.get(A_), pads])
-        tb = vtt(lin(B_), sf.indirect(d["hi"]), slo, OP.is_gt, [ts, d["thi"], lastT.get(B_)])
-        ta = turn(A_, A_, [ta])
-        tb = turn(B_, B_, [tb])
-        ba = T.bt[:, 64 * n:64 * n + 64]
-        t = vtt(ba, picked(A_), d["th"], OP.is_gt, [ta, d["tth"], tSEL])
-        lastSel[A_] = t
+            first_siblings()
+            pairs.append(evens(T.tin[:], [TL]))
+        if n < 2 and not COMB:
+            tIN = ends(IN_ + n + 1, n + 1, n + 1)
+        if n > 0 and COMB:
+            siblings(n, OUT_ + n, 1, t1, t2)
+        a = d["th"]
+        th, dl, first = T.lf[:, a:a + 128], T.lf[:, a + 64:a + 128], cols("f", 64)
+        tf = vcp(first, T.tt[:, o:o + TW].indirect(ONE), [t2, tSEL])
+        ta = vtt(T.ab[:, b0:b0 + 448], sf.indirect(d["sib"]), T.sl[:, b0:b0 + 448], OP.subtract,
+                 [sft[n], slf[n], d["tsib"]])
+        td = vtt(dl, T.tt[:, o:o + TW].indirect(TWO), first, OP.subtract, [tf])
+        tb = vtt(T.ab[:, b0 + 448:b0 + 896], sf.indirect(out1), T.sl[:, b0 + 448:b0 + 896], OP.subtract, [gout, to1])
+        t = vturn(T.abt[:, b0:b0 + 896], T.ab[:, b0:b0 + 896], [ta, tb])
+        a = take("f", 128)
+        t = vtt(T.lf[:, a:a + 128], T.abt[:, b0:b0 + 896].indirect(SELB), th, OP.is_gt, [t, td, d["tth"], tSELB])
         e, w, m = cols("f", 64), cols("f", 64), cols("f", 64)
-        t = vtt(e, picked(B_), ba, OP.not_equal, [tb, t])
-        lastSel[B_] = t
-        t = vtt(w, e, d["HI"], OP.mult, [t, d["tHI"]])
-        t = vtt(m, w, d["LO"], OP.max, [t, d["tLO"]])
-        tm = vcp(T.mu[:, 64 * n:64 * n + 64], m, [t])
-        m0, m1 = T.mu[:, 64 * n:64 * n + 28], T.mu[:, 64 * n + 32:64 * n + 60]
+        t = vtt(e, T.lf[:, a:a + 64], T.lf[:, a + 64:a + 128], OP.not_equal, [t])
+        t = vtt(w, e, dl, OP.mult, [t])
+        t = vtt(m, w, first, OP.add, [t])
+        u = 64 * n
+        tm = whole(T.mu[:, u:u + 64], m, [t])
+        m0, m1 = T.mu[:, u:u + 28], T.mu[:, u + 32:u + 60]
         need("p", tm)
-        send(mate, T.ma[:, 64 * n:64 * n + 64], T.mu[:, 64 * n:64 * n + 64], "ml%d" % n)
+        send(mate, T.ma[:, u:u + 64], T.mu[:, u:u + 64], "ml%d" % n)
         G = [T.lg[:, 448 * (3 * n + k):448 * (3 * n + k) + 448] for k in range(3)]
-        tg1 = scp(G[0], T.iot[:].indirect(m1), [tm, tIOT])
+        tg0 = scp(G[0], T.iot[:].indirect(m1), [tm], scale=M0)
         tz = []
         for b in range(4):
             p = x0 + 448 * b
             yp = T.yf[:, p:p + 448]
-            ty = vtt(yp, T.xp[:, p:p + 448].indirect(m1), T.xs[:, x0 + b:x0 + 1792:4], OP.add, [tm, tXP[b], tX[n]])
-            if b < 3:
+            ty = vtt(yp, T.xp[:, p:p + 448].indirect(m1), T.xs[:, x0 + b:x0 + 1792:4], OP.add, [tm, tXP[n][b], tX[n]])
+            k = u + ZV // 16
+            if b < 3 - Z2:
                 tz.append(scp(T.zt[:, x0 + b:x0 + 1792:4], yp.indirect(m0), [ty], scale=0.5))
+                continue
+            if b == 3:
+                tza = vts(T.zt[:, x0 + b:x0 + 4 * ZV:4], yp.indirect(T.mu[:, u:k]), 0.5, OP.mult, [ty])
             else:
-                u = 64 * n + R0 // 16
-                tza = vts(T.zt[:, x0 + b:x0 + 4 * R0:4], yp.indirect(T.mu[:, 64 * n:u]), 0.5, OP.mult, [ty])
-                tzb = scp(T.zt[:, x0 + 4 * R0 + b:x0 + 1792:4], yp.indirect(T.mu[:, u:64 * n + 28]), [ty], scale=0.5)
-        tq = [quant(T.qz, T.sz, a0, a0 + R0, T.zt[:, x0:x0 + 4 * R0], tz + [tza]),
-              quant(T.qz, T.sz, a0 + R0, a0 + 448, T.zt[:, x0 + 4 * R0:x0 + 1792], tz + [tzb])]
-        tg2 = scp(G[1], G[0].indirect(m0), [tg1])
-        need("y", tg2, thl[n])
-        Y.dma_start(T.lg[1::16, 448 * (3 * n + 1):448 * (3 * n + 2)], hrow[n]).then_inc(T.sem.lane, 16)
-        for h in range(2):
-            c0, c1 = RUNS[h]
-            tr = [mm(b + 4 * h, c1 - c0, T.wq[:, 128 * b:128 * b + 128], T.wp[:, 128 * b:128 * b + 128],
+                tz.append(scp(T.zt[:, x0 + b:x0 + 4 * ZV:4], yp.indirect(T.mu[:, u:k]), [ty], scale=0.5))
+            tzb = scp(T.zt[:, x0 + 4 * ZV + b:x0 + 1792:4], yp.indirect(T.mu[:, k:u + 28]), [ty], scale=0.5)
+        tq = [quant(T.qz, T.sz, a0 + c0, a0 + c1, T.zt[:, x0 + 4 * c0:x0 + 4 * c1], tz + [tza, tzb if c1 > ZV else None])
+              for c0, c1 in RUNS]
+        if G1AT < 0:
+            need("y", scp(G[1], G[0].indirect(m0), [tg0]), thl[n])
+            k = 448 * (3 * n + 1)
+            Y.dma_start(T.lg[1::16, k:k + 448], T.lg[1::16, 448 * (9 + n):448 * (10 + n)] if n < 2 else
+                        T.ln[1::16, LIN * LT_ + 16:LIN * LT_ + LIN]).then_inc(T.sem["hr%d" % n], 16)
+            tg1 = ("hr%d" % n, 16)
+        for h, (c0, c1) in enumerate(RUNS):
+            if h == G1AT:
+                tg1 = vtt(G[1], G[0].indirect(m0), hm(n), OP.add, [tg0, thl[n]])
+            k = 4 * h % 8
+            tr = [mm(b + k, c1 - c0, T.wq[:, 128 * b:128 * b + 128], T.wp[:, 128 * b:128 * b + 128],
                      T.qz[:, a0 + c0:a0 + c1], T.sz[:, a0 + c0:a0 + c1], [LW, tq[h]]) for b in range(4)]
-            th = []
+            tH = []
             for b in range(4):
                 o = T.ht[:, x0 + 4 * c0 + b:x0 + 4 * c1:4]
-                if h == 0 and b < 2:
-                    r = vts(o, bank(b + 4 * h, c1 - c0), 0.03125, OP.mult, [tr[b]])
+                if b in ONV[h]:
+                    r = vts(o, bank(b + k, c1 - c0), 0.03125, OP.mult, [tr[b]])
                 else:
-                    r = scp(o, bank(b + 4 * h, c1 - c0), [tr[b]], scale=0.03125)
-                free[b + 4 * h].append(r)
-                th.append(r)
-            r = quant(T.qh, T.sh, a0 + c0, a0 + c1, T.ht[:, x0 + 4 * c0:x0 + 4 * c1], th)
-            need("p", r)
-            send(mate, T.qa[:, a0 + c0:a0 + c1].bitcast(dt.uint8), T.qh[:, a0 + c0:a0 + c1].bitcast(dt.uint8), "ar%d" % n)
-            if h == 0 and n == 0:
-                te = firsts(T.tin[:], [TL])
-            elif h == 0 and n == 1:
-                l32 = cols("i", 28)
-                te = firsts(l32, [vcp(l32, told["u"], [told["t"]])])
-        send(mate, T.sa[:, a0:a0 + 448], T.sh[:, a0:a0 + 448], "ar%d" % n)
+                    r = scp(o, bank(b + k, c1 - c0), [tr[b]], scale=0.03125)
+                free[b + k].append(r)
+                tH.append(r)
+            need("p", quant(T.qh, T.sh, a0 + c0, a0 + c1, T.ht[:, x0 + 4 * c0:x0 + 4 * c1], tH))
+            j = [j for j, (s0, s1) in enumerate(LANDS) if s0 <= c0 < s1][0]
+            s0, s1 = LANDS[j]
+            send(mate, T.qa[:, a0 + c0:a0 + c1].bitcast(dt.uint8), T.qh[:, a0 + c0:a0 + c1].bitcast(dt.uint8), "a%d%d" % (j, n))
+            if c1 == s1:
+                send(mate, T.sa[:, a0 + s0:a0 + s1], T.sh[:, a0 + s0:a0 + s1], "a%d%d" % (j, n))
+        if G1AT == len(RUNS):
+            tg1 = vtt(G[1], G[0].indirect(m0), hm(n), OP.add, [tg0, thl[n]])
+        need("s", ("ml%d" % n, eng))
+        if HALVES:
+            need("v", ("ml%d" % n, eng))
+            k = 448 * (3 * n + 2)
+            t = [vcp(T.lg[:, k:k + 224], G[1].indirect(T.ma[:, u + 32:u + 46]), [tg1]),
+                 scp(T.lg[:, k + 224:k + 448], G[1].indirect(T.ma[:, u + 46:u + 60]), [tg1])]
+            tlt = [vcp(lin(LT_ + n, 0, 224), G[2].indirect(T.ma[:, u:u + 14]), [t]),
+                   scp(lin(LT_ + n, 224, 448), G[2].indirect(T.ma[:, u + 14:u + 28]), [t])]
+        else:
+            t = scp(G[2], G[1].indirect(T.ma[:, u + 32:u + 60]), [tg1])
+            tlt = scp(lin(LT_ + n), G[2].indirect(T.ma[:, u:u + 28]), [t])
         if n == 0:
-            scp(T.tp2[:, 0:448], T.iot[:], [tIOT])
-            tTP = scp(T.tp2[:, 448:896], T.iot[:], [tIOT])
-            tQE = quant(T.qe, T.se, 0, 512, T.et[:], [tE])
-            tQV = quant(T.qv, T.sv, 0, 128, T.vt[:], [LV])
-        if n < 2:
-            sibling(n + 1, [gs])
-        need("s", ("ml%d" % n, eng), ("lane", 48 * n + 16))
-        am0, am1 = T.ma[:, 64 * n:64 * n + 28], T.ma[:, 64 * n + 32:64 * n + 60]
-        t = scp(G[2], G[1].indirect(am1), [tg2])
-        tlt = scp(lin(LT_ + n), G[2].indirect(am0), [t, pads])
-        t = turn(LT_ + n, LT_, [tlt])
+            EM, tEM = word("f", T.lf[:, e0:e0 + 28], P32, OP.add, [iE, c12], TINY, OP.mult, n=28)
+            IW2, tIW = word("f", T.lf[:, w0:w0 + 64], L16, OP.add, [iW, c6], TINY / 8, OP.mult, n=64)
+        if n < 2 and not COMB:
+            siblings(n + 1, IN_ + n + 1, 0, turn(IN_ + n + 1, 0, [tIN]), turn(IN_ + n + 1, 1, [tIN]))
+        if n == 0:
+            tQE = [quant(T.qe, T.se, 128 * b, 128 * b + 128, T.et[:, 3 - b:515 - b], [tE]) for b in range(4)]
+        t1, t2 = turn(LT_ + n, 0, [tlt]), turn(LT_ + n, 1, [tlt])
+        o = TW * (LT_ + n)
         u0 = take("u", 64)
-        tl = wrap(T.lu[:, u0:u0 + 64], LT_, [t])
-        tn = T.lu[:, u0 + 32:u0 + 60]
-        told = {"u": tn, "t": tl}
+        tl = vts(T.lu[:, u0:u0 + 64], T.tt[:, o:o + TW].indirect(SELW), 224.0, OP.add, [t1, t2])
+        if n < 2:
+            invert(T.lu[:, u0 + 32:u0 + 60], [tl])
         if n == 0:
-            thl[2] = tlt
-        if n < 2:
-            tTI.append(vcp(tinv(n + 1).indirect(tn), T.iot[:], [tl]))
-            need("y", tTI[n + 1], tTP)
-            r = 448 * (n + 1)
-            Y.dma_start(T.tp2[0::16, r - 448:r], T.tinv[0::16, r:r + 448]).then_inc(T.sem.lane, 16)
-            Y.dma_start(T.tp2[1::16, r - 448:r - 1], T.tinv[1::16, r + 1:r + 448]).then_inc(T.sem.lane, 16)
+            l32 = cols("i", 28)
+            pairs.append(evens(l32, [vcp(l32, T.lu[:, u0 + 32:u0 + 60], [tl])]))
+        if n == 2:
+            tQV = quant(T.qv, T.sv, 0, 128, T.vt[:], [LV])
         tdp = [[], [], [], []]
-        need("t", ("ar%d" % n, 3 * eng))
-        for b in range(4):
-            for h in range(2):
-                c0, c1 = RUNS[h]
-                t = mm(b + 4 * h, c1 - c0, T.qe[:, 128 * b:128 * b + 128], T.se[:, 128 * b:128 * b + 128],
+        for h, (c0, c1) in enumerate(LANDS):
+            need("t", ("a%d%d" % (h, n), eng * (1 + len([r for r in RUNS if c0 <= r[0] < c1]))))
+            for b in range(4):
+                k = (b + 4 * h) % 8
+                t = mm(k, c1 - c0, T.qe[:, 128 * b:128 * b + 128], T.se[:, 128 * b:128 * b + 128],
                        T.qa[:, a0 + c0:a0 + c1], T.sa[:, a0 + c0:a0 + c1], [tQE])
-                r = scp(T.dp[:, x0 + 448 * b + c0:x0 + 448 * b + c1], bank(b + 4 * h, c1 - c0), [t])
-                free[b + 4 * h].append(r)
+                r = (scp, vcp)[b == 0 and c1 == C and VE](T.dp[:, x0 + 448 * b + c0:x0 + 448 * b + c1], bank(k, c1 - c0), [t])
+                free[k].append(r)
                 tdp[b].append(r)
+        if n == 0:
+            thl[2] = scp(hm(2), lin(LT_), [tlt], scale=M1) if G1AT >= 0 else tlt
+        laid = {}
+        for b, h in LAID:
+            c0, c1 = (HALF if n < 2 else TAIL)[h]
+            laid[(b, c0)] = scp(T.dg[:, 448 * b + c0:448 * b + c1], T.dp[:, x0 + 448 * b:x0 + 448 * b + 448].indirect(
+                T.lu[:, u0 + c0 // 16:u0 + c1 // 16]), [tl, tdp[b], tX[n]])
         if n < 2:
-            if n == 0:
-                gs = siblings(1, tn, [tl, tTI[1]])
-            need("s", ("lane", 48 * (n + 1)))
-            gl = scp(lin(LO_), T.tp2[:, a0:a0 + 448].indirect(te[0]), [te[1], lastT[LO_], tTI[n + 1]])
+            tOUT = ends(OUT_ + n + 1, n + 1, n + 2)
         else:
             need("s", tlt)
             ttp = done("s", S.activation(T.tpf[:], lin(LT_ + 2), AF.Identity, bias=224.0))
             need("y", ttp)
             Y.dma_start(T.tp[:, :], T.tpf[1::16, 0:448]).then_inc(T.sem.outs, 16)
         x1, a1 = x0 + 1792, a0 + 448
-        sft, sgt = [], []
 
         def meet(b, c0, c1):
+            if (b, c0) in laid:
+                return vtt(T.xs[:, x1 + 4 * c0 + b:x1 + 4 * c1:4], T.dg[:, 448 * b + c0:448 * b + c1],
+                           T.xs[:, x0 + 4 * c0 + b:x0 + 4 * c1:4], OP.add, [laid[(b, c0)]])
             return vtt(T.xs[:, x1 + 4 * c0 + b:x1 + 4 * c1:4],
                        T.dp[:, x0 + 448 * b:x0 + 448 * b + 448].indirect(T.lu[:, u0 + c0 // 16:u0 + c1 // 16]),
                        T.xs[:, x0 + 4 * c0 + b:x0 + 4 * c1:4], OP.add, [tl, tdp[b], tX[n]])
         if n < 2:
-            tX[n + 1] = [meet(b, 0, 448) for b in range(4)]
-        for h in range(2):
-            c0, c1 = RUNS[h]
-            if n == 2:
-                tX[3] = [meet(b, c0, c1) for b in range(4)]
-            tQX[n + 1][h] = quant(T.qx, T.sx, a1 + c0, a1 + c1, T.xs[:, x1 + 4 * c0:x1 + 4 * c1], tX[n + 1])
-            if n < 2:
-                score(n + 1, h)
-                continue
-            need("y", tQX[3][h])
+            for b in range(MW):
+                tX[n + 1].append(meet(b, 0, C))
+                plane(n + 1, b, [tX[n + 1][b]])
+            for h in range(2):
+                c0, c1 = HALF[h]
+                for b in range(MW, 4):
+                    tX[n + 1].append(meet(b, c0, c1))
+                    if h == 1:
+                        plane(n + 1, b, [tX[n + 1]])
+                tQX[n + 1][h] = quant(T.qx, T.sx, a1 + c0, a1 + c1, T.xs[:, x1 + 4 * c0:x1 + 4 * c1], tX[n + 1])
+                if h == 0 or not VA:
+                    score(n + 1, h)
+                    selves(n + 1, h)
+            continue
+        t0 = [meet(b, 0, C) for b in range(TW0)]
+        for h, (c0, c1) in enumerate(TAIL):
+            t = [meet(b, c0, c1) for b in range(TW0, 4)] + t0
+            t = quant(T.qx, T.sx, a1 + c0, a1 + c1, T.xs[:, x1 + 4 * c0:x1 + 4 * c1], t)
+            need("y", t)
             Y.dma_start(T.oc[:, 4 * c0:4 * c1], T.qx[:, a1 + c0:a1 + c1].bitcast(dt.uint8)).then_inc(T.sem.outs, 16)
-            k = mm(4 * h, c1 - c0, T.qv[:, 0:128], T.sv[:, 0:128], T.qx[:, a1 + c0:a1 + c1], T.sx[:, a1 + c0:a1 + c1],
-                   [tQV, tQX[3][h]])
-            need("s", scp(T.yo[:, c0:c1], bank(4 * h, c1 - c0), [k]))
+            k = mm(h, c1 - c0, T.qv[:, 0:128], T.sv[:, 0:128], T.qx[:, a1 + c0:a1 + c1], T.sx[:, a1 + c0:a1 + c1],
+                   [tQV, t])
+            need("s", scp(T.yo[:, c0:c1], bank(h, c1 - c0), [k]))
             S.dma_start(T.y[:, c0:c1], T.yo[:, c0:c1]).then_inc(T.sem.outs, 16)
-        if n < 2:
-            outs(n + 1, gl, None)
     for k in range(4):
         Y.dma_start(T.osc[4 * k:4 * k + 4, 0:448], T.sx[32 * k:32 * k + 4, 1344:1792]).then_inc(T.sem.outs, 16)
-    need("y", ("outs", 16 * 9), ("loc", nloc[0]), ("lww", 32), ("lvv", 16), [("c" + q, cnt[q]) for q in cnt])
+    need("y", ("outs", 16 * (5 + 2 * len(TAIL))), ("loc", nloc[0]), ("lww", 32), ("lvv", 16), [("c" + q, cnt[q]) for q in cnt])

@@ -3,20 +3,7 @@ from concourse.mybir import dt, AluOpType, ActivationFunctionType
 C = 448
 STEP = [1, 2, 3]
 RUNS = [(0, 224), (224, C)]
-LANDS = [(0, 224), (224, C)]
-LAID = [(2, 0), (3, 0), (2, 1), (3, 1)]
-ZV = 224
-VE = False
-G1AT = 0
-HALVES = False
-COMB = False
-TW0 = 1
-Z2 = 0
-MW = 2
-VA = 0
-ONV = [(2,), (1,)]
-HALF = [(0, 224), (224, C)]
-TAIL = [(0, 160), (160, 320), (320, C)]
+ONV = [(3,), (2, 3)]
 TINY, UP = 2.0 ** -91, 1024.0
 LIN = 464
 TW = 928
@@ -46,17 +33,17 @@ SCRATCH = {
     "zt": _bf(3 * 1792), "ht": _bf(3 * 1792), "dp": _bf(3 * 1792), "dg": _bf(1792),
     "qu0": _codes(128), "su0": _plane(128), "qu": _codes(128), "su": _plane(128), "qv": _codes(128), "sv": _plane(128),
     "wq": _codes(512), "wp": _plane(512), "qe": _codes(512), "se": _plane(512),
-    "qx": _codes(4 * 448), "sx": _plane(4 * 448), "qz": _codes(3 * 448), "sz": _plane(3 * 448),
+    "qx": _codes(4 * C), "sx": _plane(4 * C), "qz": _codes(3 * C), "sz": _plane(3 * C),
     "qh": _codes(3 * C), "sh": _plane(3 * C), "qa": _codes(3 * C), "sa": _plane(3 * C),
-    "sf": _sb(3 * 448, "float32"), "sl": _sb(3 * 896, "float32"), "ab": _bf(3 * 896), "abt": _bf(3 * 896),
-    "iot": _bf(448), "ln": _bf(9 * LIN + 16), "tt": _bf(9 * TW), "lg": _bf(12 * 448), "inv": _bf(4 * 448),
-    "li": _sb(512, "int32"), "lu": _sb(1024, "uint16"), "lf": _sb(2560, "float32"),
+    "sf": _sb(3 * C, "float32"), "sl": _sb(6 * C, "float32"), "ab": _bf(6 * C), "abt": _bf(6 * C), "bt": _bf(3 * 192),
+    "iot": _bf(C), "ln": _bf(9 * LIN + 16), "tt": _bf(9 * TW), "lg": _bf(12 * C), "inv": _bf(4 * C), "sw": _bf(2 * C),
+    "li": _sb(512, "int32"), "lu": _sb(1024, "uint16"), "lf": _sb(2048, "float32"),
     "mu": _sb(192, "uint16"), "ma": _sb(192, "uint16"),
-    "tpf": _sb(448, "float32"), "yo": _sb(448, "float32"),
+    "tpf": _sb(C, "float32"), "yo": _sb(C, "float32"),
     "ps": ("psum", [128, 4096], "float32"),
 }
-SEMAPHORES = (["cv", "cs", "ct", "cp", "loc", "ltl", "lhl", "lxx", "luu", "lww", "lvv", "outs", "sh3"]
-              + ["%s%d" % (k, n) for k in ["ml", "sh", "hr"] + ["a%d" % j for j in range(len(LANDS))] for n in range(3)])
+SEMAPHORES = (["cv", "cs", "ct", "cp", "loc", "ltl", "lhl", "lxx", "luu", "lww", "lvv", "outs"]
+              + ["%s%d" % (k, n) for k in ("ml", "on", "a0", "a1") for n in range(3)])
 
 
 def rank_program(g, core, T, topo):
@@ -145,11 +132,11 @@ def rank_program(g, core, T, topo):
     def bank(k, n):
         return T.ps[:, 512 * k:512 * k + n]
 
-    def lin(k, a=0, b=C):
-        return T.ln[:, LIN * k + 16 + a:LIN * k + 16 + b]
+    def lin(k):
+        return T.ln[:, LIN * k + 16:LIN * k + LIN]
 
     def inv(k):
-        return T.inv[:, 448 * k:448 * k + 448]
+        return T.inv[:, C * k:C * k + C]
 
     S.dma_start(T.tin[:], T.tl[:, :]).then_inc(T.sem.ltl, 16)
     Y.dma_start(T.hin[:], T.hl[:, :]).then_inc(T.sem.lhl, 16)
@@ -159,178 +146,163 @@ def rank_program(g, core, T, topo):
 
     a, iP = count("i", [[0, 8]], 0, 1)
     part = T.li[:, a:a + 8]
+    tIOT = done("p", g.iota(T.iot[:], [[1, C]], -224, 0, allow_small_or_imprecise_dtypes=True))
     a, iU = count("i", [[32, 4], [0, 2]], 0, 0)
     upos = T.li[:, a:a + 8]
     d0, iD = count("f", [[8, 2], [0, 2], [256, 2]], 0, 0)
-    count("f", [[8, 2], [0, 2], [256, 2]], 1, 0)
     a, iD = count("f", [[1, 2], [256, 2]], 0, 0)
-    p0, iB = count("f", [[448, 2], [1, 2], [256, 2]], 0, 0)
-    e0, iE = count("f", [[32, 14], [0, 2]], -224, 0)
+    p0, iB = count("f", [[C, 2], [1, 2], [256, 2]], 0, 0)
+    e0, iE = count("f", [[32, 7], [0, 2]], 0, 0)
     w0, iW = count("f", [[0, 2], [256, 32]], -3584, 0)
-    tIOT = done("p", g.iota(T.iot[:], [[1, 448]], -224, 0, allow_small_or_imprecise_dtypes=True))
     tONE = done("v", V.memset(T.ones[:], 1.0))
 
     def word(k, in0, s1, op0, deps, s2=None, op1=None, n=8):
-        o = cols(k, n)
-        return o, vts(o, in0, s1, op0, deps, s2, op1)
+        a = take(k, n)
+        return tabs[k][:, a:a + n], vts(tabs[k][:, a:a + n], in0, s1, op0, deps, s2, op1), tabs[k][:, a:a + 1]
 
-    def column(x, y, deps):
-        a = take("f", 8)
-        return T.lf[:, a:a + 1], vtt(T.lf[:, a:a + 8], x, y, OP.add, deps)
+    def both(k, x, y, deps):
+        a = take(k, 8)
+        return tabs[k][:, a:a + 8], vtt(tabs[k][:, a:a + 8], x, y, OP.add, deps), tabs[k][:, a:a + 1]
 
-    lane, c1 = word("i", part, 15, OP.bitwise_and, [iP])
-    grp, c2 = word("i", part, 4, OP.arith_shift_right, [iP])
-    odd2, c3 = word("i", part, 3, OP.arith_shift_right, [iP], 2, OP.bitwise_and)
-    p32, c4 = word("i", part, 31, OP.bitwise_and, [iP])
-    nine, c5 = word("i", lane, 9, OP.mult, [c1])
-    a = take("f", 8)
-    lane16, L16 = T.lf[:, a:a + 8], T.lf[:, a:a + 1]
-    c6 = vts(lane16, lane, 16, OP.mult, [c1])
-    mix = cols("i", 8)
-    c7 = vtt(mix, part, grp, OP.add, [c2])
-    pair, c8 = word("i", nine, 17, OP.bitwise_and, [c5])
-    flip, c9 = word("i", mix, 1, OP.bitwise_and, [c7])
-    a = take("f", 8)
-    P32 = T.lf[:, a:a + 1]
-    c12 = vcp(T.lf[:, a:a + 8], p32, [c4])
-    CP, c13 = column(lane16, odd2, [c6, c3])
-    f464, c11 = word("f", flip, 464, OP.mult, [c9])
-    ul = cols("i", 8)
-    c10 = vtt(ul, upos, pair, OP.add, [iU, c8])
-    BP, c14 = column(lane16, f464, [c6, c11])
-    UL = cols("u", 8)
-    tUL = vcp(UL, ul, [c10])
+    lane, c1, _ = word("i", part, 15, OP.bitwise_and, [iP])
+    grp, c2, _ = word("i", part, 4, OP.arith_shift_right, [iP])
+    odd2, c3, _ = word("i", part, 3, OP.arith_shift_right, [iP], 2, OP.bitwise_and)
+    p32, c4, _ = word("i", part, 31, OP.bitwise_and, [iP])
+    nine, c5, _ = word("i", lane, 9, OP.mult, [c1])
+    lane16, c6, L16 = word("f", lane, 16, OP.mult, [c1])
+    mix, c7, _ = both("i", part, grp, [c2])
+    pair, c8, _ = word("i", nine, 17, OP.bitwise_and, [c5])
+    _, c10, P32 = word("f", p32, 0, OP.add, [c4])
+    flip, c9, _ = word("i", mix, 1, OP.bitwise_and, [c7])
+    _, c13, CP = both("f", lane16, odd2, [c6, c3])
+    _, _, M0 = word("f", lane, 0, OP.is_equal, [c1])
+    f464, c11, _ = word("f", flip, 464, OP.mult, [c9])
+    _, tMASK, M1 = word("f", lane, 1, OP.is_equal, [c1])
+    _, c14, BP = both("f", lane16, f464, [c6, c11])
     pads = [scp(T.ln[:, LIN * k:LIN * k + 16], T.ones[:, 0:16], [tONE]) for k in range(10)]
-    a = take("f", 16)
-    M0, M1 = T.lf[:, a:a + 1], T.lf[:, a + 8:a + 9]
-    vts(T.lf[:, a:a + 8], lane, 0, OP.is_equal, [c1])
-    tMASK = vts(T.lf[:, a + 8:a + 16], lane, 1, OP.is_equal, [c1])
-    a = take("u", 20)
-    tSEL = vts(T.lu[:, a:a + 20], T.lf[:, d0:d0 + 20], BP, OP.add, [iD, c14], TW - 1, OP.min)
-    ONE, TWO, THREE, FOUR, SELW = [T.lu[:, a + 4 * k:a + 4 * k + 4] for k in range(5)]
-    s0 = take("u", 28)
-    tSELF = vts(T.lu[:, s0:s0 + 28], T.lf[:, e0:e0 + 28], P32, OP.add, [iE, c12], 224.0, OP.add)
-    SELF = [T.lu[:, s0:s0 + (c1 - c0) // 16] for c0, c1 in HALF]
+    ul, c12, _ = both("i", upos, pair, [iU, c8])
 
     tu, hu = cols("u", 28), cols("u", 28)
     ttu = vcp(tu, T.tin[:], [TL])
-
-    def evens(l32, deps):
-        e, u = cols("i", 28), cols("u", 28)
-        return u, vcp(u, e, [vts(e, l32, 510, OP.bitwise_and, deps)]), e
-
     tinv = [None]
 
     def invert(u, deps):
         k = len(tinv)
-        t = vcp(inv(k).indirect(u), T.iot[:], deps + [tIOT])
-        need("y", t)
-        r = 448 * k
-        Y.dma_start(T.inv[8::16, r:r + 447], T.inv[2::16, r + 1:r + 448]).then_inc(T.sem["sh%d" % k], 16)
-        if COMB and k > 1:
-            need("y", tinv[k - 1])
-            Y.dma_start(T.inv[1::8, r:r + 448], T.inv[0::8, r - 448:r]).then_inc(T.sem["sh%d" % k], 16)
-        tinv.append(("sh%d" % k, 32 if COMB and k > 1 else 16))
+        need("y", vcp(inv(k).indirect(u), T.iot[:], deps + [tIOT]))
+        Y.dma_start(T.inv[8::16, C * k:C * k + C - 1], T.inv[2::16, C * k + 1:C * k + C]).then_inc(T.sem["on%d" % (k - 1)], 16)
+        tinv.append(("on%d" % (k - 1), 16))
 
     invert(tu, [ttu])
     Y.dma_start(T.wq[:, 0:512].bitcast(dt.uint8), T.wc[:, :]).then_inc(T.sem.lww, 16)
     Y.dma_start(T.wp[:], T.ws[:, :]).then_inc(T.sem.lww, 16)
     Y.dma_start(T.vt[:], T.v[:, :]).then_inc(T.sem.lvv, 16)
-    e0_, e1, e2, he, hx = cols("i", 28), cols("i", 28), cols("i", 28), cols("u", 28), cols("u", 28)
-    t0 = vts(e0_, T.hin[:], 510, OP.bitwise_and, [HL])
+    UL, SELF = cols("u", 8), cols("u", 14)
+    tUL = vcp(UL, ul, [c12])
+    a = take("u", 12)
+    tSEL = vts(T.lu[:, a:a + 12], T.lf[:, d0:d0 + 12], BP, OP.add, [iD, c14], TW - 1, OP.min)
+    ONE, TWO, SELW = [T.lu[:, a + 4 * k:a + 4 * k + 4] for k in range(3)]
+    tSELF = vts(SELF, T.lf[:, e0:e0 + 14], P32, OP.add, [iE, c10])
+    even, odd, other, he, hx = cols("i", 28), cols("i", 28), cols("i", 28), cols("u", 28), cols("u", 28)
+    t0 = vts(even, T.hin[:], 510, OP.bitwise_and, [HL])
     thu = vcp(hu, T.hin[:], [HL])
     tq = quant(T.qu0, T.su0, 0, 128, T.ut[:], [LU])
-    t = vts(e1, e0_, 2, OP.mult, [t0], 1, OP.add)
-    pairs = [(he, vcp(he, e0_, [t0]))]
-    t = vtt(e2, e1, T.hin[:], OP.subtract, [t])
+    t = vts(odd, even, 2, OP.mult, [t0], 1, OP.add)
+    pairs = [(he, vcp(he, even, [t0]))]
+    t = vtt(other, odd, T.hin[:], OP.subtract, [t])
     tQU = [vcp(T.qu[:, 0:128].bitcast(dt.uint32), T.qu0[:, 0:128].bitcast(dt.uint32).indirect(UL), [tq, tUL])]
-    thx = vcp(hx, e2, [t])
+    thx = vcp(hx, other, [t])
     tHI = vcp(inv(0).indirect(hu), T.iot[:], [thu])
 
     def hm(n):
-        return T.lg[:, 448 * (9 + n):448 * (10 + n)]
+        return T.lg[:, C * (9 + n):C * (10 + n)]
 
     thl = [None, scp(hm(1), T.iot[:].indirect(tu), [ttu, tIOT, tMASK], scale=M1), None]
     thl[0] = scp(hm(0), T.iot[:].indirect(hu), [thu], scale=M1)
     tQU.append(scp(T.su[:, 0:128], T.su0[:, 0:128].indirect(UL), [tq, tUL]))
     tX = [[LX], [], [], []]
-    tQX = [[None, None] for _ in range(4)]
     sft, slf = [[], [], []], [[], [], []]
 
-    def score(n, h, onv=False):
-        c0, c1 = HALF[h]
-        a = 448 * n
-        t = mm(4 * h, c1 - c0, T.qu[:, 0:128], T.su[:, 0:128], T.qx[:, a + c0:a + c1], T.sx[:, a + c0:a + c1],
-               [tQU, tQX[n][h]])
-        if onv:
-            r = vts(T.sf[:, a + c0:a + c1], bank(4 * h, c1 - c0), UP, OP.mult, [t])
-        else:
-            r = scp(T.sf[:, a + c0:a + c1], bank(4 * h, c1 - c0), [t], scale=UP)
+    def score(n, h, deps):
+        c0, c1 = RUNS[h]
+        a = C * n
+        t = quant(T.qx, T.sx, a + c0, a + c1, T.xs[:, 1792 * n + 4 * c0:1792 * n + 4 * c1], deps)
+        t = mm(4 * h, c1 - c0, T.qu[:, 0:128], T.su[:, 0:128], T.qx[:, a + c0:a + c1], T.sx[:, a + c0:a + c1], [tQU, t])
+        r = scp(T.sf[:, a + c0:a + c1], bank(4 * h, c1 - c0), [t], scale=UP)
         free[4 * h].append(r)
         sft[n].append(r)
 
-    def selves(n, h, onv=False):
-        c0, c1 = HALF[h]
-        slf[n].append((scp, vcp)[onv](T.sl[:, 896 * n + c0:896 * n + c1],
-                                      T.sf[:, 448 * n + c0:448 * n + c1].indirect(SELF[h]), [sft[n][h], tSELF]))
+    def selves(n, h):
+        c0, c1 = RUNS[h]
+        slf[n].append(scp(T.sl[:, 2 * C * n + c0:2 * C * n + c1], T.sf[:, C * n + c0:C * n + c1].indirect(SELF),
+                          [sft[n][h], tSELF]))
 
-    def ends(k, n, w):
-        return scp(lin(k), inv(w).indirect(pairs[n][0]), [tinv[w], pairs[n][1]], scale=TINY)
+    def ends(n):
+        return scp(lin(OUT_ + n), inv(n + 1).indirect(pairs[n][0]), [tinv[n + 1], pairs[n][1]], scale=TINY)
 
-    tOUT = ends(OUT_, 0, 1)
+    tOUT = ends(0)
     tIN = scp(lin(IN_), inv(0).indirect(hx), [tHI, thx], scale=TINY)
-    for h in range(2):
-        c0, c1 = HALF[h]
-        tQX[0][h] = quant(T.qx, T.sx, c0, c1, T.xs[:, 4 * c0:4 * c1], [LX])
-        score(0, h)
+    score(0, 0, [LX])
+    score(0, 1, [LX])
     selves(0, 0)
     selves(0, 1)
-    IW, tIW = word("f", T.lf[:, w0:w0 + 64], L16, OP.add, [iW, c6], TINY / 16, OP.mult, n=64)
-    SELB, tSELB = word("u", T.lf[:, p0:p0 + 8], CP, OP.add, [iB, c13], 895, OP.min)
+    IW, tIW, _ = word("f", T.lf[:, w0:w0 + 64], L16, OP.add, [iW, c6], TINY / 16, OP.mult, n=64)
+    SELB, tSELB, _ = word("u", T.lf[:, p0:p0 + 8], CP, OP.add, [iB, c13], 2 * C - 1, OP.min)
 
     tXP = [[], [], []]
 
     def plane(n, b, deps):
         need("p", *deps)
         x0 = 1792 * n
-        tXP[n].append(done("p", g.affine_select(T.xp[:, x0 + 448 * b:x0 + 448 * b + 448], T.xs[:, x0 + b:x0 + 1792:4],
-                                                [[0, 448]], OP.is_ge, 0.0, 0, 0)))
+        tXP[n].append(done("p", g.affine_select(T.xp[:, x0 + C * b:x0 + C * b + C], T.xs[:, x0 + b:x0 + 1792:4],
+                                                [[0, C]], OP.is_ge, 0.0, 0, 0)))
 
     need("p", tONE)
     tE = done("p", g.affine_select(T.et[:], T.ones[:], [[1, 516]], OP.is_equal, 0.0, -3, -4))
     for b in range(4):
         plane(0, b, [LX])
 
-    def turn(k, half, deps):
+    def turn(k, deps):
         a, o = LIN * k, TW * k
-        if half == 0:
-            return vturn(T.tt[:, o:o + 448], T.ln[:, a + 16:a + 464], deps)
-        return vturn(T.tt[:, o + 448:o + TW], T.ln[:, a:a + 480], deps + [pads])
+        return (vturn(T.tt[:, o:o + C], T.ln[:, a + 16:a + LIN], deps),
+                vturn(T.tt[:, o + C:o + TW], T.ln[:, a:a + 480], [pads]))
+
+    def own(k, table):
+        return T.tt[:, TW * k:TW * k + TW].indirect(table)
+
+    def shared(k, r):
+        return T.tt[:, TW * k + r:TW * k + C:16]
 
     def whole(out, in_, deps):
         return vts(out, in_, 1.0 / TINY, OP.mult, deps, 224.0, OP.add)
 
-    tab = [{}, {}, {}]
+    def siblings(n, dep):
+        a, sib = take("f", 128), cols("u", 28)
+        t1, t2 = turn(IN_ + n, [dep])
+        t1 = whole(sib, shared(IN_ + n, 0), [t1])
+        return a, sib, t1, vtt(T.lf[:, a:a + 64], own(IN_ + n, ONE), IW, OP.subtract, [t2, tIW, tSEL])
 
-    def siblings(n, k, r0, t1, t2):
-        d = tab[n]
-        o = TW * k
-        d["th"] = a = take("f", 128)
-        s1, s2, q = cols("f", 28), cols("f", 28), cols("f", 64)
-        d["sib"] = cols("u", 28)
-        t = vtt(s1, T.tt[:, o + r0:o + 448:16], EM, OP.subtract, [t1, tEM])
-        r = vtt(q, T.tt[:, o:o + TW].indirect((ONE, THREE)[r0]), IW2, OP.subtract, [t2, tIW, tSEL])
-        t = vtt(s2, T.tt[:, o + r0 + 8:o + 448:16], s1, OP.add, [t])
-        d["tth"] = vtt(T.lf[:, a:a + 64], T.tt[:, o:o + TW].indirect((TWO, FOUR)[r0]), q, OP.add, [r])
-        d["tsib"] = whole(d["sib"], s2, [t])
+    tQE, tQV, last = [], [], [None]
 
-    def first_siblings():
-        d = tab[0]
-        d["th"] = a = take("f", 128)
-        d["sib"] = cols("u", 28)
-        t1, t2 = turn(IN_, 0, [tIN]), turn(IN_, 1, [tIN])
-        d["tsib"] = whole(d["sib"], T.tt[:, TW * IN_:TW * IN_ + 448:16], [t1])
-        d["tth"] = vtt(T.lf[:, a:a + 64], T.tt[:, TW * IN_:TW * IN_ + TW].indirect(ONE), IW, OP.subtract, [t2, tIW, tSEL])
+    def unit(b):
+        tQE.append(quant(T.qe, T.se, 128 * b, 128 * b + 128, T.et[:, 3 - b:515 - b], [tE]))
+
+    def evens(src, dep):
+        w, e, u = cols("i", 28), cols("i", 28), cols("u", 28)
+
+        def step(k):
+            if k == 0:
+                last[0] = vcp(w, src, [dep])
+            elif k == 1:
+                last[0] = vts(e, w, 510, OP.bitwise_and, [last[0]])
+            else:
+                pairs.append((u, vcp(u, e, [last[0]])))
+        return [lambda k=k: step(k) for k in range(3)]
+
+    spare = evens(tu, ttu) + [lambda b=b: unit(b) for b in range(4)]
+
+    def fill():
+        if spare:
+            spare.pop(0)()
 
     nloc = [0]
 
@@ -339,182 +311,142 @@ def rank_program(g, core, T, topo):
         g.remote_dma(out, in_, T.sem[sem], T.sem.loc, pid, rid, topo.mask(core, dst))
         nloc[0] += len(topo.engines(core, dst))
 
+    tails = tu
     for n in range(3):
-        d = tab[n]
         mate = T.cores[rank ^ STEP[n]]
         eng = len(topo.engines(core, mate))
-        x0, a0, b0 = 1792 * n, 448 * n, 896 * n
-        sf = T.sf[:, a0:a0 + 448]
-        o = TW * (OUT_ + n)
-        out0, out1 = cols("u", 28), cols("u", 28)
-        t1 = turn(OUT_ + n, 0, [tOUT])
-        t2 = turn(OUT_ + n, 1, [tOUT])
-        to0 = whole(out0, T.tt[:, o:o + 448:16], [t1])
-        to1 = whole(out1, T.tt[:, o + 8:o + 448:16], [t1])
-        if VA and n > 0:
-            score(n, 1, True)
-            selves(n, 1, VA == 2)
-        gout = scp(T.sl[:, b0 + 448:b0 + 896], sf.indirect(out0), [to0, sft[n]])
+        x0, a0, b0 = 1792 * n, C * n, 2 * C * n
+        sf = T.sf[:, a0:a0 + C]
+        out0, out1, first = cols("u", 28), cols("u", 28), cols("f", 64)
+        t1, t2 = turn(OUT_ + n, [tOUT])
+        to0 = whole(out0, shared(OUT_ + n, 0), [t1])
+        to1 = whole(out1, shared(OUT_ + n, 8), [t1])
+        tf = vcp(first, own(OUT_ + n, ONE), [t2, tSEL])
         if n == 0:
-            first_siblings()
-            pairs.append(evens(T.tin[:], [TL]))
-        if n < 2 and not COMB:
-            tIN = ends(IN_ + n + 1, n + 1, n + 1)
-        if n > 0 and COMB:
-            siblings(n, OUT_ + n, 1, t1, t2)
-        a = d["th"]
-        th, dl, first = T.lf[:, a:a + 128], T.lf[:, a + 64:a + 128], cols("f", 64)
-        tf = vcp(first, T.tt[:, o:o + TW].indirect(ONE), [t2, tSEL])
-        ta = vtt(T.ab[:, b0:b0 + 448], sf.indirect(d["sib"]), T.sl[:, b0:b0 + 448], OP.subtract,
-                 [sft[n], slf[n], d["tsib"]])
-        td = vtt(dl, T.tt[:, o:o + TW].indirect(TWO), first, OP.subtract, [tf])
-        tb = vtt(T.ab[:, b0 + 448:b0 + 896], sf.indirect(out1), T.sl[:, b0 + 448:b0 + 896], OP.subtract, [gout, to1])
-        t = vturn(T.abt[:, b0:b0 + 896], T.ab[:, b0:b0 + 896], [ta, tb])
-        a = take("f", 128)
-        t = vtt(T.lf[:, a:a + 128], T.abt[:, b0:b0 + 896].indirect(SELB), th, OP.is_gt, [t, td, d["tth"], tSELB])
-        e, w, m = cols("f", 64), cols("f", 64), cols("f", 64)
-        t = vtt(e, T.lf[:, a:a + 64], T.lf[:, a + 64:a + 128], OP.not_equal, [t])
-        t = vtt(w, e, dl, OP.mult, [t])
+            sibs = siblings(0, tIN)
+        else:
+            fill()
+        a, sib, tsib, tth = sibs
+        th, step = T.lf[:, a:a + 128], T.lf[:, a + 64:a + 128]
+        td = vtt(step, own(OUT_ + n, TWO), first, OP.subtract, [tf])
+        gout = scp(T.sl[:, b0 + C:b0 + 2 * C], sf.indirect(out0), [to0, sft[n]])
+        if n < 2:
+            r = C * (n + 1)
+            t = [scp(T.sw[:, a0:a0 + C:2], T.inv[:, r + 1:r + C:2], [tinv[n + 1]]),
+                 scp(T.sw[:, a0 + 1:a0 + C:2], T.inv[:, r:r + C:2], [])]
+            tIN = scp(lin(IN_ + n + 1), T.sw[:, a0:a0 + C].indirect(tails), [t], scale=TINY)
+        ta = vtt(T.ab[:, b0:b0 + C], sf.indirect(sib), T.sl[:, b0:b0 + C], OP.subtract, [sft[n], slf[n], tsib])
+        tb = vtt(T.ab[:, b0 + C:b0 + 2 * C], sf.indirect(out1), T.sl[:, b0 + C:b0 + 2 * C], OP.subtract, [gout, to1])
+        fill()
+        t = vturn(T.abt[:, b0:b0 + 2 * C], T.ab[:, b0:b0 + 2 * C], [ta, tb])
+        fill()
+        a = 192 * n
+        t = vtt(T.bt[:, a:a + 128], T.abt[:, b0:b0 + 2 * C].indirect(SELB), th, OP.is_gt, [t, td, tth, tSELB])
+        fill()
+        e, w, m = T.bt[:, a + 128:a + 192], cols("f", 64), cols("f", 64)
+        t = vtt(e, T.bt[:, a:a + 64], T.bt[:, a + 64:a + 128], OP.not_equal, [t])
+        fill()
+        t = vtt(w, e, step, OP.mult, [t])
+        fill()
         t = vtt(m, w, first, OP.add, [t])
+        fill()
         u = 64 * n
         tm = whole(T.mu[:, u:u + 64], m, [t])
+        fill()
         m0, m1 = T.mu[:, u:u + 28], T.mu[:, u + 32:u + 60]
         need("p", tm)
         send(mate, T.ma[:, u:u + 64], T.mu[:, u:u + 64], "ml%d" % n)
-        G = [T.lg[:, 448 * (3 * n + k):448 * (3 * n + k) + 448] for k in range(3)]
+        G = [T.lg[:, C * (3 * n + k):C * (3 * n + k) + C] for k in range(3)]
         tg0 = scp(G[0], T.iot[:].indirect(m1), [tm], scale=M0)
         tz = []
         for b in range(4):
-            p = x0 + 448 * b
-            yp = T.yf[:, p:p + 448]
-            ty = vtt(yp, T.xp[:, p:p + 448].indirect(m1), T.xs[:, x0 + b:x0 + 1792:4], OP.add, [tm, tXP[n][b], tX[n]])
-            k = u + ZV // 16
-            if b < 3 - Z2:
+            yp = T.yf[:, x0 + C * b:x0 + C * b + C]
+            ty = vtt(yp, T.xp[:, x0 + C * b:x0 + C * b + C].indirect(m1), T.xs[:, x0 + b:x0 + 1792:4], OP.add,
+                     [tm, tXP[n][b], tX[n]])
+            if b < 3:
                 tz.append(scp(T.zt[:, x0 + b:x0 + 1792:4], yp.indirect(m0), [ty], scale=0.5))
-                continue
-            if b == 3:
-                tza = vts(T.zt[:, x0 + b:x0 + 4 * ZV:4], yp.indirect(T.mu[:, u:k]), 0.5, OP.mult, [ty])
-            else:
-                tz.append(scp(T.zt[:, x0 + b:x0 + 4 * ZV:4], yp.indirect(T.mu[:, u:k]), [ty], scale=0.5))
-            tzb = scp(T.zt[:, x0 + 4 * ZV + b:x0 + 1792:4], yp.indirect(T.mu[:, k:u + 28]), [ty], scale=0.5)
-        tq = [quant(T.qz, T.sz, a0 + c0, a0 + c1, T.zt[:, x0 + 4 * c0:x0 + 4 * c1], tz + [tza, tzb if c1 > ZV else None])
-              for c0, c1 in RUNS]
-        if G1AT < 0:
-            need("y", scp(G[1], G[0].indirect(m0), [tg0]), thl[n])
-            k = 448 * (3 * n + 1)
-            Y.dma_start(T.lg[1::16, k:k + 448], T.lg[1::16, 448 * (9 + n):448 * (10 + n)] if n < 2 else
-                        T.ln[1::16, LIN * LT_ + 16:LIN * LT_ + LIN]).then_inc(T.sem["hr%d" % n], 16)
-            tg1 = ("hr%d" % n, 16)
+        tl3 = [vts(T.zt[:, x0 + 3:x0 + 896:4], yp.indirect(T.mu[:, u:u + 14]), 0.5, OP.mult, [ty]),
+               scp(T.zt[:, x0 + 899:x0 + 1792:4], yp.indirect(T.mu[:, u + 14:u + 28]), [ty], scale=0.5)]
+        tq = [quant(T.qz, T.sz, a0 + c0, a0 + c1, T.zt[:, x0 + 4 * c0:x0 + 4 * c1], tz + [tl3[h]])
+              for h, (c0, c1) in enumerate(RUNS)]
+        tg1 = vtt(G[1], G[0].indirect(m0), hm(n), OP.add, [tg0, thl[n]])
         for h, (c0, c1) in enumerate(RUNS):
-            if h == G1AT:
-                tg1 = vtt(G[1], G[0].indirect(m0), hm(n), OP.add, [tg0, thl[n]])
-            k = 4 * h % 8
-            tr = [mm(b + k, c1 - c0, T.wq[:, 128 * b:128 * b + 128], T.wp[:, 128 * b:128 * b + 128],
+            tr = [mm(b + 4 * h, c1 - c0, T.wq[:, 128 * b:128 * b + 128], T.wp[:, 128 * b:128 * b + 128],
                      T.qz[:, a0 + c0:a0 + c1], T.sz[:, a0 + c0:a0 + c1], [LW, tq[h]]) for b in range(4)]
             tH = []
             for b in range(4):
                 o = T.ht[:, x0 + 4 * c0 + b:x0 + 4 * c1:4]
                 if b in ONV[h]:
-                    r = vts(o, bank(b + k, c1 - c0), 0.03125, OP.mult, [tr[b]])
+                    r = vts(o, bank(b + 4 * h, c1 - c0), 0.03125, OP.mult, [tr[b]])
                 else:
-                    r = scp(o, bank(b + k, c1 - c0), [tr[b]], scale=0.03125)
-                free[b + k].append(r)
+                    r = scp(o, bank(b + 4 * h, c1 - c0), [tr[b]], scale=0.03125)
+                free[b + 4 * h].append(r)
                 tH.append(r)
             need("p", quant(T.qh, T.sh, a0 + c0, a0 + c1, T.ht[:, x0 + 4 * c0:x0 + 4 * c1], tH))
-            j = [j for j, (s0, s1) in enumerate(LANDS) if s0 <= c0 < s1][0]
-            s0, s1 = LANDS[j]
-            send(mate, T.qa[:, a0 + c0:a0 + c1].bitcast(dt.uint8), T.qh[:, a0 + c0:a0 + c1].bitcast(dt.uint8), "a%d%d" % (j, n))
-            if c1 == s1:
-                send(mate, T.sa[:, a0 + s0:a0 + s1], T.sh[:, a0 + s0:a0 + s1], "a%d%d" % (j, n))
-        if G1AT == len(RUNS):
-            tg1 = vtt(G[1], G[0].indirect(m0), hm(n), OP.add, [tg0, thl[n]])
+            send(mate, T.qa[:, a0 + c0:a0 + c1].bitcast(dt.uint8), T.qh[:, a0 + c0:a0 + c1].bitcast(dt.uint8), "a%d%d" % (h, n))
+            send(mate, T.sa[:, a0 + c0:a0 + c1], T.sh[:, a0 + c0:a0 + c1], "a%d%d" % (h, n))
         need("s", ("ml%d" % n, eng))
-        if HALVES:
-            need("v", ("ml%d" % n, eng))
-            k = 448 * (3 * n + 2)
-            t = [vcp(T.lg[:, k:k + 224], G[1].indirect(T.ma[:, u + 32:u + 46]), [tg1]),
-                 scp(T.lg[:, k + 224:k + 448], G[1].indirect(T.ma[:, u + 46:u + 60]), [tg1])]
-            tlt = [vcp(lin(LT_ + n, 0, 224), G[2].indirect(T.ma[:, u:u + 14]), [t]),
-                   scp(lin(LT_ + n, 224, 448), G[2].indirect(T.ma[:, u + 14:u + 28]), [t])]
-        else:
-            t = scp(G[2], G[1].indirect(T.ma[:, u + 32:u + 60]), [tg1])
-            tlt = scp(lin(LT_ + n), G[2].indirect(T.ma[:, u:u + 28]), [t])
+        t = scp(G[2], G[1].indirect(T.ma[:, u + 32:u + 60]), [tg1])
+        tlt = scp(lin(LT_ + n), G[2].indirect(T.ma[:, u:u + 28]), [t])
         if n == 0:
-            EM, tEM = word("f", T.lf[:, e0:e0 + 28], P32, OP.add, [iE, c12], TINY, OP.mult, n=28)
-            IW2, tIW = word("f", T.lf[:, w0:w0 + 64], L16, OP.add, [iW, c6], TINY / 8, OP.mult, n=64)
-        if n < 2 and not COMB:
-            siblings(n + 1, IN_ + n + 1, 0, turn(IN_ + n + 1, 0, [tIN]), turn(IN_ + n + 1, 1, [tIN]))
-        if n == 0:
-            tQE = [quant(T.qe, T.se, 128 * b, 128 * b + 128, T.et[:, 3 - b:515 - b], [tE]) for b in range(4)]
-        t1, t2 = turn(LT_ + n, 0, [tlt]), turn(LT_ + n, 1, [tlt])
-        o = TW * (LT_ + n)
-        u0 = take("u", 64)
-        tl = vts(T.lu[:, u0:u0 + 64], T.tt[:, o:o + TW].indirect(SELW), 224.0, OP.add, [t1, t2])
+            thl[2] = scp(hm(2), lin(LT_), [tlt], scale=M1)
         if n < 2:
-            invert(T.lu[:, u0 + 32:u0 + 60], [tl])
-        if n == 0:
-            l32 = cols("i", 28)
-            pairs.append(evens(l32, [vcp(l32, T.lu[:, u0 + 32:u0 + 60], [tl])]))
-        if n == 2:
-            tQV = quant(T.qv, T.sv, 0, 128, T.vt[:], [LV])
-        tdp = [[], [], [], []]
-        for h, (c0, c1) in enumerate(LANDS):
-            need("t", ("a%d%d" % (h, n), eng * (1 + len([r for r in RUNS if c0 <= r[0] < c1]))))
-            for b in range(4):
-                k = (b + 4 * h) % 8
-                t = mm(k, c1 - c0, T.qe[:, 128 * b:128 * b + 128], T.se[:, 128 * b:128 * b + 128],
-                       T.qa[:, a0 + c0:a0 + c1], T.sa[:, a0 + c0:a0 + c1], [tQE])
-                r = (scp, vcp)[b == 0 and c1 == C and VE](T.dp[:, x0 + 448 * b + c0:x0 + 448 * b + c1], bank(k, c1 - c0), [t])
-                free[k].append(r)
-                tdp[b].append(r)
-        if n == 0:
-            thl[2] = scp(hm(2), lin(LT_), [tlt], scale=M1) if G1AT >= 0 else tlt
-        laid = {}
-        for b, h in LAID:
-            c0, c1 = (HALF if n < 2 else TAIL)[h]
-            laid[(b, c0)] = scp(T.dg[:, 448 * b + c0:448 * b + c1], T.dp[:, x0 + 448 * b:x0 + 448 * b + 448].indirect(
-                T.lu[:, u0 + c0 // 16:u0 + c1 // 16]), [tl, tdp[b], tX[n]])
-        if n < 2:
-            tOUT = ends(OUT_ + n + 1, n + 1, n + 2)
+            sibs = siblings(n + 1, tIN)
         else:
             need("s", tlt)
-            ttp = done("s", S.activation(T.tpf[:], lin(LT_ + 2), AF.Identity, bias=224.0))
-            need("y", ttp)
-            Y.dma_start(T.tp[:, :], T.tpf[1::16, 0:448]).then_inc(T.sem.outs, 16)
-        x1, a1 = x0 + 1792, a0 + 448
+            need("y", done("s", S.activation(T.tpf[:], lin(LT_ + 2), AF.Identity, bias=224.0)))
+            Y.dma_start(T.tp[:, :], T.tpf[1::16, 0:C]).then_inc(T.sem.outs, 16)
+            tQV = quant(T.qv, T.sv, 0, 128, T.vt[:], [LV])
+        u0 = take("u", 64)
+        tl = vts(T.lu[:, u0:u0 + 64], own(LT_ + n, SELW), 224.0, OP.add, list(turn(LT_ + n, [tlt])))
+        if n < 2:
+            tails = T.lu[:, u0 + 32:u0 + 60]
+            invert(tails, [tl])
+        if n == 0:
+            spare += evens(tails, tl)
+        tdp = [[], [], [], []]
+        for h, (c0, c1) in enumerate(RUNS):
+            need("t", ("a%d%d" % (h, n), 2 * eng))
+            for b in range(4):
+                t = mm(b + 4 * h, c1 - c0, T.qe[:, 128 * b:128 * b + 128], T.se[:, 128 * b:128 * b + 128],
+                       T.qa[:, a0 + c0:a0 + c1], T.sa[:, a0 + c0:a0 + c1], [tQE])
+                r = (scp, vcp)[(n, h, b) == (2, 1, 0)](T.dp[:, x0 + C * b + c0:x0 + C * b + c1], bank(b + 4 * h, c1 - c0), [t])
+                free[b + 4 * h].append(r)
+                tdp[b].append(r)
+
+        def far(b, c0, c1):
+            return T.dp[:, x0 + C * b:x0 + C * b + C].indirect(T.lu[:, u0 + c0 // 16:u0 + c1 // 16])
+
+        laid = {(b, c0): scp(T.dg[:, C * b + c0:C * b + c1], far(b, c0, c1), [tl, tdp[b], tX[n]])
+                for c0, c1 in RUNS for b in (2, 3)}
+        if n < 2:
+            tOUT = ends(n + 1)
+        x1, a1 = x0 + 1792, a0 + C
 
         def meet(b, c0, c1):
-            if (b, c0) in laid:
-                return vtt(T.xs[:, x1 + 4 * c0 + b:x1 + 4 * c1:4], T.dg[:, 448 * b + c0:448 * b + c1],
-                           T.xs[:, x0 + 4 * c0 + b:x0 + 4 * c1:4], OP.add, [laid[(b, c0)]])
-            return vtt(T.xs[:, x1 + 4 * c0 + b:x1 + 4 * c1:4],
-                       T.dp[:, x0 + 448 * b:x0 + 448 * b + 448].indirect(T.lu[:, u0 + c0 // 16:u0 + c1 // 16]),
-                       T.xs[:, x0 + 4 * c0 + b:x0 + 4 * c1:4], OP.add, [tl, tdp[b], tX[n]])
-        if n < 2:
-            for b in range(MW):
-                tX[n + 1].append(meet(b, 0, C))
-                plane(n + 1, b, [tX[n + 1][b]])
-            for h in range(2):
-                c0, c1 = HALF[h]
-                for b in range(MW, 4):
-                    tX[n + 1].append(meet(b, c0, c1))
-                    if h == 1:
-                        plane(n + 1, b, [tX[n + 1]])
-                tQX[n + 1][h] = quant(T.qx, T.sx, a1 + c0, a1 + c1, T.xs[:, x1 + 4 * c0:x1 + 4 * c1], tX[n + 1])
-                if h == 0 or not VA:
-                    score(n + 1, h)
-                    selves(n + 1, h)
-            continue
-        t0 = [meet(b, 0, C) for b in range(TW0)]
-        for h, (c0, c1) in enumerate(TAIL):
-            t = [meet(b, c0, c1) for b in range(TW0, 4)] + t0
-            t = quant(T.qx, T.sx, a1 + c0, a1 + c1, T.xs[:, x1 + 4 * c0:x1 + 4 * c1], t)
+            in0, deps = (T.dg[:, C * b + c0:C * b + c1], [laid[b, c0]]) if b > 1 else (far(b, c0, c1), [tl, tdp[b], tX[n]])
+            t = vtt(T.xs[:, x1 + 4 * c0 + b:x1 + 4 * c1:4], in0, T.xs[:, x0 + 4 * c0 + b:x0 + 4 * c1:4], OP.add, deps)
+            tX[n + 1].append(t)
+            if n < 2 and c1 == C:
+                plane(n + 1, b, tX[n + 1])
+
+        at = 2 if n < 2 else 1
+        for b in range(at):
+            meet(b, 0, C)
+        for h, (c0, c1) in enumerate(RUNS):
+            for b in range(at, 4):
+                meet(b, c0, c1)
+            if n < 2:
+                score(n + 1, h, tX[n + 1])
+                selves(n + 1, h)
+                continue
+            t = quant(T.qx, T.sx, a1 + c0, a1 + c1, T.xs[:, x1 + 4 * c0:x1 + 4 * c1], tX[3])
             need("y", t)
             Y.dma_start(T.oc[:, 4 * c0:4 * c1], T.qx[:, a1 + c0:a1 + c1].bitcast(dt.uint8)).then_inc(T.sem.outs, 16)
-            k = mm(h, c1 - c0, T.qv[:, 0:128], T.sv[:, 0:128], T.qx[:, a1 + c0:a1 + c1], T.sx[:, a1 + c0:a1 + c1],
-                   [tQV, t])
-            need("s", scp(T.yo[:, c0:c1], bank(h, c1 - c0), [k]))
+            for k in range(4 * h):
+                need("ys"[k % 2], t)
+                Q["ys"[k % 2]].dma_start(T.osc[4 * k:4 * k + 4, 0:C], T.sx[32 * k:32 * k + 4, a1:a1 + C]).then_inc(T.sem.outs, 16)
+            t = mm(h, c1 - c0, T.qv[:, 0:128], T.sv[:, 0:128], T.qx[:, a1 + c0:a1 + c1], T.sx[:, a1 + c0:a1 + c1], [tQV, t])
+            need("s", (scp, vcp)[h](T.yo[:, c0:c1], bank(h, c1 - c0), [t]))
             S.dma_start(T.y[:, c0:c1], T.yo[:, c0:c1]).then_inc(T.sem.outs, 16)
-    for k in range(4):
-        Y.dma_start(T.osc[4 * k:4 * k + 4, 0:448], T.sx[32 * k:32 * k + 4, 1344:1792]).then_inc(T.sem.outs, 16)
-    need("y", ("outs", 16 * (5 + 2 * len(TAIL))), ("loc", nloc[0]), ("lww", 32), ("lvv", 16), [("c" + q, cnt[q]) for q in cnt])
+    need("y", ("outs", 16 * 9), ("loc", nloc[0]), LW, LV, [("c" + q, cnt[q]) for q in cnt])

@@ -1,13 +1,30 @@
 from concourse.mybir import dt, AluOpType, ActivationFunctionType
 
-C = 448
+C, NV = 448, 224
 STEP = [1, 2, 3]
-RUNS = [(0, 224), (224, C)]
-ONV = [(3,), (2, 3)]
-TINY, UP = 2.0 ** -91, 1024.0
+LAYER = [(0, 128), (128, 288), (288, C)]
+STATE = [(0, 320), (320, C)]
+SENT = LAYER
+ZV = 192
+ORDER = ([("z", 0), ("m", 0), ("z", 1), ("m", 1), ("z", 2), ("g", 0), ("e", 2)]
+         + [("c", 0, b, "vvvs"[b]) for b in range(4)] + [("m", 2), ("h", 0)] + [("c", 1, b, "svss"[b]) for b in range(4)]
+         + [("h", 1)] + [("c", 2, b, "svsv"[b]) for b in range(4)] + [("h", 2), ("l", "s")])
+UNPACK = (0, 1, 2, 3)
+DONV = [[], [], [(0, 1), (0, 3), (1, 1), (1, 3), (2, 0), (2, 2)]]
+LAID = [(2, 0, 320), (3, 0, 320), (1, 320, C), (2, 320, C), (3, 320, C)]
+MEET = [(0, 0, C), (1, 0, 320), (2, 0, 320), (3, 0, 320), (1, 320, C), (None, 0, 320), (2, 320, C), (3, 320, C),
+        (None, 320, C)]
+LAST = [(0, 192), (192, 320), (320, C)]
+LAID2 = [(3, 0, 192), (2, 192, 320), (3, 192, 320), (1, 320, C), (2, 320, C), (3, 320, C)]
+MEET2 = ([(b, 0, 192) for b in range(4)] + [(0, 192, 320), (None, 0, 192)] + [(b, 192, 320) for b in (1, 2, 3)]
+         + [(0, 320, C), (None, 192, 320)] + [(b, 320, C) for b in (1, 2, 3)] + [(None, 320, C)])
+START = "xy1p1ptpptpppr0p0"
+PRE = 4
+HALVES = [(0, 96), (96, NV)]
 LIN = 464
 TW = 928
-IN_, OUT_, LT_ = 0, 3, 6
+SC = 5
+M_, LT_ = 0, 3
 
 
 def _sb(n, d):
@@ -31,19 +48,20 @@ SCRATCH = {
     "ut": _bf(512), "vt": _bf(512), "ones": _bf(516), "et": _bf(516),
     "xs": _bf(4 * 1792), "xp": _bf(3 * 1792), "yf": _sb(3 * 1792, "float32"),
     "zt": _bf(3 * 1792), "ht": _bf(3 * 1792), "dp": _bf(3 * 1792), "dg": _bf(1792),
-    "qu0": _codes(128), "su0": _plane(128), "qu": _codes(128), "su": _plane(128), "qv": _codes(128), "sv": _plane(128),
+    "qu": _codes(128), "su": _plane(128), "qv": _codes(128), "sv": _plane(128),
     "wq": _codes(512), "wp": _plane(512), "qe": _codes(512), "se": _plane(512),
     "qx": _codes(4 * C), "sx": _plane(4 * C), "qz": _codes(3 * C), "sz": _plane(3 * C),
     "qh": _codes(3 * C), "sh": _plane(3 * C), "qa": _codes(3 * C), "sa": _plane(3 * C),
-    "sf": _sb(3 * C, "float32"), "sl": _sb(6 * C, "float32"), "ab": _bf(6 * C), "abt": _bf(6 * C), "bt": _bf(3 * 192),
-    "iot": _bf(C), "ln": _bf(9 * LIN + 16), "tt": _bf(9 * TW), "lg": _bf(12 * C), "inv": _bf(4 * C), "sw": _bf(2 * C),
-    "li": _sb(512, "int32"), "lu": _sb(1024, "uint16"), "lf": _sb(2048, "float32"),
+    "sf": _sb(3 * C, "float32"), "sl": _sb(3 * C, "float32"), "bt": _bf(3 * C), "rk": _bf(4 * NV),
+    "d0": _sb(SC * NV, "float16"), "d1": _bf(SC * NV), "mt": _bf(3 * SC * NV),
+    "iot": _bf(C), "ln": _bf(6 * LIN + 16), "tt": _bf(6 * TW), "lg": _bf(8 * C), "inv": _bf(4 * C), "wr": _bf(128),
+    "li": _sb(512, "int32"), "lu": _sb(1024, "uint16"), "lf": _sb(1024, "float32"),
     "mu": _sb(192, "uint16"), "ma": _sb(192, "uint16"),
     "tpf": _sb(C, "float32"), "yo": _sb(C, "float32"),
     "ps": ("psum", [128, 4096], "float32"),
 }
 SEMAPHORES = (["cv", "cs", "ct", "cp", "loc", "ltl", "lhl", "lxx", "luu", "lww", "lvv", "outs"]
-              + ["%s%d" % (k, n) for k in ("ml", "on", "a0", "a1") for n in range(3)])
+              + ["%s%d" % (k, n) for k in ("ml", "on", "a0", "a1", "a2") for n in range(3)] + ["wr%d" % k for k in range(4)])
 
 
 def rank_program(g, core, T, topo):
@@ -110,6 +128,10 @@ def rank_program(g, core, T, topo):
             return done("s", S.activation(out, in_, AF.Copy))
         return done("s", S.activation(out, in_, AF.Identity, scale=scale))
 
+    def pcp(out, in_, n, deps):
+        need("p", *deps)
+        return done("p", g.affine_select(out, in_, [[0, n]], OP.is_ge, 0.0, 0, 0))
+
     def quant(qb, sb, a, b, tile, deps):
         need("v", *deps)
         return done("v", V.quantize_mx(qb[:, a:b], sb[:, a:b], tile))
@@ -120,7 +142,7 @@ def rank_program(g, core, T, topo):
             n *= c
         a = take(k, n)
         t = done("p", g.iota(tabs[k][:, a:a + n], pattern, base, step, allow_small_or_imprecise_dtypes=(k == "f")))
-        return a, t
+        return tabs[k][:, a:a + n], t
 
     free = [[] for _ in range(8)]
 
@@ -132,11 +154,8 @@ def rank_program(g, core, T, topo):
     def bank(k, n):
         return T.ps[:, 512 * k:512 * k + n]
 
-    def lin(k):
-        return T.ln[:, LIN * k + 16:LIN * k + LIN]
-
-    def inv(k):
-        return T.inv[:, C * k:C * k + C]
+    def lin(k, a=0, b=C):
+        return T.ln[:, LIN * k + 16 + a:LIN * k + 16 + b]
 
     S.dma_start(T.tin[:], T.tl[:, :]).then_inc(T.sem.ltl, 16)
     Y.dma_start(T.hin[:], T.hl[:, :]).then_inc(T.sem.lhl, 16)
@@ -144,166 +163,166 @@ def rank_program(g, core, T, topo):
     Y.dma_start(T.xs[:, 0:1792], T.x[:, :]).then_inc(T.sem.lxx, 16)
     TL, HL, LX, LU, LW, LV = ("ltl", 16), ("lhl", 16), ("lxx", 16), ("luu", 16), ("lww", 32), ("lvv", 16)
 
-    a, iP = count("i", [[0, 8]], 0, 1)
-    part = T.li[:, a:a + 8]
+    p17, iP = count("i", [[0, 2]], 0, 17)
+    lanes, iD = count("f", [[1, 3], [256, 2]], 0, 0)
+    pairs, iS = count("f", [[1, 2], [2, 14]], 0, 0)
     tIOT = done("p", g.iota(T.iot[:], [[1, C]], -224, 0, allow_small_or_imprecise_dtypes=True))
-    a, iU = count("i", [[32, 4], [0, 2]], 0, 0)
-    upos = T.li[:, a:a + 8]
-    d0, iD = count("f", [[8, 2], [0, 2], [256, 2]], 0, 0)
-    a, iD = count("f", [[1, 2], [256, 2]], 0, 0)
-    p0, iB = count("f", [[C, 2], [1, 2], [256, 2]], 0, 0)
-    e0, iE = count("f", [[32, 7], [0, 2]], 0, 0)
-    w0, iW = count("f", [[0, 2], [256, 32]], -3584, 0)
     tONE = done("v", V.memset(T.ones[:], 1.0))
+    need("p", tONE)
+    tE = done("p", g.affine_select(T.et[:], T.ones[:], [[1, 516]], OP.is_equal, 0.0, -3, -4))
 
-    def word(k, in0, s1, op0, deps, s2=None, op1=None, n=8):
-        a = take(k, n)
-        return tabs[k][:, a:a + n], vts(tabs[k][:, a:a + n], in0, s1, op0, deps, s2, op1), tabs[k][:, a:a + 1]
+    def word(k, in0, s1, op0, deps, s2=None, op1=None):
+        a = take(k, 2)
+        return tabs[k][:, a:a + 2], vts(tabs[k][:, a:a + 2], in0, s1, op0, deps, s2, op1), tabs[k][:, a:a + 1]
 
-    def both(k, x, y, deps):
-        a = take(k, 8)
-        return tabs[k][:, a:a + 8], vtt(tabs[k][:, a:a + 8], x, y, OP.add, deps), tabs[k][:, a:a + 1]
+    def fixed(k, w):
+        return vts(T.d0[:, k:SC * NV:SC], T.ones[:, 0:NV], w, OP.mult, [tONE])
 
-    lane, c1, _ = word("i", part, 15, OP.bitwise_and, [iP])
-    grp, c2, _ = word("i", part, 4, OP.arith_shift_right, [iP])
-    odd2, c3, _ = word("i", part, 3, OP.arith_shift_right, [iP], 2, OP.bitwise_and)
-    p32, c4, _ = word("i", part, 31, OP.bitwise_and, [iP])
-    nine, c5, _ = word("i", lane, 9, OP.mult, [c1])
-    lane16, c6, L16 = word("f", lane, 16, OP.mult, [c1])
-    mix, c7, _ = both("i", part, grp, [c2])
-    pair, c8, _ = word("i", nine, 17, OP.bitwise_and, [c5])
-    _, c10, P32 = word("f", p32, 0, OP.add, [c4])
-    flip, c9, _ = word("i", mix, 1, OP.bitwise_and, [c7])
-    _, c13, CP = both("f", lane16, odd2, [c6, c3])
-    _, _, M0 = word("f", lane, 0, OP.is_equal, [c1])
-    f464, c11, _ = word("f", flip, 464, OP.mult, [c9])
-    _, tMASK, M1 = word("f", lane, 1, OP.is_equal, [c1])
-    _, c14, BP = both("f", lane16, f464, [c6, c11])
-    pads = [scp(T.ln[:, LIN * k:LIN * k + 16], T.ones[:, 0:16], [tONE]) for k in range(10)]
-    ul, c12, _ = both("i", upos, pair, [iU, c8])
+    lane, c1, _ = word("i", p17, 15, OP.bitwise_and, [iP])
+    flip, c2, _ = word("i", p17, 4, OP.arith_shift_right, [iP], 1, OP.bitwise_and)
+    tC = [fixed(0, 0.0)]
+    _, c3, L16 = word("f", lane, 16, OP.mult, [c1])
+    tC.append(fixed(3, -1.0))
+    _, c4, BA = word("f", flip, C + 16, OP.mult, [c2, c3], L16, OP.add)
+    _, c5, L28 = word("f", lane, 28, OP.mult, [])
+    tC.append(fixed(4, 1.0))
+    pads = [scp(T.ln[:, LIN * k:LIN * k + 16], T.ones[:, 0:16], [tONE]) for k in range(7)]
+    a, EO = take("u", 6), take("u", 28)
+    tSEL = [vts(T.lu[:, a:a + 6], lanes, BA, OP.add, [iD, c4], TW - 1, OP.min),
+            vts(T.lu[:, EO:EO + 28], pairs, L28, OP.add, [iS, c5])]
+    SELM, SELL = T.lu[:, a:a + 4], T.lu[:, a + 2:a + 6]
+
+    tEO, ends, trk, tscan = [], {}, {}, [None]
+
+    def invert(k, u, deps):
+        t = vcp(T.inv[:, C * k:C * k + C].indirect(u), T.iot[:], deps + [tIOT])
+        need("y", t)
+        Y.dma_start(T.wr[:, 32 * k:32 * k + 28], T.inv[0::16, C * k:C * k + C]).then_inc(T.sem["wr%d" % k], 16)
+        return t
+
+    def side(out, k, i, deps):
+        return scp(out, T.inv[:, C * k:C * k + C].indirect(T.lu[:, EO + 14 * i:EO + 14 * i + 14]), deps + [tSEL])
+
+    def sides(k, ti):
+        tEO[:] = [side(T.d1[:, 2 + j:SC * NV:SC], k, j, [ti, tscan[0]]) for j in range(2)]
+
+    def rank_of(k):
+        return T.rk[:, NV * k:NV * k + NV]
+
+    def tables(k):
+        d, c = T.d0[:, 2:SC * NV:SC], T.d1[:, 1:SC * NV:SC]
+        tok = []
+        yield tok
+        tok.append(vtt(d, T.d1[:, 3:SC * NV:SC], T.d1[:, 2:SC * NV:SC], OP.subtract, [tEO[:2], tscan[0]]))
+        yield
+        trk[k] = vts(rank_of(k), d, 0.0, OP.is_lt, [tok[0]])
+        yield
+        tok.append(vtt(c, rank_of(k - 1), rank_of(k), OP.not_equal, [trk[k - 1], trk[k]]))
+        yield
+        tok.append(vts(T.d0[:, 1:SC * NV:SC], c, -2.0, OP.mult, [tok[1]], 1.0, OP.add))
+
+    def sort(k):
+        p, u = take("f", 28), take("u", 28)
+        e, w = T.wr[:, 32 * k:32 * k + 28:2], T.wr[:, 32 * k + 1:32 * k + 28:2]
+        t1 = vtt(T.lf[:, p:p + 14], e, w, OP.min, [("wr%d" % k, 16)])
+        t2 = vtt(T.lf[:, p + 14:p + 28], e, w, OP.max, [])
+        yield
+        ends[k] = (u, vts(T.lu[:, u:u + 28], T.lf[:, p:p + 28], 224.0, OP.add, [t1, t2]))
+
+    heads = []
+
+    def places(src, dep):
+        a, v, x, y, z, u = cols("i", 28), cols("i", 28), cols("f", 28), cols("f", 28), cols("f", 28), take("u", 28)
+        ta = vts(a, src, 1 / 28, OP.mult, [dep], -13.5 / 28, OP.add)
+        yield
+        tv = vts(v, src, 0.5, OP.mult, [], -0.25, OP.add)
+        yield
+        tz = vts(z, src, 2.0, OP.mult, [], 2.0, OP.add)
+        yield
+        ta = vts(x, a, -223.0 * SC, OP.mult, [ta])
+        yield
+        tv = vts(y, v, 16.0 * SC - 4, OP.mult, [tv])
+        yield
+        t = vtt(x, x, z, OP.add, [ta, tz])
+        yield
+        t = vtt(x, x, y, OP.add, [t, tv])
+        yield
+        heads.append((u, vcp(T.lu[:, u:u + 28], x, [t])))
+
+    spare = []
+
+    def fill(k=1):
+        for _ in range(k):
+            while spare:
+                if next(spare[0], "end") != "end":
+                    break
+                spare.pop(0)
+                break
 
     tu, hu = cols("u", 28), cols("u", 28)
     ttu = vcp(tu, T.tin[:], [TL])
-    tinv = [None]
-
-    def invert(u, deps):
-        k = len(tinv)
-        need("y", vcp(inv(k).indirect(u), T.iot[:], deps + [tIOT]))
-        Y.dma_start(T.inv[8::16, C * k:C * k + C - 1], T.inv[2::16, C * k + 1:C * k + C]).then_inc(T.sem["on%d" % (k - 1)], 16)
-        tinv.append(("on%d" % (k - 1), 16))
-
-    invert(tu, [ttu])
+    thu = vcp(hu, T.hin[:], [HL])
+    ti1 = invert(1, tu, [ttu])
+    hm = [T.lg[:, C * 6:C * 7], T.lg[:, C * 7:C * 8], lin(LT_)]
+    thl = [None, scp(hm[1], T.iot[:].indirect(tu), [ttu, tIOT]), None]
+    thl[0] = scp(hm[0], T.iot[:].indirect(hu), [thu])
+    ti0 = invert(0, hu, [thu])
     Y.dma_start(T.wq[:, 0:512].bitcast(dt.uint8), T.wc[:, :]).then_inc(T.sem.lww, 16)
     Y.dma_start(T.wp[:], T.ws[:, :]).then_inc(T.sem.lww, 16)
     Y.dma_start(T.vt[:], T.v[:, :]).then_inc(T.sem.lvv, 16)
-    UL, SELF = cols("u", 8), cols("u", 14)
-    tUL = vcp(UL, ul, [c12])
-    a = take("u", 12)
-    tSEL = vts(T.lu[:, a:a + 12], T.lf[:, d0:d0 + 12], BP, OP.add, [iD, c14], TW - 1, OP.min)
-    ONE, TWO, SELW = [T.lu[:, a + 4 * k:a + 4 * k + 4] for k in range(3)]
-    tSELF = vts(SELF, T.lf[:, e0:e0 + 14], P32, OP.add, [iE, c10])
-    even, odd, other, he, hx = cols("i", 28), cols("i", 28), cols("i", 28), cols("u", 28), cols("u", 28)
-    t0 = vts(even, T.hin[:], 510, OP.bitwise_and, [HL])
-    thu = vcp(hu, T.hin[:], [HL])
-    tq = quant(T.qu0, T.su0, 0, 128, T.ut[:], [LU])
-    t = vts(odd, even, 2, OP.mult, [t0], 1, OP.add)
-    pairs = [(he, vcp(he, even, [t0]))]
-    t = vtt(other, odd, T.hin[:], OP.subtract, [t])
-    tQU = [vcp(T.qu[:, 0:128].bitcast(dt.uint32), T.qu0[:, 0:128].bitcast(dt.uint32).indirect(UL), [tq, tUL])]
-    thx = vcp(hx, other, [t])
-    tHI = vcp(inv(0).indirect(hu), T.iot[:], [thu])
-
-    def hm(n):
-        return T.lg[:, C * (9 + n):C * (10 + n)]
-
-    thl = [None, scp(hm(1), T.iot[:].indirect(tu), [ttu, tIOT, tMASK], scale=M1), None]
-    thl[0] = scp(hm(0), T.iot[:].indirect(hu), [thu], scale=M1)
-    tQU.append(scp(T.su[:, 0:128], T.su0[:, 0:128].indirect(UL), [tq, tUL]))
+    sides(1, ti1)
+    tin = [side(T.bt[:, C + NV * i:C + NV * i + NV], 0, i, [ti0]) for i in range(2)]
+    tQU = quant(T.qu, T.su, 0, 128, T.ut[:], [LU])
     tX = [[LX], [], [], []]
-    sft, slf = [[], [], []], [[], [], []]
+    sft = [[], [], []]
 
     def score(n, h, deps):
-        c0, c1 = RUNS[h]
+        c0, c1 = STATE[h]
         a = C * n
         t = quant(T.qx, T.sx, a + c0, a + c1, T.xs[:, 1792 * n + 4 * c0:1792 * n + 4 * c1], deps)
         t = mm(4 * h, c1 - c0, T.qu[:, 0:128], T.su[:, 0:128], T.qx[:, a + c0:a + c1], T.sx[:, a + c0:a + c1], [tQU, t])
-        r = scp(T.sf[:, a + c0:a + c1], bank(4 * h, c1 - c0), [t], scale=UP)
+        r = scp(T.sf[:, a + c0:a + c1], bank(4 * h, c1 - c0), [t])
         free[4 * h].append(r)
         sft[n].append(r)
 
-    def selves(n, h):
-        c0, c1 = RUNS[h]
-        slf[n].append(scp(T.sl[:, 2 * C * n + c0:2 * C * n + c1], T.sf[:, C * n + c0:C * n + c1].indirect(SELF),
-                          [sft[n][h], tSELF]))
-
-    def ends(n):
-        return scp(lin(OUT_ + n), inv(n + 1).indirect(pairs[n][0]), [tinv[n + 1], pairs[n][1]], scale=TINY)
-
-    tOUT = ends(0)
-    tIN = scp(lin(IN_), inv(0).indirect(hx), [tHI, thx], scale=TINY)
-    score(0, 0, [LX])
-    score(0, 1, [LX])
-    selves(0, 0)
-    selves(0, 1)
-    IW, tIW, _ = word("f", T.lf[:, w0:w0 + 64], L16, OP.add, [iW, c6], TINY / 16, OP.mult, n=64)
-    SELB, tSELB, _ = word("u", T.lf[:, p0:p0 + 8], CP, OP.add, [iB, c13], 2 * C - 1, OP.min)
-
-    tXP = [[], [], []]
+    spare.append(places(T.hin[:], HL))
+    tXP = [{}, {}, {}]
 
     def plane(n, b, deps):
-        need("p", *deps)
         x0 = 1792 * n
-        tXP[n].append(done("p", g.affine_select(T.xp[:, x0 + C * b:x0 + C * b + C], T.xs[:, x0 + b:x0 + 1792:4],
-                                                [[0, C]], OP.is_ge, 0.0, 0, 0)))
+        tXP[n][b] = pcp(T.xp[:, x0 + C * b:x0 + C * b + C], T.xs[:, x0 + b:x0 + 1792:4], C, deps)
 
-    need("p", tONE)
-    tE = done("p", g.affine_select(T.et[:], T.ones[:], [[1, 516]], OP.is_equal, 0.0, -3, -4))
     for b in range(4):
         plane(0, b, [LX])
 
     def turn(k, deps):
         a, o = LIN * k, TW * k
-        return (vturn(T.tt[:, o:o + C], T.ln[:, a + 16:a + LIN], deps),
-                vturn(T.tt[:, o + C:o + TW], T.ln[:, a:a + 480], [pads]))
+        return [vturn(T.tt[:, o:o + C], T.ln[:, a + 16:a + LIN], deps),
+                vturn(T.tt[:, o + C:o + TW], T.ln[:, a:a + 480], [pads])]
 
     def own(k, table):
         return T.tt[:, TW * k:TW * k + TW].indirect(table)
 
-    def shared(k, r):
-        return T.tt[:, TW * k + r:TW * k + C:16]
+    first, second = sort(1), sort(0)
+    tb = tables(1)
+    ttab = next(tb)
+    for q in START:
+        if q == "r":
+            trk[0] = vtt(rank_of(0), T.bt[:, C:C + NV], T.bt[:, C + NV:2 * C], OP.is_gt, tin)
+        elif q in "xy":
+            score(0, "xy".index(q), [LX])
+        else:
+            next({"1": first, "0": second, "t": tb, "p": spare[0]}[q], None)
+    spare.insert(0, tb)
+    tQE, tQV = [], []
 
-    def whole(out, in_, deps):
-        return vts(out, in_, 1.0 / TINY, OP.mult, deps, 224.0, OP.add)
+    def once():
+        for b in range(4):
+            tQE.append(quant(T.qe, T.se, 128 * b, 128 * b + 128, T.et[:, 3 - b:515 - b], [tE]))
+            yield
+        tQV.append(quant(T.qv, T.sv, 0, 128, T.vt[:], [LV]))
 
-    def siblings(n, dep):
-        a, sib = take("f", 128), cols("u", 28)
-        t1, t2 = turn(IN_ + n, [dep])
-        t1 = whole(sib, shared(IN_ + n, 0), [t1])
-        return a, sib, t1, vtt(T.lf[:, a:a + 64], own(IN_ + n, ONE), IW, OP.subtract, [t2, tIW, tSEL])
-
-    tQE, tQV, last = [], [], [None]
-
-    def unit(b):
-        tQE.append(quant(T.qe, T.se, 128 * b, 128 * b + 128, T.et[:, 3 - b:515 - b], [tE]))
-
-    def evens(src, dep):
-        w, e, u = cols("i", 28), cols("i", 28), cols("u", 28)
-
-        def step(k):
-            if k == 0:
-                last[0] = vcp(w, src, [dep])
-            elif k == 1:
-                last[0] = vts(e, w, 510, OP.bitwise_and, [last[0]])
-            else:
-                pairs.append((u, vcp(u, e, [last[0]])))
-        return [lambda k=k: step(k) for k in range(3)]
-
-    spare = evens(tu, ttu) + [lambda b=b: unit(b) for b in range(4)]
-
-    def fill():
-        if spare:
-            spare.pop(0)()
-
+    spare += [once(), places(T.tin[:], TL)]
     nloc = [0]
 
     def send(dst, out, in_, sem):
@@ -311,53 +330,46 @@ def rank_program(g, core, T, topo):
         g.remote_dma(out, in_, T.sem[sem], T.sem.loc, pid, rid, topo.mask(core, dst))
         nloc[0] += len(topo.engines(core, dst))
 
-    tails = tu
     for n in range(3):
         mate = T.cores[rank ^ STEP[n]]
         eng = len(topo.engines(core, mate))
-        x0, a0, b0 = 1792 * n, C * n, 2 * C * n
+        x0, a0, s0 = 1792 * n, C * n, SC * NV * n
         sf = T.sf[:, a0:a0 + C]
-        out0, out1, first = cols("u", 28), cols("u", 28), cols("f", 64)
-        t1, t2 = turn(OUT_ + n, [tOUT])
-        to0 = whole(out0, shared(OUT_ + n, 0), [t1])
-        to1 = whole(out1, shared(OUT_ + n, 8), [t1])
-        tf = vcp(first, own(OUT_ + n, ONE), [t2, tSEL])
-        if n == 0:
-            sibs = siblings(0, tIN)
-        else:
+        tb = []
+        for i in (0, 1) if n else (1, 0):
+            u, t = ends[n + i]
+            for v0, v1 in HALVES:
+                k = a0 + NV * i
+                r = scp(T.sl[:, k + v0:k + v1], sf.indirect(T.lu[:, u + v0 // 16:u + v1 // 16]), [t, sft[n]])
+                if len(ttab) < 3:
+                    fill()
+                tb.append(vtt(T.bt[:, k + v0:k + v1], sf.indirect(T.lu[:, u + 14 + v0 // 16:u + 14 + v1 // 16]),
+                              T.sl[:, k + v0:k + v1], OP.is_gt, [r]))
+        tEO.append(scp(T.d1[:, 4:SC * NV:SC], T.d1[:, 2:SC * NV:SC], [tEO]))
+        t = [vtt(T.d1[:, SC * v0:SC * v1:SC], T.bt[:, a0 + v0:a0 + v1], T.bt[:, a0 + NV + v0:a0 + NV + v1], OP.not_equal,
+                 [tb[2 + k], tscan[0]]) for k, (v0, v1) in enumerate(HALVES)]
+        mt = T.mt[:, s0:s0 + SC * NV]
+        for k, (v0, v1) in enumerate(HALVES):
+            need("v", t[k], ttab, tEO, tC)
+            tscan[0] = done("v", V.tensor_tensor_scan(T.mt[:, s0 + SC * v0:s0 + SC * v1], T.d0[:, SC * v0:SC * v1],
+                                                      T.d1[:, SC * v0:SC * v1], 0.0, OP.mult, OP.add))
+        fill()
+        while len(heads) <= n:
             fill()
-        a, sib, tsib, tth = sibs
-        th, step = T.lf[:, a:a + 128], T.lf[:, a + 64:a + 128]
-        td = vtt(step, own(OUT_ + n, TWO), first, OP.subtract, [tf])
-        gout = scp(T.sl[:, b0 + C:b0 + 2 * C], sf.indirect(out0), [to0, sft[n]])
-        if n < 2:
-            r = C * (n + 1)
-            t = [scp(T.sw[:, a0:a0 + C:2], T.inv[:, r + 1:r + C:2], [tinv[n + 1]]),
-                 scp(T.sw[:, a0 + 1:a0 + C:2], T.inv[:, r:r + C:2], [])]
-            tIN = scp(lin(IN_ + n + 1), T.sw[:, a0:a0 + C].indirect(tails), [t], scale=TINY)
-        ta = vtt(T.ab[:, b0:b0 + C], sf.indirect(sib), T.sl[:, b0:b0 + C], OP.subtract, [sft[n], slf[n], tsib])
-        tb = vtt(T.ab[:, b0 + C:b0 + 2 * C], sf.indirect(out1), T.sl[:, b0 + C:b0 + 2 * C], OP.subtract, [gout, to1])
-        fill()
-        t = vturn(T.abt[:, b0:b0 + 2 * C], T.ab[:, b0:b0 + 2 * C], [ta, tb])
-        fill()
-        a = 192 * n
-        t = vtt(T.bt[:, a:a + 128], T.abt[:, b0:b0 + 2 * C].indirect(SELB), th, OP.is_gt, [t, td, tth, tSELB])
-        fill()
-        e, w, m = T.bt[:, a + 128:a + 192], cols("f", 64), cols("f", 64)
-        t = vtt(e, T.bt[:, a:a + 64], T.bt[:, a + 64:a + 128], OP.not_equal, [t])
-        fill()
-        t = vtt(w, e, step, OP.mult, [t])
-        fill()
-        t = vtt(m, w, first, OP.add, [t])
-        fill()
+        hp, thp = heads[n]
+        tml = [vcp(lin(M_ + n, 0, NV), mt.indirect(T.lu[:, hp:hp + 14]), [tscan[0], thp]),
+               scp(lin(M_ + n, NV, C), mt.indirect(T.lu[:, hp + 14:hp + 28]), [tscan[0], thp])]
         u = 64 * n
-        tm = whole(T.mu[:, u:u + 64], m, [t])
+        t = turn(M_ + n, tml)
+        fill()
+        tm = vts(T.mu[:, u:u + 64], own(M_ + n, SELM), 224.0, OP.add, [t, tSEL])
         fill()
         m0, m1 = T.mu[:, u:u + 28], T.mu[:, u + 32:u + 60]
         need("p", tm)
         send(mate, T.ma[:, u:u + 64], T.mu[:, u:u + 64], "ml%d" % n)
-        G = [T.lg[:, C * (3 * n + k):C * (3 * n + k) + C] for k in range(3)]
-        tg0 = scp(G[0], T.iot[:].indirect(m1), [tm], scale=M0)
+        G = [T.lg[:, C * (2 * n + k):C * (2 * n + k) + C] for k in range(2)]
+        need("y", scp(G[0], lin(M_ + n).indirect(m0), [tm]), thl[n])
+        Y.dma_start(G[0][2::16, :], hm[n][2::16, :]).then_inc(T.sem["on%d" % n], 16)
         tz = []
         for b in range(4):
             yp = T.yf[:, x0 + C * b:x0 + C * b + C]
@@ -365,88 +377,112 @@ def rank_program(g, core, T, topo):
                      [tm, tXP[n][b], tX[n]])
             if b < 3:
                 tz.append(scp(T.zt[:, x0 + b:x0 + 1792:4], yp.indirect(m0), [ty], scale=0.5))
-        tl3 = [vts(T.zt[:, x0 + 3:x0 + 896:4], yp.indirect(T.mu[:, u:u + 14]), 0.5, OP.mult, [ty]),
-               scp(T.zt[:, x0 + 899:x0 + 1792:4], yp.indirect(T.mu[:, u + 14:u + 28]), [ty], scale=0.5)]
-        tq = [quant(T.qz, T.sz, a0 + c0, a0 + c1, T.zt[:, x0 + 4 * c0:x0 + 4 * c1], tz + [tl3[h]])
-              for h, (c0, c1) in enumerate(RUNS)]
-        tg1 = vtt(G[1], G[0].indirect(m0), hm(n), OP.add, [tg0, thl[n]])
-        for h, (c0, c1) in enumerate(RUNS):
-            tr = [mm(b + 4 * h, c1 - c0, T.wq[:, 128 * b:128 * b + 128], T.wp[:, 128 * b:128 * b + 128],
-                     T.qz[:, a0 + c0:a0 + c1], T.sz[:, a0 + c0:a0 + c1], [LW, tq[h]]) for b in range(4)]
-            tH = []
-            for b in range(4):
-                o = T.ht[:, x0 + 4 * c0 + b:x0 + 4 * c1:4]
-                if b in ONV[h]:
-                    r = vts(o, bank(b + 4 * h, c1 - c0), 0.03125, OP.mult, [tr[b]])
+        fill()
+        tl3 = [vts(T.zt[:, x0 + 3:x0 + 4 * ZV:4], yp.indirect(T.mu[:, u:u + ZV // 16]), 0.5, OP.mult, [ty]),
+               scp(T.zt[:, x0 + 4 * ZV + 3:x0 + 1792:4], yp.indirect(T.mu[:, u + ZV // 16:u + 28]), [ty], scale=0.5)]
+        fill()
+        tq, tr, tH = {}, {}, {}
+        for step in ORDER:
+            k = step[1]
+            if step[0] == "z":
+                c0, c1 = LAYER[k]
+                tq[k] = quant(T.qz, T.sz, a0 + c0, a0 + c1, T.zt[:, x0 + 4 * c0:x0 + 4 * c1], tz + tl3[:1 + (c1 > ZV)])
+            elif step[0] == "m":
+                c0, c1 = LAYER[k]
+                for b in range(4):
+                    tr[k, b] = mm(b + 4 * (k % 2), c1 - c0, T.wq[:, 128 * b:128 * b + 128], T.wp[:, 128 * b:128 * b + 128],
+                                  T.qz[:, a0 + c0:a0 + c1], T.sz[:, a0 + c0:a0 + c1], [LW, tq[k]])
+            elif step[0] == "c":
+                (c0, c1), b = LAYER[k], step[2]
+                o, j = T.ht[:, x0 + 4 * c0 + b:x0 + 4 * c1:4], b + 4 * (k % 2)
+                if step[3] == "v":
+                    tH[k, b] = vts(o, bank(j, c1 - c0), 0.03125, OP.mult, [tr[k, b]])
                 else:
-                    r = scp(o, bank(b + 4 * h, c1 - c0), [tr[b]], scale=0.03125)
-                free[b + 4 * h].append(r)
-                tH.append(r)
-            need("p", quant(T.qh, T.sh, a0 + c0, a0 + c1, T.ht[:, x0 + 4 * c0:x0 + 4 * c1], tH))
-            send(mate, T.qa[:, a0 + c0:a0 + c1].bitcast(dt.uint8), T.qh[:, a0 + c0:a0 + c1].bitcast(dt.uint8), "a%d%d" % (h, n))
-            send(mate, T.sa[:, a0 + c0:a0 + c1], T.sh[:, a0 + c0:a0 + c1], "a%d%d" % (h, n))
-        need("s", ("ml%d" % n, eng))
-        t = scp(G[2], G[1].indirect(T.ma[:, u + 32:u + 60]), [tg1])
-        tlt = scp(lin(LT_ + n), G[2].indirect(T.ma[:, u:u + 28]), [t])
+                    tH[k, b] = scp(o, bank(j, c1 - c0), [tr[k, b]], scale=0.03125)
+                free[j].append(tH[k, b])
+            elif step[0] == "h":
+                c0, c1 = SENT[k]
+                fill()
+                need("p", quant(T.qh, T.sh, a0 + c0, a0 + c1, T.ht[:, x0 + 4 * c0:x0 + 4 * c1],
+                                [t for (j, b), t in tH.items() if LAYER[j][0] < c1]))
+                send(mate, T.qa[:, a0 + c0:a0 + c1].bitcast(dt.uint8), T.qh[:, a0 + c0:a0 + c1].bitcast(dt.uint8), "a%d%d" % (k, n))
+                send(mate, T.sa[:, a0 + c0:a0 + c1], T.sh[:, a0 + c0:a0 + c1], "a%d%d" % (k, n))
+            elif step[0] == "g":
+                tg = scp(G[1], G[0].indirect(T.ma[:, u + 32:u + 60]), [("ml%d" % n, eng), ("on%d" % n, 16)])
+            elif step[0] == "l":
+                tlt = (scp, vcp)[k == "v"](lin(LT_ + n), G[1].indirect(T.ma[:, u:u + 28]), [tg])
+            else:
+                fill(k)
         if n == 0:
-            thl[2] = scp(hm(2), lin(LT_), [tlt], scale=M1)
-        if n < 2:
-            sibs = siblings(n + 1, tIN)
-        else:
+            thl[2] = tlt
+        if n == 2:
             need("s", tlt)
             need("y", done("s", S.activation(T.tpf[:], lin(LT_ + 2), AF.Identity, bias=224.0)))
-            Y.dma_start(T.tp[:, :], T.tpf[1::16, 0:C]).then_inc(T.sem.outs, 16)
-            tQV = quant(T.qv, T.sv, 0, 128, T.vt[:], [LV])
+            Y.dma_start(T.tp[:, :], T.tpf[2::16, 0:C]).then_inc(T.sem.outs, 16)
         u0 = take("u", 64)
-        tl = vts(T.lu[:, u0:u0 + 64], own(LT_ + n, SELW), 224.0, OP.add, list(turn(LT_ + n, [tlt])))
+        fill(3)
+        t = turn(LT_ + n, [tlt])
+        fill()
+        tl = vts(T.lu[:, u0:u0 + 64], own(LT_ + n, SELL), 224.0, OP.add, t)
+        fill()
         if n < 2:
             tails = T.lu[:, u0 + 32:u0 + 60]
-            invert(tails, [tl])
+            ti = invert(n + 2, tails, [tl])
         if n == 0:
-            spare += evens(tails, tl)
+            spare.append(places(tails, tl))
+        while len(tQE) < 4:
+            fill()
         tdp = [[], [], [], []]
-        for h, (c0, c1) in enumerate(RUNS):
+        for h, (c0, c1) in enumerate(SENT):
             need("t", ("a%d%d" % (h, n), 2 * eng))
-            for b in range(4):
-                t = mm(b + 4 * h, c1 - c0, T.qe[:, 128 * b:128 * b + 128], T.se[:, 128 * b:128 * b + 128],
+            for b in UNPACK:
+                j = b + 4 * (h % 2)
+                t = mm(j, c1 - c0, T.qe[:, 128 * b:128 * b + 128], T.se[:, 128 * b:128 * b + 128],
                        T.qa[:, a0 + c0:a0 + c1], T.sa[:, a0 + c0:a0 + c1], [tQE])
-                r = (scp, vcp)[(n, h, b) == (2, 1, 0)](T.dp[:, x0 + C * b + c0:x0 + C * b + c1], bank(b + 4 * h, c1 - c0), [t])
-                free[b + 4 * h].append(r)
+                r = (scp, vcp)[(h, b) in DONV[n]](T.dp[:, x0 + C * b + c0:x0 + C * b + c1], bank(j, c1 - c0), [t])
+                free[j].append(r)
                 tdp[b].append(r)
 
         def far(b, c0, c1):
             return T.dp[:, x0 + C * b:x0 + C * b + C].indirect(T.lu[:, u0 + c0 // 16:u0 + c1 // 16])
 
-        laid = {(b, c0): scp(T.dg[:, C * b + c0:C * b + c1], far(b, c0, c1), [tl, tdp[b], tX[n]])
-                for c0, c1 in RUNS for b in (2, 3)}
+        runs, lay, order = (STATE, LAID, MEET) if n < 2 else (LAST, LAID2, MEET2)
+        laid = [(b, c0, c1, scp(T.dg[:, C * b + c0:C * b + c1], far(b, c0, c1), [tl, tdp[b], tX[n]])) for b, c0, c1 in lay]
         if n < 2:
-            tOUT = ends(n + 1)
+            sides(n + 2, ti)
         x1, a1 = x0 + 1792, a0 + C
-
-        def meet(b, c0, c1):
-            in0, deps = (T.dg[:, C * b + c0:C * b + c1], [laid[b, c0]]) if b > 1 else (far(b, c0, c1), [tl, tdp[b], tX[n]])
-            t = vtt(T.xs[:, x1 + 4 * c0 + b:x1 + 4 * c1:4], in0, T.xs[:, x0 + 4 * c0 + b:x0 + 4 * c1:4], OP.add, deps)
-            tX[n + 1].append(t)
-            if n < 2 and c1 == C:
-                plane(n + 1, b, tX[n + 1])
-
-        at = 2 if n < 2 else 1
-        for b in range(at):
-            meet(b, 0, C)
-        for h, (c0, c1) in enumerate(RUNS):
-            for b in range(at, 4):
-                meet(b, c0, c1)
-            if n < 2:
-                score(n + 1, h, tX[n + 1])
-                selves(n + 1, h)
+        made = [[] for _ in runs]
+        for b, c0, c1 in order:
+            if b is not None:
+                deps = [t for k, d0, d1, t in laid if k == b and d0 < c1 and c0 < d1]
+                in0 = T.dg[:, C * b + c0:C * b + c1] if deps else far(b, c0, c1)
+                t = vtt(T.xs[:, x1 + 4 * c0 + b:x1 + 4 * c1:4], in0, T.xs[:, x0 + 4 * c0 + b:x0 + 4 * c1:4], OP.add,
+                        deps or [tl, tdp[b], tX[n]])
+                tX[n + 1].append(t)
+                for k, (d0, d1) in enumerate(runs):
+                    if d0 < c1 and c0 < d1:
+                        made[k].append(t)
+                if n < 2 and c1 == C:
+                    plane(n + 1, b, tX[n + 1])
                 continue
-            t = quant(T.qx, T.sx, a1 + c0, a1 + c1, T.xs[:, x1 + 4 * c0:x1 + 4 * c1], tX[3])
+            h = runs.index((c0, c1))
+            if n < 2:
+                score(n + 1, h, made[h])
+                continue
+            t = quant(T.qx, T.sx, a1 + c0, a1 + c1, T.xs[:, x1 + 4 * c0:x1 + 4 * c1], made[h])
             need("y", t)
             Y.dma_start(T.oc[:, 4 * c0:4 * c1], T.qx[:, a1 + c0:a1 + c1].bitcast(dt.uint8)).then_inc(T.sem.outs, 16)
-            for k in range(4 * h):
+            for k in range(4 * (c1 == C)):
                 need("ys"[k % 2], t)
                 Q["ys"[k % 2]].dma_start(T.osc[4 * k:4 * k + 4, 0:C], T.sx[32 * k:32 * k + 4, a1:a1 + C]).then_inc(T.sem.outs, 16)
             t = mm(h, c1 - c0, T.qv[:, 0:128], T.sv[:, 0:128], T.qx[:, a1 + c0:a1 + c1], T.sx[:, a1 + c0:a1 + c1], [tQV, t])
-            need("s", (scp, vcp)[h](T.yo[:, c0:c1], bank(h, c1 - c0), [t]))
+            need("s", (scp, vcp)[c1 == C](T.yo[:, c0:c1], bank(h, c1 - c0), [t]))
             S.dma_start(T.y[:, c0:c1], T.yo[:, c0:c1]).then_inc(T.sem.outs, 16)
-    need("y", ("outs", 16 * 9), ("loc", nloc[0]), LW, LV, [("c" + q, cnt[q]) for q in cnt])
+        if n < 2:
+            first, tb = sort(n + 2), tables(n + 2)
+            ttab = next(tb)
+            for gen in (first, tb, first, tb):
+                next(gen, None)
+            fill()
+            spare.insert(0, tb)
+    need("y", ("outs", 16 * (5 + 2 * len(LAST))), ("loc", nloc[0]), LW, LV, [("c" + q, cnt[q]) for q in cnt])

from concourse.mybir import dt, AluOpType, ActivationFunctionType

C, NV = 448, 224
STEP = [1, 2, 3]
LAYER = [(0, 128), (128, 288), (288, C)]
STATE = [(0, 320), (320, C)]
SENT = LAYER
ZV = 192
ORDER = ([("z", 0), ("m", 0), ("z", 1), ("m", 1), ("z", 2), ("g", 0), ("e", 2)]
         + [("c", 0, b, "vvvs"[b]) for b in range(4)] + [("m", 2), ("h", 0)] + [("c", 1, b, "svss"[b]) for b in range(4)]
         + [("h", 1)] + [("c", 2, b, "svsv"[b]) for b in range(4)] + [("h", 2), ("l", "s")])
UNPACK = (0, 1, 2, 3)
DONV = [[], [], [(0, 1), (0, 3), (1, 1), (1, 3), (2, 0), (2, 2)]]
LAID = [(2, 0, 320), (3, 0, 320), (1, 320, C), (2, 320, C), (3, 320, C)]
MEET = [(0, 0, C), (1, 0, 320), (2, 0, 320), (3, 0, 320), (1, 320, C), (None, 0, 320), (2, 320, C), (3, 320, C),
        (None, 320, C)]
LAST = [(0, 192), (192, 320), (320, C)]
LAID2 = [(3, 0, 192), (2, 192, 320), (3, 192, 320), (1, 320, C), (2, 320, C), (3, 320, C)]
MEET2 = ([(b, 0, 192) for b in range(4)] + [(0, 192, 320), (None, 0, 192)] + [(b, 192, 320) for b in (1, 2, 3)]
         + [(0, 320, C), (None, 192, 320)] + [(b, 320, C) for b in (1, 2, 3)] + [(None, 320, C)])
START = "xy1p1ptpptpppr0p0"
PRE = 4
HALVES = [(0, 96), (96, NV)]
LIN = 464
TW = 928
SC = 5
M_, LT_ = 0, 3


def _sb(n, d):
    return ("sbuf", [128, n], d)


def _bf(n):
    return _sb(n, "bfloat16")


def _codes(n):
    return _sb(n, "float8_e4m3fn_x4")


def _plane(n):
    return _sb(n, "uint8")


SCRATCH = {
    "hin": _sb(28, "int32"), "tin": _sb(28, "int32"),
    "ut": _bf(512), "vt": _bf(512), "ones": _bf(516), "et": _bf(516),
    "xs": _bf(4 * 1792), "xp": _bf(3 * 1792), "yf": _sb(3 * 1792, "float32"),
    "zt": _bf(3 * 1792), "ht": _bf(3 * 1792), "dp": _bf(3 * 1792), "dg": _bf(1792),
    "qu": _codes(128), "su": _plane(128), "qv": _codes(128), "sv": _plane(128),
    "wq": _codes(512), "wp": _plane(512), "qe": _codes(512), "se": _plane(512),
    "qx": _codes(4 * C), "sx": _plane(4 * C), "qz": _codes(3 * C), "sz": _plane(3 * C),
    "qh": _codes(3 * C), "sh": _plane(3 * C), "qa": _codes(3 * C), "sa": _plane(3 * C),
    "sf": _sb(3 * C, "float32"), "sl": _sb(3 * C, "float32"), "bt": _bf(3 * C), "rk": _bf(4 * NV),
    "d0": _sb(SC * NV, "float16"), "d1": _bf(SC * NV), "mt": _bf(3 * SC * NV),
    "iot": _bf(C), "ln": _bf(6 * LIN + 16), "tt": _bf(6 * TW), "lg": _bf(8 * C), "inv": _bf(4 * C), "wr": _bf(128),
    "li": _sb(512, "int32"), "lu": _sb(1024, "uint16"), "lf": _sb(1024, "float32"),
    "mu": _sb(192, "uint16"), "ma": _sb(192, "uint16"),
    "tpf": _sb(C, "float32"), "yo": _sb(C, "float32"),
    "ps": ("psum", [128, 4096], "float32"),
}
SEMAPHORES = (["cv", "cs", "ct", "cp", "loc", "ltl", "lhl", "lxx", "luu", "lww", "lvv", "outs"]
              + ["%s%d" % (k, n) for k in ("ml", "on", "a0", "a1", "a2") for n in range(3)] + ["wr%d" % k for k in range(4)])


def rank_program(g, core, T, topo):
    rank = T.rank_of(core)
    if rank is None:
        return
    OP, AF = AluOpType, ActivationFunctionType
    V, S, PE, Y = g.vector, g.scalar, g.tensor, g.sync
    Q = {"v": V, "s": S, "t": PE, "p": g, "y": Y}
    cnt = {"v": 0, "s": 0, "t": 0, "p": 0}
    seen = {q: {} for q in Q}
    ncl = {"i": 0, "u": 0, "f": 0}
    tabs = {"i": T.li, "u": T.lu, "f": T.lf}

    def need(q, *toks):
        best = {}
        todo = list(toks)
        while todo:
            a = todo.pop()
            if isinstance(a, list):
                todo += a
            elif a is not None:
                best[a[0]] = max(best.get(a[0], 0), a[1])
        for k, v in best.items():
            if seen[q].get(k, 0) < v:
                Q[q].wait_ge(T.sem[k], v)
                seen[q][k] = v

    def done(q, inst):
        cnt[q] += 1
        inst.then_inc(T.sem["c" + q], 1)
        return ("c" + q, cnt[q])

    def take(k, n):
        a = ncl[k]
        ncl[k] = a + n
        return a

    def cols(k, n):
        a = take(k, n)
        return tabs[k][:, a:a + n]

    def vts(out, in0, s1, op0, deps, s2=None, op1=None):
        need("v", *deps)
        if op1 is None:
            return done("v", V.tensor_scalar(out, in0, s1, None, op0))
        return done("v", V.tensor_scalar(out, in0, s1, s2, op0, op1))

    def vtt(out, in0, in1, op, deps):
        need("v", *deps)
        return done("v", V.tensor_tensor(out, in0, in1, op))

    def vcp(out, in_, deps):
        need("v", *deps)
        return done("v", V.tensor_copy(out, in_))

    def vturn(out, in_, deps):
        need("v", *deps)
        return done("v", V.transpose(out, in_))

    def scp(out, in_, deps, scale=None):
        need("s", *deps)
        if scale is None:
            return done("s", S.activation(out, in_, AF.Copy))
        return done("s", S.activation(out, in_, AF.Identity, scale=scale))

    def pcp(out, in_, n, deps):
        need("p", *deps)
        return done("p", g.affine_select(out, in_, [[0, n]], OP.is_ge, 0.0, 0, 0))

    def quant(qb, sb, a, b, tile, deps):
        need("v", *deps)
        return done("v", V.quantize_mx(qb[:, a:b], sb[:, a:b], tile))

    def count(k, pattern, base, step):
        n = 1
        for s, c in pattern:
            n *= c
        a = take(k, n)
        t = done("p", g.iota(tabs[k][:, a:a + n], pattern, base, step, allow_small_or_imprecise_dtypes=(k == "f")))
        return tabs[k][:, a:a + n], t

    free = [[] for _ in range(8)]

    def mm(k, n, l, ls, r, rs, deps):
        need("t", free[k], *deps)
        free[k] = []
        return done("t", PE.matmul_mx(T.ps[:, 512 * k:512 * k + n], l, ls, r, rs, True, True))

    def bank(k, n):
        return T.ps[:, 512 * k:512 * k + n]

    def lin(k, a=0, b=C):
        return T.ln[:, LIN * k + 16 + a:LIN * k + 16 + b]

    S.dma_start(T.tin[:], T.tl[:, :]).then_inc(T.sem.ltl, 16)
    Y.dma_start(T.hin[:], T.hl[:, :]).then_inc(T.sem.lhl, 16)
    S.dma_start(T.ut[:], T.u[:, :]).then_inc(T.sem.luu, 16)
    Y.dma_start(T.xs[:, 0:1792], T.x[:, :]).then_inc(T.sem.lxx, 16)
    TL, HL, LX, LU, LW, LV = ("ltl", 16), ("lhl", 16), ("lxx", 16), ("luu", 16), ("lww", 32), ("lvv", 16)

    p17, iP = count("i", [[0, 2]], 0, 17)
    lanes, iD = count("f", [[1, 3], [256, 2]], 0, 0)
    pairs, iS = count("f", [[1, 2], [2, 14]], 0, 0)
    tIOT = done("p", g.iota(T.iot[:], [[1, C]], -224, 0, allow_small_or_imprecise_dtypes=True))
    tONE = done("v", V.memset(T.ones[:], 1.0))
    need("p", tONE)
    tE = done("p", g.affine_select(T.et[:], T.ones[:], [[1, 516]], OP.is_equal, 0.0, -3, -4))

    def word(k, in0, s1, op0, deps, s2=None, op1=None):
        a = take(k, 2)
        return tabs[k][:, a:a + 2], vts(tabs[k][:, a:a + 2], in0, s1, op0, deps, s2, op1), tabs[k][:, a:a + 1]

    def fixed(k, w):
        return vts(T.d0[:, k:SC * NV:SC], T.ones[:, 0:NV], w, OP.mult, [tONE])

    lane, c1, _ = word("i", p17, 15, OP.bitwise_and, [iP])
    flip, c2, _ = word("i", p17, 4, OP.arith_shift_right, [iP], 1, OP.bitwise_and)
    tC = [fixed(0, 0.0)]
    _, c3, L16 = word("f", lane, 16, OP.mult, [c1])
    tC.append(fixed(3, -1.0))
    _, c4, BA = word("f", flip, C + 16, OP.mult, [c2, c3], L16, OP.add)
    _, c5, L28 = word("f", lane, 28, OP.mult, [])
    tC.append(fixed(4, 1.0))
    pads = [scp(T.ln[:, LIN * k:LIN * k + 16], T.ones[:, 0:16], [tONE]) for k in range(7)]
    a, EO = take("u", 6), take("u", 28)
    tSEL = [vts(T.lu[:, a:a + 6], lanes, BA, OP.add, [iD, c4], TW - 1, OP.min),
            vts(T.lu[:, EO:EO + 28], pairs, L28, OP.add, [iS, c5])]
    SELM, SELL = T.lu[:, a:a + 4], T.lu[:, a + 2:a + 6]

    tEO, ends, trk, tscan = [], {}, {}, [None]

    def invert(k, u, deps):
        t = vcp(T.inv[:, C * k:C * k + C].indirect(u), T.iot[:], deps + [tIOT])
        need("y", t)
        Y.dma_start(T.wr[:, 32 * k:32 * k + 28], T.inv[0::16, C * k:C * k + C]).then_inc(T.sem["wr%d" % k], 16)
        return t

    def side(out, k, i, deps):
        return scp(out, T.inv[:, C * k:C * k + C].indirect(T.lu[:, EO + 14 * i:EO + 14 * i + 14]), deps + [tSEL])

    def sides(k, ti):
        tEO[:] = [side(T.d1[:, 2 + j:SC * NV:SC], k, j, [ti, tscan[0]]) for j in range(2)]

    def rank_of(k):
        return T.rk[:, NV * k:NV * k + NV]

    def tables(k):
        d, c = T.d0[:, 2:SC * NV:SC], T.d1[:, 1:SC * NV:SC]
        tok = []
        yield tok
        tok.append(vtt(d, T.d1[:, 3:SC * NV:SC], T.d1[:, 2:SC * NV:SC], OP.subtract, [tEO[:2], tscan[0]]))
        yield
        trk[k] = vts(rank_of(k), d, 0.0, OP.is_lt, [tok[0]])
        yield
        tok.append(vtt(c, rank_of(k - 1), rank_of(k), OP.not_equal, [trk[k - 1], trk[k]]))
        yield
        tok.append(vts(T.d0[:, 1:SC * NV:SC], c, -2.0, OP.mult, [tok[1]], 1.0, OP.add))

    def sort(k):
        p, u = take("f", 28), take("u", 28)
        e, w = T.wr[:, 32 * k:32 * k + 28:2], T.wr[:, 32 * k + 1:32 * k + 28:2]
        t1 = vtt(T.lf[:, p:p + 14], e, w, OP.min, [("wr%d" % k, 16)])
        t2 = vtt(T.lf[:, p + 14:p + 28], e, w, OP.max, [])
        yield
        ends[k] = (u, vts(T.lu[:, u:u + 28], T.lf[:, p:p + 28], 224.0, OP.add, [t1, t2]))

    heads = []

    def places(src, dep):
        a, v, x, y, z, u = cols("i", 28), cols("i", 28), cols("f", 28), cols("f", 28), cols("f", 28), take("u", 28)
        ta = vts(a, src, 1 / 28, OP.mult, [dep], -13.5 / 28, OP.add)
        yield
        tv = vts(v, src, 0.5, OP.mult, [], -0.25, OP.add)
        yield
        tz = vts(z, src, 2.0, OP.mult, [], 2.0, OP.add)
        yield
        ta = vts(x, a, -223.0 * SC, OP.mult, [ta])
        yield
        tv = vts(y, v, 16.0 * SC - 4, OP.mult, [tv])
        yield
        t = vtt(x, x, z, OP.add, [ta, tz])
        yield
        t = vtt(x, x, y, OP.add, [t, tv])
        yield
        heads.append((u, vcp(T.lu[:, u:u + 28], x, [t])))

    spare = []

    def fill(k=1):
        for _ in range(k):
            while spare:
                if next(spare[0], "end") != "end":
                    break
                spare.pop(0)
                break

    tu, hu = cols("u", 28), cols("u", 28)
    ttu = vcp(tu, T.tin[:], [TL])
    thu = vcp(hu, T.hin[:], [HL])
    ti1 = invert(1, tu, [ttu])
    hm = [T.lg[:, C * 6:C * 7], T.lg[:, C * 7:C * 8], lin(LT_)]
    thl = [None, scp(hm[1], T.iot[:].indirect(tu), [ttu, tIOT]), None]
    thl[0] = scp(hm[0], T.iot[:].indirect(hu), [thu])
    ti0 = invert(0, hu, [thu])
    Y.dma_start(T.wq[:, 0:512].bitcast(dt.uint8), T.wc[:, :]).then_inc(T.sem.lww, 16)
    Y.dma_start(T.wp[:], T.ws[:, :]).then_inc(T.sem.lww, 16)
    Y.dma_start(T.vt[:], T.v[:, :]).then_inc(T.sem.lvv, 16)
    sides(1, ti1)
    tin = [side(T.bt[:, C + NV * i:C + NV * i + NV], 0, i, [ti0]) for i in range(2)]
    tQU = quant(T.qu, T.su, 0, 128, T.ut[:], [LU])
    tX = [[LX], [], [], []]
    sft = [[], [], []]

    def score(n, h, deps):
        c0, c1 = STATE[h]
        a = C * n
        t = quant(T.qx, T.sx, a + c0, a + c1, T.xs[:, 1792 * n + 4 * c0:1792 * n + 4 * c1], deps)
        t = mm(4 * h, c1 - c0, T.qu[:, 0:128], T.su[:, 0:128], T.qx[:, a + c0:a + c1], T.sx[:, a + c0:a + c1], [tQU, t])
        r = scp(T.sf[:, a + c0:a + c1], bank(4 * h, c1 - c0), [t])
        free[4 * h].append(r)
        sft[n].append(r)

    spare.append(places(T.hin[:], HL))
    tXP = [{}, {}, {}]

    def plane(n, b, deps):
        x0 = 1792 * n
        tXP[n][b] = pcp(T.xp[:, x0 + C * b:x0 + C * b + C], T.xs[:, x0 + b:x0 + 1792:4], C, deps)

    for b in range(4):
        plane(0, b, [LX])

    def turn(k, deps):
        a, o = LIN * k, TW * k
        return [vturn(T.tt[:, o:o + C], T.ln[:, a + 16:a + LIN], deps),
                vturn(T.tt[:, o + C:o + TW], T.ln[:, a:a + 480], [pads])]

    def own(k, table):
        return T.tt[:, TW * k:TW * k + TW].indirect(table)

    first, second = sort(1), sort(0)
    tb = tables(1)
    ttab = next(tb)
    for q in START:
        if q == "r":
            trk[0] = vtt(rank_of(0), T.bt[:, C:C + NV], T.bt[:, C + NV:2 * C], OP.is_gt, tin)
        elif q in "xy":
            score(0, "xy".index(q), [LX])
        else:
            next({"1": first, "0": second, "t": tb, "p": spare[0]}[q], None)
    spare.insert(0, tb)
    tQE, tQV = [], []

    def once():
        for b in range(4):
            tQE.append(quant(T.qe, T.se, 128 * b, 128 * b + 128, T.et[:, 3 - b:515 - b], [tE]))
            yield
        tQV.append(quant(T.qv, T.sv, 0, 128, T.vt[:], [LV]))

    spare += [once(), places(T.tin[:], TL)]
    nloc = [0]

    def send(dst, out, in_, sem):
        rid, pid, _ = topo.addr(dst)
        g.remote_dma(out, in_, T.sem[sem], T.sem.loc, pid, rid, topo.mask(core, dst))
        nloc[0] += len(topo.engines(core, dst))

    for n in range(3):
        mate = T.cores[rank ^ STEP[n]]
        eng = len(topo.engines(core, mate))
        x0, a0, s0 = 1792 * n, C * n, SC * NV * n
        sf = T.sf[:, a0:a0 + C]
        tb = []
        for i in (0, 1) if n else (1, 0):
            u, t = ends[n + i]
            for v0, v1 in HALVES:
                k = a0 + NV * i
                r = scp(T.sl[:, k + v0:k + v1], sf.indirect(T.lu[:, u + v0 // 16:u + v1 // 16]), [t, sft[n]])
                if len(ttab) < 3:
                    fill()
                tb.append(vtt(T.bt[:, k + v0:k + v1], sf.indirect(T.lu[:, u + 14 + v0 // 16:u + 14 + v1 // 16]),
                              T.sl[:, k + v0:k + v1], OP.is_gt, [r]))
        tEO.append(scp(T.d1[:, 4:SC * NV:SC], T.d1[:, 2:SC * NV:SC], [tEO]))
        t = [vtt(T.d1[:, SC * v0:SC * v1:SC], T.bt[:, a0 + v0:a0 + v1], T.bt[:, a0 + NV + v0:a0 + NV + v1], OP.not_equal,
                 [tb[2 + k], tscan[0]]) for k, (v0, v1) in enumerate(HALVES)]
        mt = T.mt[:, s0:s0 + SC * NV]
        for k, (v0, v1) in enumerate(HALVES):
            need("v", t[k], ttab, tEO, tC)
            tscan[0] = done("v", V.tensor_tensor_scan(T.mt[:, s0 + SC * v0:s0 + SC * v1], T.d0[:, SC * v0:SC * v1],
                                                      T.d1[:, SC * v0:SC * v1], 0.0, OP.mult, OP.add))
        fill()
        while len(heads) <= n:
            fill()
        hp, thp = heads[n]
        tml = [vcp(lin(M_ + n, 0, NV), mt.indirect(T.lu[:, hp:hp + 14]), [tscan[0], thp]),
               scp(lin(M_ + n, NV, C), mt.indirect(T.lu[:, hp + 14:hp + 28]), [tscan[0], thp])]
        u = 64 * n
        t = turn(M_ + n, tml)
        fill()
        tm = vts(T.mu[:, u:u + 64], own(M_ + n, SELM), 224.0, OP.add, [t, tSEL])
        fill()
        m0, m1 = T.mu[:, u:u + 28], T.mu[:, u + 32:u + 60]
        need("p", tm)
        send(mate, T.ma[:, u:u + 64], T.mu[:, u:u + 64], "ml%d" % n)
        G = [T.lg[:, C * (2 * n + k):C * (2 * n + k) + C] for k in range(2)]
        need("y", scp(G[0], lin(M_ + n).indirect(m0), [tm]), thl[n])
        Y.dma_start(G[0][2::16, :], hm[n][2::16, :]).then_inc(T.sem["on%d" % n], 16)
        tz = []
        for b in range(4):
            yp = T.yf[:, x0 + C * b:x0 + C * b + C]
            ty = vtt(yp, T.xp[:, x0 + C * b:x0 + C * b + C].indirect(m1), T.xs[:, x0 + b:x0 + 1792:4], OP.add,
                     [tm, tXP[n][b], tX[n]])
            if b < 3:
                tz.append(scp(T.zt[:, x0 + b:x0 + 1792:4], yp.indirect(m0), [ty], scale=0.5))
        fill()
        tl3 = [vts(T.zt[:, x0 + 3:x0 + 4 * ZV:4], yp.indirect(T.mu[:, u:u + ZV // 16]), 0.5, OP.mult, [ty]),
               scp(T.zt[:, x0 + 4 * ZV + 3:x0 + 1792:4], yp.indirect(T.mu[:, u + ZV // 16:u + 28]), [ty], scale=0.5)]
        fill()
        tq, tr, tH = {}, {}, {}
        for step in ORDER:
            k = step[1]
            if step[0] == "z":
                c0, c1 = LAYER[k]
                tq[k] = quant(T.qz, T.sz, a0 + c0, a0 + c1, T.zt[:, x0 + 4 * c0:x0 + 4 * c1], tz + tl3[:1 + (c1 > ZV)])
            elif step[0] == "m":
                c0, c1 = LAYER[k]
                for b in range(4):
                    tr[k, b] = mm(b + 4 * (k % 2), c1 - c0, T.wq[:, 128 * b:128 * b + 128], T.wp[:, 128 * b:128 * b + 128],
                                  T.qz[:, a0 + c0:a0 + c1], T.sz[:, a0 + c0:a0 + c1], [LW, tq[k]])
            elif step[0] == "c":
                (c0, c1), b = LAYER[k], step[2]
                o, j = T.ht[:, x0 + 4 * c0 + b:x0 + 4 * c1:4], b + 4 * (k % 2)
                if step[3] == "v":
                    tH[k, b] = vts(o, bank(j, c1 - c0), 0.03125, OP.mult, [tr[k, b]])
                else:
                    tH[k, b] = scp(o, bank(j, c1 - c0), [tr[k, b]], scale=0.03125)
                free[j].append(tH[k, b])
            elif step[0] == "h":
                c0, c1 = SENT[k]
                fill()
                need("p", quant(T.qh, T.sh, a0 + c0, a0 + c1, T.ht[:, x0 + 4 * c0:x0 + 4 * c1],
                                [t for (j, b), t in tH.items() if LAYER[j][0] < c1]))
                send(mate, T.qa[:, a0 + c0:a0 + c1].bitcast(dt.uint8), T.qh[:, a0 + c0:a0 + c1].bitcast(dt.uint8), "a%d%d" % (k, n))
                send(mate, T.sa[:, a0 + c0:a0 + c1], T.sh[:, a0 + c0:a0 + c1], "a%d%d" % (k, n))
            elif step[0] == "g":
                tg = scp(G[1], G[0].indirect(T.ma[:, u + 32:u + 60]), [("ml%d" % n, eng), ("on%d" % n, 16)])
            elif step[0] == "l":
                tlt = (scp, vcp)[k == "v"](lin(LT_ + n), G[1].indirect(T.ma[:, u:u + 28]), [tg])
            else:
                fill(k)
        if n == 0:
            thl[2] = tlt
        if n == 2:
            need("s", tlt)
            need("y", done("s", S.activation(T.tpf[:], lin(LT_ + 2), AF.Identity, bias=224.0)))
            Y.dma_start(T.tp[:, :], T.tpf[2::16, 0:C]).then_inc(T.sem.outs, 16)
        u0 = take("u", 64)
        fill(3)
        t = turn(LT_ + n, [tlt])
        fill()
        tl = vts(T.lu[:, u0:u0 + 64], own(LT_ + n, SELL), 224.0, OP.add, t)
        fill()
        if n < 2:
            tails = T.lu[:, u0 + 32:u0 + 60]
            ti = invert(n + 2, tails, [tl])
        if n == 0:
            spare.append(places(tails, tl))
        while len(tQE) < 4:
            fill()
        tdp = [[], [], [], []]
        for h, (c0, c1) in enumerate(SENT):
            need("t", ("a%d%d" % (h, n), 2 * eng))
            for b in UNPACK:
                j = b + 4 * (h % 2)
                t = mm(j, c1 - c0, T.qe[:, 128 * b:128 * b + 128], T.se[:, 128 * b:128 * b + 128],
                       T.qa[:, a0 + c0:a0 + c1], T.sa[:, a0 + c0:a0 + c1], [tQE])
                r = (scp, vcp)[(h, b) in DONV[n]](T.dp[:, x0 + C * b + c0:x0 + C * b + c1], bank(j, c1 - c0), [t])
                free[j].append(r)
                tdp[b].append(r)

        def far(b, c0, c1):
            return T.dp[:, x0 + C * b:x0 + C * b + C].indirect(T.lu[:, u0 + c0 // 16:u0 + c1 // 16])

        runs, lay, order = (STATE, LAID, MEET) if n < 2 else (LAST, LAID2, MEET2)
        laid = [(b, c0, c1, scp(T.dg[:, C * b + c0:C * b + c1], far(b, c0, c1), [tl, tdp[b], tX[n]])) for b, c0, c1 in lay]
        if n < 2:
            sides(n + 2, ti)
        x1, a1 = x0 + 1792, a0 + C
        made = [[] for _ in runs]
        for b, c0, c1 in order:
            if b is not None:
                deps = [t for k, d0, d1, t in laid if k == b and d0 < c1 and c0 < d1]
                in0 = T.dg[:, C * b + c0:C * b + c1] if deps else far(b, c0, c1)
                t = vtt(T.xs[:, x1 + 4 * c0 + b:x1 + 4 * c1:4], in0, T.xs[:, x0 + 4 * c0 + b:x0 + 4 * c1:4], OP.add,
                        deps or [tl, tdp[b], tX[n]])
                tX[n + 1].append(t)
                for k, (d0, d1) in enumerate(runs):
                    if d0 < c1 and c0 < d1:
                        made[k].append(t)
                if n < 2 and c1 == C:
                    plane(n + 1, b, tX[n + 1])
                continue
            h = runs.index((c0, c1))
            if n < 2:
                score(n + 1, h, made[h])
                continue
            t = quant(T.qx, T.sx, a1 + c0, a1 + c1, T.xs[:, x1 + 4 * c0:x1 + 4 * c1], made[h])
            need("y", t)
            Y.dma_start(T.oc[:, 4 * c0:4 * c1], T.qx[:, a1 + c0:a1 + c1].bitcast(dt.uint8)).then_inc(T.sem.outs, 16)
            for k in range(4 * (c1 == C)):
                need("ys"[k % 2], t)
                Q["ys"[k % 2]].dma_start(T.osc[4 * k:4 * k + 4, 0:C], T.sx[32 * k:32 * k + 4, a1:a1 + C]).then_inc(T.sem.outs, 16)
            t = mm(h, c1 - c0, T.qv[:, 0:128], T.sv[:, 0:128], T.qx[:, a1 + c0:a1 + c1], T.sx[:, a1 + c0:a1 + c1], [tQV, t])
            need("s", (scp, vcp)[c1 == C](T.yo[:, c0:c1], bank(h, c1 - c0), [t]))
            S.dma_start(T.y[:, c0:c1], T.yo[:, c0:c1]).then_inc(T.sem.outs, 16)
        if n < 2:
            first, tb = sort(n + 2), tables(n + 2)
            ttab = next(tb)
            for gen in (first, tb, first, tb):
                next(gen, None)
            fill()
            spare.insert(0, tb)
    need("y", ("outs", 16 * (5 + 2 * len(LAST))), ("loc", nloc[0]), LW, LV, [("c" + q, cnt[q]) for q in cnt])
